import numpy as np
import ml_dtypes


def mxq(x, axis, fmt="e4m3"):
    dtype, down = {"e4m3": (ml_dtypes.float8_e4m3fn, 7), "e5m2": (ml_dtypes.float8_e5m2, 14)}[fmt]
    v = np.moveaxis(np.asarray(x, np.float32).astype(ml_dtypes.bfloat16).astype(np.float64), axis, -1)
    blocks = v.reshape(v.shape[:-1] + (-1, 32))
    amax = np.abs(blocks).max(-1, keepdims=True)
    byte = np.maximum(np.where(amax > 0, np.frexp(amax)[1] - 1 + 127, 0) - down, 1)
    scale = np.exp2(byte - 127.0)
    codes = (blocks / scale).astype(np.float32).astype(dtype).astype(np.float64)
    return np.moveaxis((codes * scale).reshape(v.shape), -1, axis)


WIDE = False


def mx_kscale(k):
    if not WIDE:
        return np.ones(k)
    levels = np.array([10, -10, 5, -5, 0])
    if k % 512:
        return np.exp2(np.random.permutation(np.resize(levels, k // 32))).repeat(32)
    a = np.empty((k // 512, 16))
    for p in range(k // 512):
        a[p, :8] = np.random.permutation(np.resize(levels, 8))
        for g in range(8):
            far = levels[np.abs(levels - a[p, g]) >= 10]
            a[p, g + 8] = far[np.random.randint(len(far))]
    return np.exp2(a.ravel()).repeat(32)


def f64(x):
    return np.asarray(x).astype(np.float64)


def striped(idx):
    return np.tile(np.asarray(idx).reshape(-1, 16).T, (8, 1)).astype(np.uint16)


def unstriped(offs):
    return offs[:16].T.reshape(-1).astype(np.int64)


E2M1 = np.array([0.0, 0.5, 1.0, 1.5, 2.0, 3.0, 4.0, 6.0, -0.0, -0.5, -1.0, -1.5, -2.0, -3.0, -4.0, -6.0])


def pack_weight(w, fmt):
    k, n = w.shape
    w = f64(np.asarray(w, np.float32).astype(ml_dtypes.bfloat16)).reshape(k // 32, 32, n)
    amax = np.abs(w).max(1)
    if fmt == "e4m3":
        byte = np.frexp(amax)[1] - 1 + 127 - 7
    else:
        mant, ex = np.frexp(amax / 6.0)
        byte = np.where(mant > 0.5, ex, ex - 1) + 127
    byte = np.clip(np.where(amax > 0, byte, 1), 1, 254)
    scaled = (w * np.exp2(127.0 - byte)[:, None, :]).reshape(k, n).astype(np.float32)
    by_word = np.ascontiguousarray(scaled.reshape(k // 512, 128, 4, n).transpose(0, 1, 3, 2))
    if fmt == "e4m3":
        words = by_word.astype(ml_dtypes.float8_e4m3fn).view(np.uint8)
    else:
        c = by_word.astype(ml_dtypes.float4_e2m1fn).view(np.uint8) & 0xF
        words = (c[..., 0::2] | (c[..., 1::2] << 4)).reshape(k // 512, 128, 2 * n)
    return np.ascontiguousarray(words), np.ascontiguousarray(byte.astype(np.uint8).reshape(k // 512, 16, n))


def unpack_weight(words, scales, fmt):
    g, _, n = scales.shape
    words = np.ascontiguousarray(words).reshape(g, 128, n, -1)
    if fmt == "e4m3":
        vals = words.view(ml_dtypes.float8_e4m3fn).astype(np.float64)
    else:
        nib = np.empty((g, 128, n, 4), np.uint8)
        nib[..., 0::2] = words & 0xF
        nib[..., 1::2] = words >> 4
        vals = E2M1[nib]
    vals = vals * np.repeat(np.exp2(scales.astype(np.float64) - 127.0), 8, axis=1)[..., None]
    return vals.transpose(0, 1, 3, 2).reshape(g * 512, n)


B, N, T, D, DV, NQ = 1, 512, 1024, 1024, 256, 256


def setup_inputs():
    n = np.random.standard_normal
    idx = np.sort(np.random.permutation(T)[:B * N].reshape(B, N), axis=1).reshape(-1)
    s = mx_kscale(D)[:, None]
    u = np.ones(T)
    u[idx] = mx_kscale(B * N)
    r = np.random.uniform(0.5, 2.0, T)
    qp = [pack_weight(x, "e4m3") for x in n((B, D, NQ)) * s * (1.00 / np.sqrt(D))]
    k = n((D, T)) / s
    v = n((DV, T)) / (u * r)
    kp = pack_weight(k, "e2m1")
    return {
        "q_words": np.stack([x[0] for x in qp]),
        "q_scales": np.stack([x[1] for x in qp]),
        "k_words": np.ascontiguousarray(kp[0].reshape(D // 1024, 2, 128, T, 2).transpose(0, 2, 3, 1, 4)).reshape(D // 1024, 128, T, 4),
        "k_scales": kp[1],
        "vT": v.astype(np.float32),
        "vs": np.tile(u * r, (128, 1)).astype(np.float32),
        "kb": np.tile(n(T), (128, 1)).astype(np.float32),
        "offs": striped(idx),
    }


def reference(q_words, q_scales, k_words, k_scales, vT, vs, kb, offs):
    idx = unstriped(offs)
    k = unpack_weight(k_words.reshape(D // 1024, 128, T, 2, 2).transpose(0, 3, 1, 2, 4).reshape(D // 512, 128, 2 * T), k_scales, "e2m1")
    v = f64(vT)
    pick = lambda x: x[:, idx].reshape(x.shape[0], B, N).transpose(1, 0, 2)
    q = np.stack([unpack_weight(q_words[b], q_scales[b], "e4m3") for b in range(B)])
    score = q.transpose(0, 2, 1) @ pick(k)
    score = score + pick(f64(kb))[:, :1, :]
    p = np.square(np.maximum(score, 0.0))
    total = p.sum(-1, keepdims=True) + 1.0
    w = p * pick(f64(vs))[:, :1, :]
    y = mxq(w, 2, "e4m3") @ mxq(pick(v).transpose(0, 2, 1), 1, "e4m3")
    y = y / total
    return y

@@ -1,0 +1,179 @@
+from contextlib import ExitStack
+
+import concourse.mybir as mybir
+from concourse.masks import make_identity
+
+F32 = mybir.dt.float32
+BF16 = mybir.dt.bfloat16
+I32 = mybir.dt.int32
+U32 = mybir.dt.uint32
+U16 = mybir.dt.uint16
+U8 = mybir.dt.uint8
+FP8X4 = mybir.dt.float8_e4m3fn_x4
+FP4X4 = mybir.dt.float4_e2m1fn_x4
+ACT = mybir.ActivationFunctionType
+ALU = mybir.AluOpType
+
+P = 128
+N, T, D, DV, NQ = 512, 1024, 1024, 256, 256
+FLOPS = 2 * NQ * N * D + 2 * NQ * N * DV
+
+
+def tile_attend_rel2_kb_srtq256n512t1024_kernel(tc, q_words, q_scales, k_words, k_scales, vT, vs, kb, offs, out):
+    nc = tc.nc
+    with ExitStack() as ctx:
+        sb = ctx.enter_context(tc.tile_pool(name="sb", bufs=1))
+        ps = ctx.enter_context(tc.psum_pool(name="ps", bufs=1))
+
+        offsets = sb.tile([P, N // 16], U16, name="offsets")
+        kw_pool = sb.tile([P, T], I32, name="kw_pool", align_bytes=64)
+        ks_pool = sb.tile([P, 2, T // 4], I32, name="ks_pool", align_bytes=64)
+        kb_pool = sb.tile([P, T], F32, name="kb_pool", align_bytes=64)
+        vs_pool = sb.tile([P, T], F32, name="vs_pool", align_bytes=64)
+        v_pool = sb.tile([P, 2, T], F32, name="v_pool", align_bytes=64)
+        qw = sb.tile([P, 2, NQ], I32, name="qw", align_bytes=64)
+        qs = sb.tile([P, 2, NQ], U8, name="qs", align_bytes=64)
+        ident = sb.tile([P, P], F32, name="ident", align_bytes=64)
+
+        nc.vector.memset(kb_pool[:].bitcast(I32), 0)
+        nc.vector.memset(ks_pool[:], 0)
+        nc.vector.memset(vs_pool[:].bitcast(I32), 0)
+        nc.vector.memset(qs[:].bitcast(I32), 0)
+        make_identity(nc, ident[:])
+        nc.gpsimd.dma_start(v_pool[:], vT.rearrange("(h p) t -> p h t", h=2))
+        warm = sb.tile([P, 1], F32, name="warm")
+        nc.scalar.activation(warm[:], ident[:, 0:1], ACT.Relu)
+
+        nc.sync.dma_start(offsets[:], offs)
+        nc.sync.dma_start(kw_pool[:], k_words[0].rearrange("g t b -> g (t b)").bitcast(I32))
+        nc.sync.dma_start(kb_pool[0:1, :], kb[0:1, :])
+        ks_rows = k_scales.rearrange("o (Q r) t -> r Q o t", r=4)
+        for r in range(4):
+            nc.sync.dma_start(ks_pool[r:P:32], ks_rows[r].bitcast(I32))
+        nc.sync.dma_start(vs_pool[0:1, :], vs[0:1, :])
+        nc.sync.dma_start(qw[:], q_words[0].rearrange("o g q r -> g o (q r)").bitcast(I32))
+        qs_rows = q_scales[0].rearrange("o (Q r) q -> r Q o q", r=4)
+        for r in range(4):
+            nc.sync.dma_start(qs[r:P:32].bitcast(I32), qs_rows[r].bitcast(I32))
+
+        kw_g = sb.tile([P, N], U32, name="kw_g", align_bytes=64)
+        nc.vector.tensor_copy(
+            kw_g[:].rearrange("p (t g j) -> p g t j", t=4, j=8),
+            kw_pool[:].bitcast(U32).indirect(offsets[:]),
+        )
+        kb_g = sb.tile([P, N], F32, name="kb_g", align_bytes=64)
+        nc.vector.tensor_copy(kb_g[:], kb_pool[:].indirect(offsets[:]))
+        kw = sb.tile([P, 2, 2 * N], U8, name="kw", align_bytes=64)
+        nc.vector.tensor_copy(kw[:].bitcast(U16), kw_g[:].bitcast(U16).rearrange("p (n o) -> p o n", o=2))
+        ks_g = sb.tile([P, 2, N], U8, name="ks_g", align_bytes=64)
+        for o in range(2):
+            nc.vector.tensor_copy(ks_g[:, o, :], ks_pool[:, o, :].bitcast(U8).indirect(offsets[:]))
+        ks = sb.tile([P, 2, N], U8, name="ks", align_bytes=64)
+        nc.vector.tensor_copy(
+            ks[:].bitcast(I32).rearrange("p o (t g j) -> p o t g j", t=4, j=2),
+            ks_g[:].bitcast(I32).rearrange("p o (g t j) -> p o t g j", t=4, j=2),
+        )
+        vs_g = sb.tile([P, N], F32, name="vs_g", align_bytes=64)
+        nc.vector.tensor_copy(vs_g[:], vs_pool[:].indirect(offsets[:]))
+        v_g = sb.tile([P, 2, N], BF16, name="v_g", align_bytes=64)
+        for h in range(2):
+            nc.vector.tensor_copy(
+                v_g[:, h, :].rearrange("p (u g j b) -> p g u b j", u=2, j=8, b=2),
+                v_pool[:, h, :].indirect(offsets[:]),
+            )
+
+        def to_columns(gathered, name):
+            ordered = sb.tile([P, N], F32, name=name + "_ord", align_bytes=64)
+            nc.scalar.copy(
+                ordered[:].rearrange("p (t g j) -> p t g j", t=4, j=8),
+                gathered[:].rearrange("p (g t j) -> p t g j", t=4, j=8),
+            )
+            turned = ps.tile([P, 4, P], F32, name=name + "_t")
+            for t in range(4):
+                nc.tensor.transpose(turned[:, t, :], ordered[:, t * P : (t + 1) * P], ident[:])
+            return turned
+
+        kb_t = to_columns(kb_g, "kb")
+        kb_col = sb.tile([P, 4], F32, name="kb_col")
+        nc.scalar.copy(kb_col[:], kb_t[:, :, 0])
+        vs_t = to_columns(vs_g, "vs")
+
+        scores = [ps.tile([P, NQ], F32, name="scores%d" % t) for t in range(4)]
+        for t in range(4):
+            for qb in range(2):
+                for o in range(2):
+                    nc.tensor.matmul_mx(
+                        out=scores[t][:, qb * P : (qb + 1) * P],
+                        lhsT=kw[:, o, 2 * P * t : 2 * P * (t + 1)].bitcast(FP4X4),
+                        lhsT_scale=ks[:, o, P * t : P * (t + 1)],
+                        rhs=qw[:, o, qb * P : (qb + 1) * P].bitcast(FP8X4),
+                        rhs_scale=qs[:, o, qb * P : (qb + 1) * P],
+                        start=(o == 0),
+                        stop=(o == 1),
+                    )
+
+        relu = sb.tile([P, 4, NQ], F32, name="relu", align_bytes=64)
+        for t in range(4):
+            nc.scalar.activation(relu[:, t, :], scores[t][:], ACT.Relu, bias=kb_col[:, t : t + 1])
+        p = sb.tile([P, 4, NQ], F32, name="p", align_bytes=64)
+        for qb in range(2):
+            cols = slice(qb * P, (qb + 1) * P)
+            nc.scalar.activation(p[:, :, cols], relu[:, :, cols], ACT.Square)
+
+        v_t = ps.tile([P, 2, 2, P], F32, name="v_t")
+        v_words = v_g[:].bitcast(F32)
+        for h in range(2):
+            for u in range(2):
+                nc.tensor.transpose(v_t[:, h, u, :], v_words[:, h, u * P : (u + 1) * P], ident[:])
+        v_in = sb.tile([P, DV * 4], BF16, name="v_in", align_bytes=64)
+        nc.scalar.copy(
+            v_in[:].bitcast(F32).rearrange("p (h e u) -> p h e u", h=2, u=2),
+            v_t[:].rearrange("p h u e -> p h e u"),
+        )
+
+        w_in = sb.tile([P, NQ, 4], BF16, name="w_in", align_bytes=64)
+        wq = sb.tile([P, NQ], U32, name="wq", align_bytes=64)
+        wq_s = sb.tile([P, NQ], U8, name="wq_s", align_bytes=64)
+        for qb in range(2):
+            cols = slice(qb * P, (qb + 1) * P)
+            nc.vector.tensor_tensor(
+                w_in[:, cols, :],
+                p[:, :, cols].rearrange("p t q -> p q t"),
+                vs_t[:, :, 0:1].to_broadcast([P, 4, P]).rearrange("p t q -> p q t"),
+                ALU.mult,
+            )
+        vq = sb.tile([P, DV], U32, name="vq", align_bytes=64)
+        vq_s = sb.tile([P, DV], U8, name="vq_s", align_bytes=64)
+        nc.vector.quantize_mx(out=vq[:].bitcast(FP8X4), scales=vq_s[:], in_=v_in[:])
+        for qb in range(2):
+            cols = slice(qb * P, (qb + 1) * P)
+            nc.vector.quantize_mx(
+                out=wq[:, cols].bitcast(FP8X4), scales=wq_s[:, cols], in_=w_in[:, cols, :].rearrange("p q t -> p (q t)")
+            )
+
+        p_t = ps.tile([P, 2, P], F32, name="p_t")
+        for qb in range(2):
+            for t in range(4):
+                nc.tensor.matmul(
+                    p_t[:, qb, :], p[:, t, qb * P : (qb + 1) * P], ident[:], start=(t == 0), stop=(t == 3), is_transpose=True
+                )
+        total = sb.tile([P, 2], F32, name="total")
+        spent = sb.tile([P, 2, P], F32, name="spent")
+        for qb in range(2):
+            nc.scalar.activation(spent[:, qb, :], p_t[:, qb, :], ACT.Copy, bias=1.0 / P, accum_out=total[:, qb : qb + 1])
+        inv = sb.tile([P, 2], F32, name="inv")
+        nc.vector.reciprocal(inv[:], total[:])
+
+        for qb in range(2):
+            cols = slice(qb * P, (qb + 1) * P)
+            y = ps.tile([P, DV], F32, name="scores%d" % qb)
+            nc.tensor.matmul_mx(
+                out=y[:], lhsT=wq[:, cols].bitcast(FP8X4), lhsT_scale=wq_s[:, cols],
+                rhs=vq[:].bitcast(FP8X4), rhs_scale=vq_s[:], start=True, stop=True,
+            )
+            res = sb.tile([P, DV], F32, name="res%d" % qb, align_bytes=64)
+            if qb == 0:
+                nc.scalar.activation(res[:], y[:], ACT.Copy, scale=inv[:, qb : qb + 1])
+            else:
+                nc.vector.tensor_scalar(res[:], y[:], inv[:, qb : qb + 1], None, ALU.mult)
+            (nc.scalar if qb == 0 else nc.sync).dma_start(out[0, cols, :], res[:])

@@ -29,134 +29,137 @@ def tile_attend_rel2_kb_srtq256n512t1024_kernel(tc, q_words, q_scales, k_words, 
         kw_pool = sb.tile([P, T], I32, name="kw_pool", align_bytes=64)
         ks_pool = sb.tile([P, 2, T // 4], I32, name="ks_pool", align_bytes=64)
         kb_pool = sb.tile([P, T], F32, name="kb_pool", align_bytes=64)
-        vs_pool = sb.tile([P, T], F32, name="vs_pool", align_bytes=64)
-        v_pool = sb.tile([P, 2, T], F32, name="v_pool", align_bytes=64)
+        vs_pool = sb.tile([P, T], F32, name="vs_pool", tag="vs_then_v", align_bytes=64)
+        v_pool = [sb.tile([P, T], F32, name="v_pool%d" % h, align_bytes=64) for h in range(2)]
         qw = sb.tile([P, 2, NQ], I32, name="qw", align_bytes=64)
         qs = sb.tile([P, 2, NQ], U8, name="qs", align_bytes=64)
         ident = sb.tile([P, P], F32, name="ident", align_bytes=64)
 
-        nc.vector.memset(kb_pool[:].bitcast(I32), 0)
+        warm_in = sb.tile([P, 1], F32, name="warm_in")
+        warm_out = sb.tile([P, 1], F32, name="warm_out")
+        nc.gpsimd.memset(warm_in[:], 0.0)
+        nc.scalar.activation(warm_out[:], warm_in[:], ACT.Relu)
+
         nc.vector.memset(ks_pool[:], 0)
+        nc.vector.memset(kb_pool[0:96, :].bitcast(I32), 0)
         nc.vector.memset(vs_pool[:].bitcast(I32), 0)
         nc.vector.memset(qs[:].bitcast(I32), 0)
         make_identity(nc, ident[:])
-        nc.gpsimd.dma_start(v_pool[:], vT.rearrange("(h p) t -> p h t", h=2))
-        warm = sb.tile([P, 1], F32, name="warm")
-        nc.scalar.activation(warm[:], ident[:, 0:1], ACT.Relu)
+        nc.gpsimd.dma_start(v_pool[1][:], vT[P : 2 * P, :])
+        ident_bf = sb.tile([P, P], BF16, name="ident_bf", align_bytes=64)
+        nc.scalar.copy(ident_bf[:], ident[:])
 
         nc.sync.dma_start(offsets[:], offs)
+        nc.sync.dma_start(kb_pool[96:P, :], kb[96:P, :])
         nc.sync.dma_start(kw_pool[:], k_words[0].rearrange("g t b -> g (t b)").bitcast(I32))
-        nc.sync.dma_start(kb_pool[0:1, :], kb[0:1, :])
+        nc.sync.dma_start(v_pool[0][:], vT[0:P, :])
+        nc.sync.dma_start(qw[:], q_words[0].rearrange("o g q r -> g o (q r)").bitcast(I32))
         ks_rows = k_scales.rearrange("o (Q r) t -> r Q o t", r=4)
         for r in range(4):
-            nc.sync.dma_start(ks_pool[r:P:32], ks_rows[r].bitcast(I32))
+            nc.scalar.dma_start(ks_pool[r:P:32], ks_rows[r].bitcast(I32))
         nc.sync.dma_start(vs_pool[0:1, :], vs[0:1, :])
-        nc.sync.dma_start(qw[:], q_words[0].rearrange("o g q r -> g o (q r)").bitcast(I32))
         qs_rows = q_scales[0].rearrange("o (Q r) q -> r Q o q", r=4)
         for r in range(4):
             nc.sync.dma_start(qs[r:P:32].bitcast(I32), qs_rows[r].bitcast(I32))
 
-        kw_g = sb.tile([P, N], U32, name="kw_g", align_bytes=64)
-        nc.vector.tensor_copy(
-            kw_g[:].rearrange("p (t g j) -> p g t j", t=4, j=8),
-            kw_pool[:].bitcast(U32).indirect(offsets[:]),
-        )
+        def by_place(ap):
+            return ap.rearrange("p (t g j) -> p g t j", t=4, j=8)
+
+        def by_pair(ap):
+            return ap.rearrange("p (u g j b) -> p g u b j", u=2, j=8, b=2)
+
         kb_g = sb.tile([P, N], F32, name="kb_g", align_bytes=64)
-        nc.vector.tensor_copy(kb_g[:], kb_pool[:].indirect(offsets[:]))
+        nc.vector.tensor_copy(by_place(kb_g[:].bitcast(U32)), kb_pool[:].bitcast(U32).indirect(offsets[:]))
+        kw_g = sb.tile([P, N], U32, name="kw_g", align_bytes=64)
+        nc.vector.tensor_copy(by_place(kw_g[:]), kw_pool[:].bitcast(U32).indirect(offsets[:]))
         kw = sb.tile([P, 2, 2 * N], U8, name="kw", align_bytes=64)
-        nc.vector.tensor_copy(kw[:].bitcast(U16), kw_g[:].bitcast(U16).rearrange("p (n o) -> p o n", o=2))
-        ks_g = sb.tile([P, 2, N], U8, name="ks_g", align_bytes=64)
-        for o in range(2):
-            nc.vector.tensor_copy(ks_g[:, o, :], ks_pool[:, o, :].bitcast(U8).indirect(offsets[:]))
         ks = sb.tile([P, 2, N], U8, name="ks", align_bytes=64)
+        ks_g = sb.tile([P, 2, N], U8, name="ks_g", tag="ks_g_then_vs", align_bytes=64)
+        nc.vector.tensor_copy(ks_g[:, 0, :], ks_pool[:, 0, :].bitcast(U8).indirect(offsets[:]))
+        nc.vector.tensor_copy(kw[:].bitcast(U16), kw_g[:].bitcast(U16).rearrange("p (n o) -> p o n", o=2))
+        nc.vector.tensor_copy(ks_g[:, 1, :], ks_pool[:, 1, :].bitcast(U8).indirect(offsets[:]))
         nc.vector.tensor_copy(
             ks[:].bitcast(I32).rearrange("p o (t g j) -> p o t g j", t=4, j=2),
             ks_g[:].bitcast(I32).rearrange("p o (g t j) -> p o t g j", t=4, j=2),
         )
-        vs_g = sb.tile([P, N], F32, name="vs_g", align_bytes=64)
-        nc.vector.tensor_copy(vs_g[:], vs_pool[:].indirect(offsets[:]))
-        v_g = sb.tile([P, 2, N], BF16, name="v_g", align_bytes=64)
-        for h in range(2):
-            nc.vector.tensor_copy(
-                v_g[:, h, :].rearrange("p (u g j b) -> p g u b j", u=2, j=8, b=2),
-                v_pool[:, h, :].indirect(offsets[:]),
-            )
+        vs_g = sb.tile([P, N], F32, name="vs_g", tag="ks_g_then_vs", align_bytes=64)
+        nc.vector.tensor_copy(by_place(vs_g[:].bitcast(U32)), vs_pool[:].bitcast(U32).indirect(offsets[:]))
+        v_g = [
+            sb.tile([P, N], BF16, name="v_g0", align_bytes=64),
+            sb.tile([P, N], BF16, name="v_g1", tag="vs_then_v", align_bytes=64),
+        ]
+        nc.vector.tensor_copy(by_pair(v_g[1][:]), v_pool[1][:].indirect(offsets[:]))
 
-        def to_columns(gathered, name):
-            ordered = sb.tile([P, N], F32, name=name + "_ord", align_bytes=64)
-            nc.scalar.copy(
-                ordered[:].rearrange("p (t g j) -> p t g j", t=4, j=8),
-                gathered[:].rearrange("p (g t j) -> p t g j", t=4, j=8),
-            )
-            turned = ps.tile([P, 4, P], F32, name=name + "_t")
+        v_half = sb.tile([P, T], BF16, name="v_half", align_bytes=64)
+        nc.scalar.activation(v_half[:], v_pool[0][:], ACT.Copy)
+        nc.scalar.activation(by_place(v_g[0][:]), v_half[:].indirect(offsets[:]), ACT.Copy)
+
+        def turn(gathered, name):
+            turned = ps.tile([P, 4, P], F32, name=name)
             for t in range(4):
-                nc.tensor.transpose(turned[:, t, :], ordered[:, t * P : (t + 1) * P], ident[:])
+                nc.tensor.transpose(turned[:, t, :], gathered[:, t * P : (t + 1) * P], ident[:])
             return turned
 
-        kb_t = to_columns(kb_g, "kb")
+        kb_t = turn(kb_g, "kb_t")
         kb_col = sb.tile([P, 4], F32, name="kb_col")
-        nc.scalar.copy(kb_col[:], kb_t[:, :, 0])
-        vs_t = to_columns(vs_g, "vs")
+        nc.scalar.copy(kb_col[:], kb_t[:, :, 96])
 
-        scores = [ps.tile([P, NQ], F32, name="scores%d" % t) for t in range(4)]
+        v_in = sb.tile([P, 2, P * 4], BF16, name="v_in", align_bytes=64)
+
+        v0_t = ps.tile([P, 4, P], BF16, name="v_t")
         for t in range(4):
-            for qb in range(2):
+            nc.tensor.transpose(v0_t[:, t, :], v_g[0][:, t * P : (t + 1) * P], ident_bf[:])
+        nc.scalar.copy(v_in[:, 0, :].rearrange("p (e t) -> p e t", t=4), v0_t[:].rearrange("p t e -> p e t"))
+
+        relu = sb.tile([P, 2, 4, P], F32, name="relu", align_bytes=64)
+        p = sb.tile([P, 2, 4, P], F32, name="p", align_bytes=64)
+        for qb in range(2):
+            cols = slice(qb * P, (qb + 1) * P)
+            for t in range(4):
+                score = ps.tile([P, P], F32, name="score%d" % t)
                 for o in range(2):
                     nc.tensor.matmul_mx(
-                        out=scores[t][:, qb * P : (qb + 1) * P],
+                        out=score[:],
                         lhsT=kw[:, o, 2 * P * t : 2 * P * (t + 1)].bitcast(FP4X4),
                         lhsT_scale=ks[:, o, P * t : P * (t + 1)],
-                        rhs=qw[:, o, qb * P : (qb + 1) * P].bitcast(FP8X4),
-                        rhs_scale=qs[:, o, qb * P : (qb + 1) * P],
+                        rhs=qw[:, o, cols].bitcast(FP8X4),
+                        rhs_scale=qs[:, o, cols],
                         start=(o == 0),
                         stop=(o == 1),
                     )
+                nc.scalar.activation(relu[:, qb, t, :], score[:], ACT.Relu, bias=kb_col[:, t : t + 1])
+            nc.scalar.activation(p[:, qb], relu[:, qb], ACT.Square)
 
-        relu = sb.tile([P, 4, NQ], F32, name="relu", align_bytes=64)
-        for t in range(4):
-            nc.scalar.activation(relu[:, t, :], scores[t][:], ACT.Relu, bias=kb_col[:, t : t + 1])
-        p = sb.tile([P, 4, NQ], F32, name="p", align_bytes=64)
-        for qb in range(2):
-            cols = slice(qb * P, (qb + 1) * P)
-            nc.scalar.activation(p[:, :, cols], relu[:, :, cols], ACT.Square)
+        vs_t = turn(vs_g, "score0")
+        v1_t = ps.tile([P, 2, P], F32, name="v_t")
+        v1_words = v_g[1][:].bitcast(F32)
+        for u in range(2):
+            nc.tensor.transpose(v1_t[:, u, :], v1_words[:, u * P : (u + 1) * P], ident[:])
+        nc.scalar.copy(v_in[:, 1, :].bitcast(F32).rearrange("p (e u) -> p e u", u=2), v1_t[:].rearrange("p u e -> p e u"))
 
-        v_t = ps.tile([P, 2, 2, P], F32, name="v_t")
-        v_words = v_g[:].bitcast(F32)
-        for h in range(2):
-            for u in range(2):
-                nc.tensor.transpose(v_t[:, h, u, :], v_words[:, h, u * P : (u + 1) * P], ident[:])
-        v_in = sb.tile([P, DV * 4], BF16, name="v_in", align_bytes=64)
-        nc.scalar.copy(
-            v_in[:].bitcast(F32).rearrange("p (h e u) -> p h e u", h=2, u=2),
-            v_t[:].rearrange("p h u e -> p h e u"),
-        )
-
-        w_in = sb.tile([P, NQ, 4], BF16, name="w_in", align_bytes=64)
+        w_in = sb.tile([P, 2, P, 4], BF16, name="w_in", align_bytes=64)
         wq = sb.tile([P, NQ], U32, name="wq", align_bytes=64)
         wq_s = sb.tile([P, NQ], U8, name="wq_s", align_bytes=64)
+        vq = sb.tile([P, DV], U32, name="vq", align_bytes=64)
+        vq_s = sb.tile([P, DV], U8, name="vq_s", align_bytes=64)
         for qb in range(2):
-            cols = slice(qb * P, (qb + 1) * P)
             nc.vector.tensor_tensor(
-                w_in[:, cols, :],
-                p[:, :, cols].rearrange("p t q -> p q t"),
+                w_in[:, qb],
+                p[:, qb].rearrange("p t q -> p q t"),
                 vs_t[:, :, 0:1].to_broadcast([P, 4, P]).rearrange("p t q -> p q t"),
                 ALU.mult,
             )
-        vq = sb.tile([P, DV], U32, name="vq", align_bytes=64)
-        vq_s = sb.tile([P, DV], U8, name="vq_s", align_bytes=64)
-        nc.vector.quantize_mx(out=vq[:].bitcast(FP8X4), scales=vq_s[:], in_=v_in[:])
         for qb in range(2):
             cols = slice(qb * P, (qb + 1) * P)
             nc.vector.quantize_mx(
-                out=wq[:, cols].bitcast(FP8X4), scales=wq_s[:, cols], in_=w_in[:, cols, :].rearrange("p q t -> p (q t)")
+                out=wq[:, cols].bitcast(FP8X4), scales=wq_s[:, cols], in_=w_in[:, qb].rearrange("p q t -> p (q t)")
             )
+        nc.vector.quantize_mx(out=vq[:].bitcast(FP8X4), scales=vq_s[:], in_=v_in[:].rearrange("p h x -> p (h x)"))
 
-        p_t = ps.tile([P, 2, P], F32, name="p_t")
+        p_t = ps.tile([P, 2, P], F32, name="kb_t")
         for qb in range(2):
             for t in range(4):
-                nc.tensor.matmul(
-                    p_t[:, qb, :], p[:, t, qb * P : (qb + 1) * P], ident[:], start=(t == 0), stop=(t == 3), is_transpose=True
-                )
+                nc.tensor.matmul(p_t[:, qb, :], p[:, qb, t, :], ident[:], start=(t == 0), stop=(t == 3), is_transpose=True)
         total = sb.tile([P, 2], F32, name="total")
         spent = sb.tile([P, 2, P], F32, name="spent")
         for qb in range(2):
@@ -166,7 +169,7 @@ def tile_attend_rel2_kb_srtq256n512t1024_kernel(tc, q_words, q_scales, k_words, 
 
         for qb in range(2):
             cols = slice(qb * P, (qb + 1) * P)
-            y = ps.tile([P, DV], F32, name="scores%d" % qb)
+            y = ps.tile([P, DV], F32, name="y%d" % qb)
             nc.tensor.matmul_mx(
                 out=y[:], lhsT=wq[:, cols].bitcast(FP8X4), lhsT_scale=wq_s[:, cols],
                 rhs=vq[:].bitcast(FP8X4), rhs_scale=vq_s[:], start=True, stop=True,

@@ -29,7 +29,7 @@ def tile_attend_rel2_kb_srtq256n512t1024_kernel(tc, q_words, q_scales, k_words, 
         kw_pool = sb.tile([P, T], I32, name="kw_pool", align_bytes=64)
         ks_pool = sb.tile([P, 2, T // 4], I32, name="ks_pool", align_bytes=64)
         kb_pool = sb.tile([P, T], F32, name="kb_pool", align_bytes=64)
-        vs_pool = sb.tile([P, T], F32, name="vs_pool", tag="vs_then_v", align_bytes=64)
+        vs_pool = sb.tile([P, T], F32, name="vs_pool", align_bytes=64)
         v_pool = [sb.tile([P, T], F32, name="v_pool%d" % h, align_bytes=64) for h in range(2)]
         qw = sb.tile([P, 2, NQ], I32, name="qw", align_bytes=64)
         qs = sb.tile([P, 2, NQ], U8, name="qs", align_bytes=64)
@@ -70,23 +70,24 @@ def tile_attend_rel2_kb_srtq256n512t1024_kernel(tc, q_words, q_scales, k_words, 
 
         kb_g = sb.tile([P, N], F32, name="kb_g", align_bytes=64)
         nc.vector.tensor_copy(by_place(kb_g[:].bitcast(U32)), kb_pool[:].bitcast(U32).indirect(offsets[:]))
-        kw_g = sb.tile([P, N], U32, name="kw_g", align_bytes=64)
+        kw_g = sb.tile([P, N], U32, name="kw_g", tag="kw_then_vs", align_bytes=64)
         nc.vector.tensor_copy(by_place(kw_g[:]), kw_pool[:].bitcast(U32).indirect(offsets[:]))
-        kw = sb.tile([P, 2, 2 * N], U8, name="kw", align_bytes=64)
-        ks = sb.tile([P, 2, N], U8, name="ks", align_bytes=64)
-        ks_g = sb.tile([P, 2, N], U8, name="ks_g", tag="ks_g_then_vs", align_bytes=64)
-        nc.vector.tensor_copy(ks_g[:, 0, :], ks_pool[:, 0, :].bitcast(U8).indirect(offsets[:]))
-        nc.vector.tensor_copy(kw[:].bitcast(U16), kw_g[:].bitcast(U16).rearrange("p (n o) -> p o n", o=2))
-        nc.vector.tensor_copy(ks_g[:, 1, :], ks_pool[:, 1, :].bitcast(U8).indirect(offsets[:]))
-        nc.vector.tensor_copy(
-            ks[:].bitcast(I32).rearrange("p o (t g j) -> p o t g j", t=4, j=2),
-            ks_g[:].bitcast(I32).rearrange("p o (g t j) -> p o t g j", t=4, j=2),
-        )
-        vs_g = sb.tile([P, N], F32, name="vs_g", tag="ks_g_then_vs", align_bytes=64)
+        kw = [sb.tile([P, 2 * N], U8, name="kw%d" % o, align_bytes=64) for o in range(2)]
+        ks = [sb.tile([P, N], U8, name="ks%d" % o, align_bytes=64) for o in range(2)]
+        ks_g = [sb.tile([P, N], U8, name="ks_g%d" % o, tag="ks_g%d" % o, align_bytes=64) for o in range(2)]
+        halves = kw_g[:].bitcast(U16).rearrange("p (n o) -> p o n", o=2)
+        for o in range(2):
+            nc.vector.tensor_copy(ks_g[o][:], ks_pool[:, o, :].bitcast(U8).indirect(offsets[:]))
+            nc.vector.tensor_copy(kw[o][:].bitcast(U16), halves[:, o, :])
+            nc.vector.tensor_copy(
+                ks[o][:].bitcast(I32).rearrange("p (t g j) -> p t g j", t=4, j=2),
+                ks_g[o][:].bitcast(I32).rearrange("p (g t j) -> p t g j", t=4, j=2),
+            )
+        vs_g = sb.tile([P, N], F32, name="vs_g", tag="kw_then_vs", align_bytes=64)
         nc.vector.tensor_copy(by_place(vs_g[:].bitcast(U32)), vs_pool[:].bitcast(U32).indirect(offsets[:]))
         v_g = [
             sb.tile([P, N], BF16, name="v_g0", align_bytes=64),
-            sb.tile([P, N], BF16, name="v_g1", tag="vs_then_v", align_bytes=64),
+            sb.tile([P, N], BF16, name="v_g1", tag="ks_g1", align_bytes=64),
         ]
         nc.vector.tensor_copy(by_pair(v_g[1][:]), v_pool[1][:].indirect(offsets[:]))
 
@@ -94,44 +95,56 @@ def tile_attend_rel2_kb_srtq256n512t1024_kernel(tc, q_words, q_scales, k_words, 
         nc.scalar.activation(v_half[:], v_pool[0][:], ACT.Copy)
         nc.scalar.activation(by_place(v_g[0][:]), v_half[:].indirect(offsets[:]), ACT.Copy)
 
-        def turn(gathered, name):
-            turned = ps.tile([P, 4, P], F32, name=name)
+        def turn(gathered, name, bank):
+            turned = ps.tile([P, 4, P], F32, name=name, tag=bank)
             for t in range(4):
                 nc.tensor.transpose(turned[:, t, :], gathered[:, t * P : (t + 1) * P], ident[:])
             return turned
 
-        kb_t = turn(kb_g, "kb_t")
+        kb_t = turn(kb_g, "kb_t", "bank6")
         kb_col = sb.tile([P, 4], F32, name="kb_col")
         nc.scalar.copy(kb_col[:], kb_t[:, :, 96])
 
         v_in = sb.tile([P, 2, P * 4], BF16, name="v_in", align_bytes=64)
 
-        v0_t = ps.tile([P, 4, P], BF16, name="v_t")
+        v0_t = ps.tile([P, 4, P], BF16, name="v0_t", tag="bank7")
         for t in range(4):
             nc.tensor.transpose(v0_t[:, t, :], v_g[0][:, t * P : (t + 1) * P], ident_bf[:])
         nc.scalar.copy(v_in[:, 0, :].rearrange("p (e t) -> p e t", t=4), v0_t[:].rearrange("p t e -> p e t"))
 
         relu = sb.tile([P, 2, 4, P], F32, name="relu", align_bytes=64)
         p = sb.tile([P, 2, 4, P], F32, name="p", align_bytes=64)
-        for qb in range(2):
-            cols = slice(qb * P, (qb + 1) * P)
-            for t in range(4):
-                score = ps.tile([P, P], F32, name="score%d" % t)
-                for o in range(2):
-                    nc.tensor.matmul_mx(
-                        out=score[:],
-                        lhsT=kw[:, o, 2 * P * t : 2 * P * (t + 1)].bitcast(FP4X4),
-                        lhsT_scale=ks[:, o, P * t : P * (t + 1)],
-                        rhs=qw[:, o, cols].bitcast(FP8X4),
-                        rhs_scale=qs[:, o, cols],
-                        start=(o == 0),
-                        stop=(o == 1),
-                    )
-                nc.scalar.activation(relu[:, qb, t, :], score[:], ACT.Relu, bias=kb_col[:, t : t + 1])
-            nc.scalar.activation(p[:, qb], relu[:, qb], ACT.Square)
+        scores = [ps.tile([P, P], F32, name="score%d" % i, tag="bank%d" % i) for i in range(8)]
 
-        vs_t = turn(vs_g, "score0")
-        v1_t = ps.tile([P, 2, P], F32, name="v_t")
+        def score_pass(i, o):
+            qb, t = divmod(i, 4)
+            cols = slice(qb * P, (qb + 1) * P)
+            nc.tensor.matmul_mx(
+                out=scores[i][:],
+                lhsT=kw[o][:, 2 * P * t : 2 * P * (t + 1)].bitcast(FP4X4),
+                lhsT_scale=ks[o][:, P * t : P * (t + 1)],
+                rhs=qw[:, o, cols].bitcast(FP8X4),
+                rhs_scale=qs[:, o, cols],
+                start=(o == 0),
+                stop=(o == 1),
+            )
+
+        for i in range(7):
+            score_pass(i, 0)
+        for i in range(7):
+            score_pass(i, 1)
+        score_pass(7, 0)
+        score_pass(7, 1)
+        for qb in range(2):
+            for t in range(4):
+                nc.scalar.activation(relu[:, qb, t, :], scores[4 * qb + t][:], ACT.Relu, bias=kb_col[:, t : t + 1])
+                if qb == 1 and t % 2 == 1:
+                    nc.scalar.activation(p[:, qb, t - 1 : t + 1], relu[:, qb, t - 1 : t + 1], ACT.Square)
+            if qb == 0:
+                nc.scalar.activation(p[:, qb], relu[:, qb], ACT.Square)
+
+        vs_t = turn(vs_g, "vs_t", "bank0")
+        v1_t = ps.tile([P, 2, P], F32, name="v1_t", tag="bank1")
         v1_words = v_g[1][:].bitcast(F32)
         for u in range(2):
             nc.tensor.transpose(v1_t[:, u, :], v1_words[:, u * P : (u + 1) * P], ident[:])
@@ -149,34 +162,38 @@ def tile_attend_rel2_kb_srtq256n512t1024_kernel(tc, q_words, q_scales, k_words, 
                 vs_t[:, :, 0:1].to_broadcast([P, 4, P]).rearrange("p t q -> p q t"),
                 ALU.mult,
             )
+        nc.vector.quantize_mx(out=vq[:].bitcast(FP8X4), scales=vq_s[:], in_=v_in[:].rearrange("p h x -> p (h x)"))
         for qb in range(2):
             cols = slice(qb * P, (qb + 1) * P)
             nc.vector.quantize_mx(
                 out=wq[:, cols].bitcast(FP8X4), scales=wq_s[:, cols], in_=w_in[:, qb].rearrange("p q t -> p (q t)")
             )
-        nc.vector.quantize_mx(out=vq[:].bitcast(FP8X4), scales=vq_s[:], in_=v_in[:].rearrange("p h x -> p (h x)"))
 
-        p_t = ps.tile([P, 2, P], F32, name="kb_t")
-        for qb in range(2):
-            for t in range(4):
-                nc.tensor.matmul(p_t[:, qb, :], p[:, qb, t, :], ident[:], start=(t == 0), stop=(t == 3), is_transpose=True)
-        total = sb.tile([P, 2], F32, name="total")
+        total = [sb.tile([P, 1], F32, name="total%d" % qb) for qb in range(2)]
+        inv = [sb.tile([P, 1], F32, name="inv%d" % qb) for qb in range(2)]
         spent = sb.tile([P, 2, P], F32, name="spent")
         for qb in range(2):
-            nc.scalar.activation(spent[:, qb, :], p_t[:, qb, :], ACT.Copy, bias=1.0 / P, accum_out=total[:, qb : qb + 1])
-        inv = sb.tile([P, 2], F32, name="inv")
-        nc.vector.reciprocal(inv[:], total[:])
+            p_t = ps.tile([P, P], F32, name="p_t%d" % qb, tag="bank%d" % (2 + qb))
+            for t in range(4):
+                nc.tensor.matmul(p_t[:], p[:, qb, t, :], ident[:], start=(t == 0), stop=(t == 3), is_transpose=True)
+            nc.scalar.activation(spent[:, qb, :], p_t[:], ACT.Copy, bias=1.0 / P, accum_out=total[qb][:])
+            nc.vector.reciprocal(inv[qb][:], total[qb][:])
 
-        for qb in range(2):
-            cols = slice(qb * P, (qb + 1) * P)
-            y = ps.tile([P, DV], F32, name="y%d" % qb)
+        def product(qb, cols, name, bank):
+            rows = slice(qb * P, (qb + 1) * P)
+            y = ps.tile([P, cols.stop - cols.start], F32, name=name, tag=bank)
             nc.tensor.matmul_mx(
-                out=y[:], lhsT=wq[:, cols].bitcast(FP8X4), lhsT_scale=wq_s[:, cols],
-                rhs=vq[:].bitcast(FP8X4), rhs_scale=vq_s[:], start=True, stop=True,
+                out=y[:], lhsT=wq[:, rows].bitcast(FP8X4), lhsT_scale=wq_s[:, rows],
+                rhs=vq[:, cols].bitcast(FP8X4), rhs_scale=vq_s[:, cols], start=True, stop=True,
             )
-            res = sb.tile([P, DV], F32, name="res%d" % qb, align_bytes=64)
-            if qb == 0:
-                nc.scalar.activation(res[:], y[:], ACT.Copy, scale=inv[:, qb : qb + 1])
-            else:
-                nc.vector.tensor_scalar(res[:], y[:], inv[:, qb : qb + 1], None, ALU.mult)
-            (nc.scalar if qb == 0 else nc.sync).dma_start(out[0, cols, :], res[:])
+            return y
+
+        res = [sb.tile([P, DV], F32, name="res%d" % qb, align_bytes=64) for qb in range(2)]
+        y0 = product(0, slice(0, DV), "y0", "bank4")
+        nc.scalar.activation(res[0][:], y0[:], ACT.Copy, scale=inv[0][:])
+        nc.sync.dma_start(out[0, 0:P, :], res[0][:])
+        y1a = product(1, slice(0, P), "y1a", "bank5")
+        y1b = product(1, slice(P, DV), "y1b", "bank6")
+        nc.vector.tensor_scalar(res[1][:, 0:P], y1a[:], inv[1][:], None, ALU.mult)
+        nc.scalar.activation(res[1][:, P:DV], y1b[:], ACT.Copy, scale=inv[1][:])
+        nc.sync.dma_start(out[0, P:NQ, :], res[1][:])

@@ -26,41 +26,39 @@ def tile_attend_rel2_kb_srtq256n512t1024_kernel(tc, q_words, q_scales, k_words, 
         ps = ctx.enter_context(tc.psum_pool(name="ps", bufs=1))
 
         offsets = sb.tile([P, N // 16], U16, name="offsets")
-        kw_pool = sb.tile([P, T], I32, name="kw_pool", align_bytes=64)
-        ks_pool = sb.tile([P, 2, T // 4], I32, name="ks_pool", align_bytes=64)
-        kb_pool = sb.tile([P, T], F32, name="kb_pool", align_bytes=64)
-        vs_pool = sb.tile([P, T], F32, name="vs_pool", align_bytes=64)
-        v_pool = [sb.tile([P, T], F32, name="v_pool%d" % h, align_bytes=64) for h in range(2)]
-        qw = sb.tile([P, 2, NQ], I32, name="qw", align_bytes=64)
+        kw_pool = sb.tile([P, T], I32, name="kw_pool", tag="kw_then_v1", align_bytes=64)
+        ks_pool = sb.tile([P, T // 4], I32, name="ks_pool", align_bytes=64)
+        kb_pool = sb.tile([P, T], F32, name="kb_pool", tag="kb_then_vs_g", align_bytes=64)
+        vs_pool = sb.tile([P, T], F32, name="vs_pool", tag="vs_then_v_g", align_bytes=64)
+        v_pool0 = sb.tile([P, T], F32, name="v_pool0", align_bytes=64)
         qs = sb.tile([P, 2, NQ], U8, name="qs", align_bytes=64)
         ident = sb.tile([P, P], F32, name="ident", align_bytes=64)
 
         warm_in = sb.tile([P, 1], F32, name="warm_in")
-        warm_out = sb.tile([P, 1], F32, name="warm_out")
+        warm_out = sb.tile([P, 1], F32, name="warm_out", tag="warm_then_qw", align_bytes=64)
         nc.gpsimd.memset(warm_in[:], 0.0)
         nc.scalar.activation(warm_out[:], warm_in[:], ACT.Relu)
-
-        nc.vector.memset(ks_pool[:], 0)
-        nc.vector.memset(kb_pool[0:96, :].bitcast(I32), 0)
-        nc.vector.memset(vs_pool[:].bitcast(I32), 0)
-        nc.vector.memset(qs[:].bitcast(I32), 0)
         make_identity(nc, ident[:])
-        nc.gpsimd.dma_start(v_pool[1][:], vT[P : 2 * P, :])
-        ident_bf = sb.tile([P, P], BF16, name="ident_bf", align_bytes=64)
-        nc.scalar.copy(ident_bf[:], ident[:])
+        nc.vector.memset(ks_pool[:], 0)
+        nc.vector.memset(kb_pool[:].bitcast(I32), 0)
+        nc.vector.memset(qs[:].bitcast(I32), 0)
+        nc.vector.memset(vs_pool[:].bitcast(I32), 0)
 
         nc.sync.dma_start(offsets[:], offs)
-        nc.sync.dma_start(kb_pool[96:P, :], kb[96:P, :])
         nc.sync.dma_start(kw_pool[:], k_words[0].rearrange("g t b -> g (t b)").bitcast(I32))
-        nc.sync.dma_start(v_pool[0][:], vT[0:P, :])
-        nc.sync.dma_start(qw[:], q_words[0].rearrange("o g q r -> g o (q r)").bitcast(I32))
-        ks_rows = k_scales.rearrange("o (Q r) t -> r Q o t", r=4)
-        for r in range(4):
-            nc.scalar.dma_start(ks_pool[r:P:32], ks_rows[r].bitcast(I32))
-        nc.sync.dma_start(vs_pool[0:1, :], vs[0:1, :])
+        nc.sync.dma_start(v_pool0[:], vT[0:P, :])
+        ks_rows = k_scales.rearrange("o (Q r) t -> Q o r t", r=4)
+        for Q in range(4):
+            nc.sync.dma_start(ks_pool[32 * Q : 32 * Q + 8, :], ks_rows[Q].bitcast(I32))
+        qw = sb.tile([P, 2, NQ], I32, name="qw", tag="warm_then_qw", align_bytes=64)
+        nc.scalar.dma_start(qw[:], q_words[0].rearrange("o g q r -> g o (q r)").bitcast(I32))
+        ident_bf = sb.tile([P, P], BF16, name="ident_bf", align_bytes=64)
+        nc.scalar.copy(ident_bf[:], ident[:])
+        nc.sync.dma_start(kb_pool[0:1, :], kb[0:1, :])
         qs_rows = q_scales[0].rearrange("o (Q r) q -> r Q o q", r=4)
         for r in range(4):
             nc.sync.dma_start(qs[r:P:32].bitcast(I32), qs_rows[r].bitcast(I32))
+        nc.sync.dma_start(vs_pool[0:1, :], vs[0:1, :])
 
         def by_place(ap):
             return ap.rearrange("p (t g j) -> p g t j", t=4, j=8)
@@ -68,31 +66,35 @@ def tile_attend_rel2_kb_srtq256n512t1024_kernel(tc, q_words, q_scales, k_words, 
         def by_pair(ap):
             return ap.rearrange("p (u g j b) -> p g u b j", u=2, j=8, b=2)
 
-        kb_g = sb.tile([P, N], F32, name="kb_g", align_bytes=64)
-        nc.vector.tensor_copy(by_place(kb_g[:].bitcast(U32)), kb_pool[:].bitcast(U32).indirect(offsets[:]))
-        kw_g = sb.tile([P, N], U32, name="kw_g", tag="kw_then_vs", align_bytes=64)
+        kw_g = sb.tile([P, N], U32, name="kw_g", align_bytes=64)
         nc.vector.tensor_copy(by_place(kw_g[:]), kw_pool[:].bitcast(U32).indirect(offsets[:]))
+        v_pool1 = sb.tile([P, T], F32, name="v_pool1", tag="kw_then_v1", align_bytes=64)
+        nc.sync.dma_start(v_pool1[:], vT[P : 2 * P, :])
+        ks_g = sb.tile([P, N], U8, name="ks_g", tag="ks_g_then_kb", align_bytes=64)
+        nc.vector.tensor_copy(ks_g[:], ks_pool[:].bitcast(U8).indirect(offsets[:]))
         kw = [sb.tile([P, 2 * N], U8, name="kw%d" % o, align_bytes=64) for o in range(2)]
         ks = [sb.tile([P, N], U8, name="ks%d" % o, align_bytes=64) for o in range(2)]
-        ks_g = [sb.tile([P, N], U8, name="ks_g%d" % o, tag="ks_g%d" % o, align_bytes=64) for o in range(2)]
         halves = kw_g[:].bitcast(U16).rearrange("p (n o) -> p o n", o=2)
-        for o in range(2):
-            nc.vector.tensor_copy(ks_g[o][:], ks_pool[:, o, :].bitcast(U8).indirect(offsets[:]))
-            nc.vector.tensor_copy(kw[o][:].bitcast(U16), halves[:, o, :])
-            nc.vector.tensor_copy(
-                ks[o][:].bitcast(I32).rearrange("p (t g j) -> p t g j", t=4, j=2),
-                ks_g[o][:].bitcast(I32).rearrange("p (g t j) -> p t g j", t=4, j=2),
-            )
-        vs_g = sb.tile([P, N], F32, name="vs_g", tag="kw_then_vs", align_bytes=64)
+        nc.vector.tensor_copy(kw[0][:].bitcast(U16), halves[:, 0, :])
+        nc.vector.tensor_copy(
+            ks[0][:].bitcast(I32).rearrange("p (t g j) -> p t g j", t=4, j=2),
+            ks_g[:].bitcast(I32).rearrange("p (g t j) -> p t g j", t=4, j=2),
+        )
+        nc.sync.dma_start(ks[1][0:100, :].bitcast(I32), ks[0][4:104, :].bitcast(I32))
+
+        kb_g = sb.tile([P, N], F32, name="kb_g", tag="ks_g_then_kb", align_bytes=64)
+        nc.vector.tensor_copy(by_place(kb_g[:].bitcast(U32)), kb_pool[:].bitcast(U32).indirect(offsets[:]))
+        nc.vector.tensor_copy(kw[1][:].bitcast(U16), halves[:, 1, :])
+        vs_g = sb.tile([P, N], F32, name="vs_g", tag="kb_then_vs_g", align_bytes=64)
         nc.vector.tensor_copy(by_place(vs_g[:].bitcast(U32)), vs_pool[:].bitcast(U32).indirect(offsets[:]))
         v_g = [
             sb.tile([P, N], BF16, name="v_g0", align_bytes=64),
-            sb.tile([P, N], BF16, name="v_g1", tag="ks_g1", align_bytes=64),
+            sb.tile([P, N], BF16, name="v_g1", tag="vs_then_v_g", align_bytes=64),
         ]
-        nc.vector.tensor_copy(by_pair(v_g[1][:]), v_pool[1][:].indirect(offsets[:]))
+        nc.vector.tensor_copy(by_pair(v_g[1][:]), v_pool1[:].indirect(offsets[:]))
 
         v_half = sb.tile([P, T], BF16, name="v_half", align_bytes=64)
-        nc.scalar.activation(v_half[:], v_pool[0][:], ACT.Copy)
+        nc.scalar.activation(v_half[:], v_pool0[:], ACT.Copy)
         nc.scalar.activation(by_place(v_g[0][:]), v_half[:].indirect(offsets[:]), ACT.Copy)
 
         def turn(gathered, name, bank):
@@ -101,20 +103,10 @@ def tile_attend_rel2_kb_srtq256n512t1024_kernel(tc, q_words, q_scales, k_words, 
                 nc.tensor.transpose(turned[:, t, :], gathered[:, t * P : (t + 1) * P], ident[:])
             return turned
 
-        kb_t = turn(kb_g, "kb_t", "bank6")
-        kb_col = sb.tile([P, 4], F32, name="kb_col")
-        nc.scalar.copy(kb_col[:], kb_t[:, :, 96])
-
-        v_in = sb.tile([P, 2, P * 4], BF16, name="v_in", align_bytes=64)
-
-        v0_t = ps.tile([P, 4, P], BF16, name="v0_t", tag="bank7")
-        for t in range(4):
-            nc.tensor.transpose(v0_t[:, t, :], v_g[0][:, t * P : (t + 1) * P], ident_bf[:])
-        nc.scalar.copy(v_in[:, 0, :].rearrange("p (e t) -> p e t", t=4), v0_t[:].rearrange("p t e -> p e t"))
-
         relu = sb.tile([P, 2, 4, P], F32, name="relu", align_bytes=64)
         p = sb.tile([P, 2, 4, P], F32, name="p", align_bytes=64)
-        scores = [ps.tile([P, P], F32, name="score%d" % i, tag="bank%d" % i) for i in range(8)]
+        score_bank = [0, 1, 2, 3, 4, 5, 7, 0]
+        scores = {}
 
         def score_pass(i, o):
             qb, t = divmod(i, 4)
@@ -129,22 +121,38 @@ def tile_attend_rel2_kb_srtq256n512t1024_kernel(tc, q_words, q_scales, k_words, 
                 stop=(o == 1),
             )
 
-        for i in range(7):
+        def open_score(i):
+            scores[i] = ps.tile([P, P], F32, name="score%d" % i, tag="bank%d" % score_bank[i])
             score_pass(i, 0)
-        for i in range(7):
-            score_pass(i, 1)
-        score_pass(7, 0)
-        score_pass(7, 1)
+
+        for i in range(6):
+            open_score(i)
+
+        kb_t = turn(kb_g, "kb_t", "bank7")
+        kb_col = sb.tile([P, 4], F32, name="kb_col")
+        nc.scalar.copy(kb_col[:], kb_t[:, :, 0])
+
+        v_in = sb.tile([P, 2, P * 4], BF16, name="v_in", align_bytes=64)
+
+        v0_t = ps.tile([P, 4, P], BF16, name="v0_t", tag="bank6")
+        for t in range(4):
+            nc.tensor.transpose(v0_t[:, t, :], v_g[0][:, t * P : (t + 1) * P], ident_bf[:])
+        nc.scalar.copy(v_in[:, 0, :].rearrange("p (e t) -> p e t", t=4), v0_t[:].rearrange("p t e -> p e t"))
+
         for qb in range(2):
             for t in range(4):
+                i = 4 * qb + t
+                if i >= 6:
+                    open_score(i)
+                score_pass(i, 1)
                 nc.scalar.activation(relu[:, qb, t, :], scores[4 * qb + t][:], ACT.Relu, bias=kb_col[:, t : t + 1])
                 if qb == 1 and t % 2 == 1:
                     nc.scalar.activation(p[:, qb, t - 1 : t + 1], relu[:, qb, t - 1 : t + 1], ACT.Square)
             if qb == 0:
                 nc.scalar.activation(p[:, qb], relu[:, qb], ACT.Square)
 
-        vs_t = turn(vs_g, "vs_t", "bank0")
-        v1_t = ps.tile([P, 2, P], F32, name="v1_t", tag="bank1")
+        vs_t = turn(vs_g, "vs_t", "bank1")
+        v1_t = ps.tile([P, 2, P], F32, name="v1_t", tag="bank2")
         v1_words = v_g[1][:].bitcast(F32)
         for u in range(2):
             nc.tensor.transpose(v1_t[:, u, :], v1_words[:, u * P : (u + 1) * P], ident[:])
@@ -173,7 +181,7 @@ def tile_attend_rel2_kb_srtq256n512t1024_kernel(tc, q_words, q_scales, k_words, 
         inv = [sb.tile([P, 1], F32, name="inv%d" % qb) for qb in range(2)]
         spent = sb.tile([P, 2, P], F32, name="spent")
         for qb in range(2):
-            p_t = ps.tile([P, P], F32, name="p_t%d" % qb, tag="bank%d" % (2 + qb))
+            p_t = ps.tile([P, P], F32, name="p_t%d" % qb, tag="bank%d" % (3 + qb))
             for t in range(4):
                 nc.tensor.matmul(p_t[:], p[:, qb, t, :], ident[:], start=(t == 0), stop=(t == 3), is_transpose=True)
             nc.scalar.activation(spent[:, qb, :], p_t[:], ACT.Copy, bias=1.0 / P, accum_out=total[qb][:])
@@ -189,10 +197,10 @@ def tile_attend_rel2_kb_srtq256n512t1024_kernel(tc, q_words, q_scales, k_words, 
             return y
 
         res = [sb.tile([P, DV], F32, name="res%d" % qb, align_bytes=64) for qb in range(2)]
-        y0 = product(0, slice(0, DV), "y0", "bank4")
+        y0 = product(0, slice(0, DV), "y0", "bank5")
         nc.scalar.activation(res[0][:], y0[:], ACT.Copy, scale=inv[0][:])
         nc.sync.dma_start(out[0, 0:P, :], res[0][:])
-        y1a = product(1, slice(0, P), "y1a", "bank5")
+        y1a = product(1, slice(0, P), "y1a", "bank7")
         y1b = product(1, slice(P, DV), "y1b", "bank6")
         nc.vector.tensor_scalar(res[1][:, 0:P], y1a[:], inv[1][:], None, ALU.mult)
         nc.scalar.activation(res[1][:, P:DV], y1b[:], ACT.Copy, scale=inv[1][:])

@@ -26,35 +26,33 @@ def tile_attend_rel2_kb_srtq256n512t1024_kernel(tc, q_words, q_scales, k_words, 
         ps = ctx.enter_context(tc.psum_pool(name="ps", bufs=1))
 
         offsets = sb.tile([P, N // 16], U16, name="offsets")
-        kw_pool = sb.tile([P, T], I32, name="kw_pool", tag="kw_then_v1", align_bytes=64)
-        ks_pool = sb.tile([P, T // 4], I32, name="ks_pool", align_bytes=64)
-        kb_pool = sb.tile([P, T], F32, name="kb_pool", tag="kb_then_vs_g", align_bytes=64)
+        ks_pool = sb.tile([P, T // 4], I32, name="ks_pool", tag="ks_then_kw_g", align_bytes=64)
+        kb_pool = sb.tile([P, T], F32, name="kb_pool", tag="kb_then_qw", align_bytes=64)
+        kw_pool = sb.tile([P, T], I32, name="kw_pool", tag="kw_then_vs_g", align_bytes=64)
         vs_pool = sb.tile([P, T], F32, name="vs_pool", tag="vs_then_v_g", align_bytes=64)
-        v_pool0 = sb.tile([P, T], F32, name="v_pool0", align_bytes=64)
         qs = sb.tile([P, 2, NQ], U8, name="qs", align_bytes=64)
         ident = sb.tile([P, P], F32, name="ident", align_bytes=64)
+        ident_bf = sb.tile([P, P], BF16, name="ident_bf", align_bytes=64)
 
         warm_in = sb.tile([P, 1], F32, name="warm_in")
-        warm_out = sb.tile([P, 1], F32, name="warm_out", tag="warm_then_qw", align_bytes=64)
+        warm_out = sb.tile([P, 1], F32, name="warm_out", tag="warm_then_v0", align_bytes=64)
+        nc.gpsimd.memset(ks_pool[:], 0)
         nc.gpsimd.memset(warm_in[:], 0.0)
-        nc.scalar.activation(warm_out[:], warm_in[:], ACT.Relu)
         make_identity(nc, ident[:])
-        nc.vector.memset(ks_pool[:], 0)
-        nc.vector.memset(kb_pool[:].bitcast(I32), 0)
+        make_identity(nc, ident_bf[:])
+        nc.vector.memset(kb_pool[0:96, :].bitcast(I32), 0)
         nc.vector.memset(qs[:].bitcast(I32), 0)
         nc.vector.memset(vs_pool[:].bitcast(I32), 0)
 
         nc.sync.dma_start(offsets[:], offs)
+        nc.sync.dma_start(kb_pool[96:P, :], kb[96:P, :])
         nc.sync.dma_start(kw_pool[:], k_words[0].rearrange("g t b -> g (t b)").bitcast(I32))
-        nc.sync.dma_start(v_pool0[:], vT[0:P, :])
         ks_rows = k_scales.rearrange("o (Q r) t -> Q o r t", r=4)
         for Q in range(4):
-            nc.sync.dma_start(ks_pool[32 * Q : 32 * Q + 8, :], ks_rows[Q].bitcast(I32))
-        qw = sb.tile([P, 2, NQ], I32, name="qw", tag="warm_then_qw", align_bytes=64)
-        nc.scalar.dma_start(qw[:], q_words[0].rearrange("o g q r -> g o (q r)").bitcast(I32))
-        ident_bf = sb.tile([P, P], BF16, name="ident_bf", align_bytes=64)
-        nc.scalar.copy(ident_bf[:], ident[:])
-        nc.sync.dma_start(kb_pool[0:1, :], kb[0:1, :])
+            nc.scalar.dma_start(ks_pool[32 * Q : 32 * Q + 8, :], ks_rows[Q].bitcast(I32))
+        nc.scalar.activation(warm_out[:], warm_in[:], ACT.Relu)
+        v_pool0 = sb.tile([P, T], F32, name="v_pool0", tag="warm_then_v0", align_bytes=64)
+        nc.scalar.dma_start(v_pool0[:], vT[0:P, :])
         qs_rows = q_scales[0].rearrange("o (Q r) q -> r Q o q", r=4)
         for r in range(4):
             nc.sync.dma_start(qs[r:P:32].bitcast(I32), qs_rows[r].bitcast(I32))
@@ -66,26 +64,27 @@ def tile_attend_rel2_kb_srtq256n512t1024_kernel(tc, q_words, q_scales, k_words, 
         def by_pair(ap):
             return ap.rearrange("p (u g j b) -> p g u b j", u=2, j=8, b=2)
 
-        kw_g = sb.tile([P, N], U32, name="kw_g", align_bytes=64)
-        nc.vector.tensor_copy(by_place(kw_g[:]), kw_pool[:].bitcast(U32).indirect(offsets[:]))
-        v_pool1 = sb.tile([P, T], F32, name="v_pool1", tag="kw_then_v1", align_bytes=64)
-        nc.sync.dma_start(v_pool1[:], vT[P : 2 * P, :])
-        ks_g = sb.tile([P, N], U8, name="ks_g", tag="ks_g_then_kb", align_bytes=64)
+        kb_g = sb.tile([P, N], F32, name="kb_g", align_bytes=64)
+        nc.vector.tensor_copy(by_place(kb_g[:].bitcast(U32)), kb_pool[:].bitcast(U32).indirect(offsets[:]))
+        qw = sb.tile([P, 2, NQ], I32, name="qw", tag="kb_then_qw", align_bytes=64)
+        nc.sync.dma_start(qw[:], q_words[0].rearrange("o g q r -> g o (q r)").bitcast(I32))
+        ks_g = sb.tile([P, N], U8, name="ks_g", tag="ks_g_then_v1", align_bytes=64)
         nc.vector.tensor_copy(ks_g[:], ks_pool[:].bitcast(U8).indirect(offsets[:]))
         kw = [sb.tile([P, 2 * N], U8, name="kw%d" % o, align_bytes=64) for o in range(2)]
         ks = [sb.tile([P, N], U8, name="ks%d" % o, align_bytes=64) for o in range(2)]
-        halves = kw_g[:].bitcast(U16).rearrange("p (n o) -> p o n", o=2)
-        nc.vector.tensor_copy(kw[0][:].bitcast(U16), halves[:, 0, :])
         nc.vector.tensor_copy(
             ks[0][:].bitcast(I32).rearrange("p (t g j) -> p t g j", t=4, j=2),
             ks_g[:].bitcast(I32).rearrange("p (g t j) -> p t g j", t=4, j=2),
         )
         nc.sync.dma_start(ks[1][0:100, :].bitcast(I32), ks[0][4:104, :].bitcast(I32))
-
-        kb_g = sb.tile([P, N], F32, name="kb_g", tag="ks_g_then_kb", align_bytes=64)
-        nc.vector.tensor_copy(by_place(kb_g[:].bitcast(U32)), kb_pool[:].bitcast(U32).indirect(offsets[:]))
-        nc.vector.tensor_copy(kw[1][:].bitcast(U16), halves[:, 1, :])
-        vs_g = sb.tile([P, N], F32, name="vs_g", tag="kb_then_vs_g", align_bytes=64)
+        v_pool1 = sb.tile([P, T], F32, name="v_pool1", tag="ks_g_then_v1", align_bytes=64)
+        nc.sync.dma_start(v_pool1[:], vT[P : 2 * P, :])
+        kw_g = sb.tile([P, N], U32, name="kw_g", tag="ks_then_kw_g", align_bytes=64)
+        nc.vector.tensor_copy(by_place(kw_g[:]), kw_pool[:].bitcast(U32).indirect(offsets[:]))
+        halves = kw_g[:].bitcast(U16).rearrange("p (n o) -> p o n", o=2)
+        for o in range(2):
+            nc.vector.tensor_copy(kw[o][:].bitcast(U16), halves[:, o, :])
+        vs_g = sb.tile([P, N], F32, name="vs_g", tag="kw_then_vs_g", align_bytes=64)
         nc.vector.tensor_copy(by_place(vs_g[:].bitcast(U32)), vs_pool[:].bitcast(U32).indirect(offsets[:]))
         v_g = [
             sb.tile([P, N], BF16, name="v_g0", align_bytes=64),
@@ -103,9 +102,13 @@ def tile_attend_rel2_kb_srtq256n512t1024_kernel(tc, q_words, q_scales, k_words, 
                 nc.tensor.transpose(turned[:, t, :], gathered[:, t * P : (t + 1) * P], ident[:])
             return turned
 
+        kb_t = turn(kb_g, "kb_t", "bank7")
+        kb_col = sb.tile([P, 4], F32, name="kb_col")
+        nc.scalar.copy(kb_col[:], kb_t[:, :, 96])
+
         relu = sb.tile([P, 2, 4, P], F32, name="relu", align_bytes=64)
         p = sb.tile([P, 2, 4, P], F32, name="p", align_bytes=64)
-        score_bank = [0, 1, 2, 3, 4, 5, 7, 0]
+        score_bank = [0, 1, 2, 3, 4, 5, 6, 7]
         scores = {}
 
         def score_pass(i, o):
@@ -125,24 +128,13 @@ def tile_attend_rel2_kb_srtq256n512t1024_kernel(tc, q_words, q_scales, k_words, 
             scores[i] = ps.tile([P, P], F32, name="score%d" % i, tag="bank%d" % score_bank[i])
             score_pass(i, 0)
 
-        for i in range(6):
+        for i in range(7):
             open_score(i)
-
-        kb_t = turn(kb_g, "kb_t", "bank7")
-        kb_col = sb.tile([P, 4], F32, name="kb_col")
-        nc.scalar.copy(kb_col[:], kb_t[:, :, 0])
-
-        v_in = sb.tile([P, 2, P * 4], BF16, name="v_in", align_bytes=64)
-
-        v0_t = ps.tile([P, 4, P], BF16, name="v0_t", tag="bank6")
-        for t in range(4):
-            nc.tensor.transpose(v0_t[:, t, :], v_g[0][:, t * P : (t + 1) * P], ident_bf[:])
-        nc.scalar.copy(v_in[:, 0, :].rearrange("p (e t) -> p e t", t=4), v0_t[:].rearrange("p t e -> p e t"))
 
         for qb in range(2):
             for t in range(4):
                 i = 4 * qb + t
-                if i >= 6:
+                if i == 7:
                     open_score(i)
                 score_pass(i, 1)
                 nc.scalar.activation(relu[:, qb, t, :], scores[4 * qb + t][:], ACT.Relu, bias=kb_col[:, t : t + 1])
@@ -152,6 +144,13 @@ def tile_attend_rel2_kb_srtq256n512t1024_kernel(tc, q_words, q_scales, k_words, 
                 nc.scalar.activation(p[:, qb], relu[:, qb], ACT.Square)
 
         vs_t = turn(vs_g, "vs_t", "bank1")
+        v_in = sb.tile([P, 2, P * 4], BF16, name="v_in", align_bytes=64)
+
+        v0_t = ps.tile([P, 4, P], BF16, name="v0_t", tag="bank0")
+        for t in range(4):
+            nc.tensor.transpose(v0_t[:, t, :], v_g[0][:, t * P : (t + 1) * P], ident_bf[:])
+        nc.scalar.copy(v_in[:, 0, :].rearrange("p (e t) -> p e t", t=4), v0_t[:].rearrange("p t e -> p e t"))
+
         v1_t = ps.tile([P, 2, P], F32, name="v1_t", tag="bank2")
         v1_words = v_g[1][:].bitcast(F32)
         for u in range(2):

@@ -35,7 +35,7 @@ def tile_attend_rel2_kb_srtq256n512t1024_kernel(tc, q_words, q_scales, k_words, 
         ident_bf = sb.tile([P, P], BF16, name="ident_bf", align_bytes=64)
 
         warm_in = sb.tile([P, 1], F32, name="warm_in")
-        warm_out = sb.tile([P, 1], F32, name="warm_out", tag="warm_then_v0", align_bytes=64)
+        warm_out = sb.tile([P, 1], F32, name="warm_out")
         nc.gpsimd.memset(ks_pool[:], 0)
         nc.gpsimd.memset(warm_in[:], 0.0)
         make_identity(nc, ident[:])
@@ -49,10 +49,10 @@ def tile_attend_rel2_kb_srtq256n512t1024_kernel(tc, q_words, q_scales, k_words, 
         nc.sync.dma_start(kw_pool[:], k_words[0].rearrange("g t b -> g (t b)").bitcast(I32))
         ks_rows = k_scales.rearrange("o (Q r) t -> Q o r t", r=4)
         for Q in range(4):
-            nc.scalar.dma_start(ks_pool[32 * Q : 32 * Q + 8, :], ks_rows[Q].bitcast(I32))
+            nc.sync.dma_start(ks_pool[32 * Q : 32 * Q + 8, :], ks_rows[Q].bitcast(I32))
         nc.scalar.activation(warm_out[:], warm_in[:], ACT.Relu)
-        v_pool0 = sb.tile([P, T], F32, name="v_pool0", tag="warm_then_v0", align_bytes=64)
-        nc.scalar.dma_start(v_pool0[:], vT[0:P, :])
+        v_pool0 = sb.tile([P, T], F32, name="v_pool0", align_bytes=64)
+        nc.sync.dma_start(v_pool0[:], vT[0:P, :])
         qs_rows = q_scales[0].rearrange("o (Q r) q -> r Q o q", r=4)
         for r in range(4):
             nc.sync.dma_start(qs[r:P:32].bitcast(I32), qs_rows[r].bitcast(I32))
@@ -76,7 +76,8 @@ def tile_attend_rel2_kb_srtq256n512t1024_kernel(tc, q_words, q_scales, k_words, 
             ks[0][:].bitcast(I32).rearrange("p (t g j) -> p t g j", t=4, j=2),
             ks_g[:].bitcast(I32).rearrange("p (g t j) -> p t g j", t=4, j=2),
         )
-        nc.sync.dma_start(ks[1][0:100, :].bitcast(I32), ks[0][4:104, :].bitcast(I32))
+        for Q in range(4):
+            nc.sync.dma_start(ks[1][32 * Q : 32 * Q + 4, :].bitcast(I32), ks[0][32 * Q + 4 : 32 * Q + 8, :].bitcast(I32))
         v_pool1 = sb.tile([P, T], F32, name="v_pool1", tag="ks_g_then_v1", align_bytes=64)
         nc.sync.dma_start(v_pool1[:], vT[P : 2 * P, :])
         kw_g = sb.tile([P, N], U32, name="kw_g", tag="ks_then_kw_g", align_bytes=64)

@@ -107,7 +107,8 @@ def tile_attend_rel2_kb_srtq256n512t1024_kernel(tc, q_words, q_scales, k_words, 
         kb_col = sb.tile([P, 4], F32, name="kb_col")
         nc.scalar.copy(kb_col[:], kb_t[:, :, 96])
 
-        relu = sb.tile([P, 2, 4, P], F32, name="relu", align_bytes=64)
+        relu = sb.tile([P, 6, P], F32, name="relu", align_bytes=64)
+        relu_last = sb.tile([P, 2, P], F32, name="relu_last", tag="ks_g_then_v1", align_bytes=64)
         p = sb.tile([P, 2, 4, P], F32, name="p", align_bytes=64)
         score_bank = [0, 1, 2, 3, 4, 5, 6, 7]
         scores = {}
@@ -138,11 +139,16 @@ def tile_attend_rel2_kb_srtq256n512t1024_kernel(tc, q_words, q_scales, k_words, 
                 if i == 7:
                     open_score(i)
                 score_pass(i, 1)
-                nc.scalar.activation(relu[:, qb, t, :], scores[4 * qb + t][:], ACT.Relu, bias=kb_col[:, t : t + 1])
-                if qb == 1 and t % 2 == 1:
-                    nc.scalar.activation(p[:, qb, t - 1 : t + 1], relu[:, qb, t - 1 : t + 1], ACT.Square)
-            if qb == 0:
-                nc.scalar.activation(p[:, qb], relu[:, qb], ACT.Square)
+                if i < 6:
+                    nc.scalar.activation(relu[:, i, :], scores[i][:], ACT.Relu, bias=kb_col[:, t : t + 1])
+                else:
+                    nc.vector.tensor_scalar(relu_last[:, i - 6, :], scores[i][:], kb_col[:, t : t + 1], 0.0, ALU.add, ALU.max)
+                if i == 3:
+                    nc.scalar.activation(p[:, 0], relu[:, 0:4], ACT.Square)
+                if i == 5:
+                    nc.scalar.activation(p[:, 1, 0:2], relu[:, 4:6], ACT.Square)
+                if i == 7:
+                    nc.scalar.activation(p[:, 1, 2:4], relu_last[:], ACT.Square)
 
         vs_t = turn(vs_g, "vs_t", "bank1")
         v_in = sb.tile([P, 2, P * 4], BF16, name="v_in", align_bytes=64)

@@ -202,12 +202,13 @@ def tile_attend_rel2_kb_srtq256n512t1024_kernel(tc, q_words, q_scales, k_words, 
             )
             return y
 
-        res = [sb.tile([P, DV], F32, name="res%d" % qb, align_bytes=64) for qb in range(2)]
-        y0 = product(0, slice(0, DV), "y0", "bank5")
-        nc.scalar.activation(res[0][:], y0[:], ACT.Copy, scale=inv[0][:])
-        nc.sync.dma_start(out[0, 0:P, :], res[0][:])
-        y1a = product(1, slice(0, P), "y1a", "bank7")
-        y1b = product(1, slice(P, DV), "y1b", "bank6")
-        nc.vector.tensor_scalar(res[1][:, 0:P], y1a[:], inv[1][:], None, ALU.mult)
-        nc.scalar.activation(res[1][:, P:DV], y1b[:], ACT.Copy, scale=inv[1][:])
-        nc.sync.dma_start(out[0, P:NQ, :], res[1][:])
+        for qb in range(2):
+            rows = slice(qb * P, (qb + 1) * P)
+            left, right = slice(0, P), slice(P, DV)
+            res = sb.tile([P, DV], F32, name="res%d" % qb, align_bytes=64)
+            y_left = product(qb, left, "y%d_left" % qb, ("bank5", "bank7")[qb])
+            y_right = product(qb, right, "y%d_right" % qb, ("bank0", "bank6")[qb])
+            nc.vector.tensor_scalar(res[:, left], y_left[:], inv[qb][:], None, ALU.mult)
+            nc.scalar.activation(res[:, right], y_right[:], ACT.Copy, scale=inv[qb][:])
+            nc.sync.dma_start(out[0, rows, left], res[:, left])
+            nc.scalar.dma_start(out[0, rows, right], res[:, right])

@@ -15,6 +15,7 @@ ACT = mybir.ActivationFunctionType
 ALU = mybir.AluOpType
 
 P = 128
+ROW = P - 1
 N, T, D, DV, NQ = 512, 1024, 1024, 256, 256
 FLOPS = 2 * NQ * N * D + 2 * NQ * N * DV
 
@@ -34,29 +35,24 @@ def tile_attend_rel2_kb_srtq256n512t1024_kernel(tc, q_words, q_scales, k_words, 
         ident = sb.tile([P, P], F32, name="ident", align_bytes=64)
         ident_bf = sb.tile([P, P], BF16, name="ident_bf", align_bytes=64)
 
-        warm_in = sb.tile([P, 1], F32, name="warm_in")
-        warm_out = sb.tile([P, 1], F32, name="warm_out")
-        nc.gpsimd.memset(ks_pool[:], 0)
-        nc.gpsimd.memset(warm_in[:], 0.0)
         make_identity(nc, ident[:])
-        make_identity(nc, ident_bf[:])
-        nc.vector.memset(kb_pool[0:96, :].bitcast(I32), 0)
-        nc.vector.memset(qs[:].bitcast(I32), 0)
-        nc.vector.memset(vs_pool[:].bitcast(I32), 0)
+        nc.scalar.activation(ident_bf[:], ident[:], ACT.Copy)
+        nc.vector.memset(ks_pool[:], 0)
+        nc.vector.memset(kb_pool[0:ROW, :].bitcast(I32), 0)
+        nc.vector.memset(vs_pool[0:ROW, :].bitcast(I32), 0)
 
         nc.sync.dma_start(offsets[:], offs)
-        nc.sync.dma_start(kb_pool[96:P, :], kb[96:P, :])
-        nc.sync.dma_start(kw_pool[:], k_words[0].rearrange("g t b -> g (t b)").bitcast(I32))
+        nc.sync.dma_start(kb_pool[ROW:P, :], kb[0:1, :])
         ks_rows = k_scales.rearrange("o (Q r) t -> Q o r t", r=4)
         for Q in range(4):
             nc.sync.dma_start(ks_pool[32 * Q : 32 * Q + 8, :], ks_rows[Q].bitcast(I32))
-        nc.scalar.activation(warm_out[:], warm_in[:], ACT.Relu)
+        nc.sync.dma_start(kw_pool[:], k_words[0].rearrange("g t b -> g (t b)").bitcast(I32))
         v_pool0 = sb.tile([P, T], F32, name="v_pool0", align_bytes=64)
         nc.sync.dma_start(v_pool0[:], vT[0:P, :])
         qs_rows = q_scales[0].rearrange("o (Q r) q -> r Q o q", r=4)
         for r in range(4):
             nc.sync.dma_start(qs[r:P:32].bitcast(I32), qs_rows[r].bitcast(I32))
-        nc.sync.dma_start(vs_pool[0:1, :], vs[0:1, :])
+        nc.sync.dma_start(vs_pool[ROW:P, :], vs[0:1, :])
 
         def by_place(ap):
             return ap.rearrange("p (t g j) -> p g t j", t=4, j=8)
@@ -105,7 +101,7 @@ def tile_attend_rel2_kb_srtq256n512t1024_kernel(tc, q_words, q_scales, k_words, 
 
         kb_t = turn(kb_g, "kb_t", "bank7")
         kb_col = sb.tile([P, 4], F32, name="kb_col")
-        nc.scalar.copy(kb_col[:], kb_t[:, :, 96])
+        nc.scalar.copy(kb_col[:], kb_t[:, :, ROW])
 
         relu = sb.tile([P, 6, P], F32, name="relu", align_bytes=64)
         relu_last = sb.tile([P, 2, P], F32, name="relu_last", tag="ks_g_then_v1", align_bytes=64)
@@ -173,7 +169,7 @@ def tile_attend_rel2_kb_srtq256n512t1024_kernel(tc, q_words, q_scales, k_words, 
             nc.vector.tensor_tensor(
                 w_in[:, qb],
                 p[:, qb].rearrange("p t q -> p q t"),
-                vs_t[:, :, 0:1].to_broadcast([P, 4, P]).rearrange("p t q -> p q t"),
+                vs_t[:, :, ROW:P].to_broadcast([P, 4, P]).rearrange("p t q -> p q t"),
                 ALU.mult,
             )
         nc.vector.quantize_mx(out=vq[:].bitcast(FP8X4), scales=vq_s[:], in_=v_in[:].rearrange("p h x -> p (h x)"))

@@ -33,10 +33,8 @@ def tile_attend_rel2_kb_srtq256n512t1024_kernel(tc, q_words, q_scales, k_words, 
         vs_pool = sb.tile([P, T], F32, name="vs_pool", tag="vs_then_v_g", align_bytes=64)
         qs = sb.tile([P, 2, NQ], U8, name="qs", align_bytes=64)
         ident = sb.tile([P, P], F32, name="ident", align_bytes=64)
-        ident_bf = sb.tile([P, P], BF16, name="ident_bf", align_bytes=64)
 
         make_identity(nc, ident[:])
-        nc.scalar.activation(ident_bf[:], ident[:], ACT.Copy)
         nc.vector.memset(ks_pool[:], 0)
         nc.vector.memset(kb_pool[0:ROW, :].bitcast(I32), 0)
         nc.vector.memset(vs_pool[0:ROW, :].bitcast(I32), 0)
@@ -54,14 +52,11 @@ def tile_attend_rel2_kb_srtq256n512t1024_kernel(tc, q_words, q_scales, k_words, 
             nc.sync.dma_start(qs[r:P:32].bitcast(I32), qs_rows[r].bitcast(I32))
         nc.sync.dma_start(vs_pool[ROW:P, :], vs[0:1, :])
 
-        def by_place(ap):
-            return ap.rearrange("p (t g j) -> p g t j", t=4, j=8)
-
-        def by_pair(ap):
-            return ap.rearrange("p (u g j b) -> p g u b j", u=2, j=8, b=2)
+        def by_half(ap):
+            return ap.rearrange("p (u g x) -> p g u x", u=2, x=16)
 
         kb_g = sb.tile([P, N], F32, name="kb_g", align_bytes=64)
-        nc.vector.tensor_copy(by_place(kb_g[:].bitcast(U32)), kb_pool[:].bitcast(U32).indirect(offsets[:]))
+        nc.vector.tensor_copy(by_half(kb_g[:].bitcast(U32)), kb_pool[:].bitcast(U32).indirect(offsets[:]))
         qw = sb.tile([P, 2, NQ], I32, name="qw", tag="kb_then_qw", align_bytes=64)
         nc.sync.dma_start(qw[:], q_words[0].rearrange("o g q r -> g o (q r)").bitcast(I32))
         ks_g = sb.tile([P, N], U8, name="ks_g", tag="ks_g_then_v1", align_bytes=64)
@@ -69,34 +64,35 @@ def tile_attend_rel2_kb_srtq256n512t1024_kernel(tc, q_words, q_scales, k_words, 
         kw = [sb.tile([P, 2 * N], U8, name="kw%d" % o, align_bytes=64) for o in range(2)]
         ks = [sb.tile([P, N], U8, name="ks%d" % o, align_bytes=64) for o in range(2)]
         nc.vector.tensor_copy(
-            ks[0][:].bitcast(I32).rearrange("p (t g j) -> p t g j", t=4, j=2),
-            ks_g[:].bitcast(I32).rearrange("p (g t j) -> p t g j", t=4, j=2),
+            ks[0][:].rearrange("p (u b g j) -> p u b g j", u=2, b=2, j=8),
+            ks_g[:].rearrange("p (g u j b) -> p u b g j", u=2, j=8, b=2),
         )
         for Q in range(4):
             nc.sync.dma_start(ks[1][32 * Q : 32 * Q + 4, :].bitcast(I32), ks[0][32 * Q + 4 : 32 * Q + 8, :].bitcast(I32))
         v_pool1 = sb.tile([P, T], F32, name="v_pool1", tag="ks_g_then_v1", align_bytes=64)
         nc.sync.dma_start(v_pool1[:], vT[P : 2 * P, :])
         kw_g = sb.tile([P, N], U32, name="kw_g", tag="ks_then_kw_g", align_bytes=64)
-        nc.vector.tensor_copy(by_place(kw_g[:]), kw_pool[:].bitcast(U32).indirect(offsets[:]))
-        halves = kw_g[:].bitcast(U16).rearrange("p (n o) -> p o n", o=2)
+        nc.vector.tensor_copy(by_half(kw_g[:]), kw_pool[:].bitcast(U32).indirect(offsets[:]))
+        halves = kw_g[:].bitcast(U16).rearrange("p (u m b o) -> p o u b m", u=2, b=2, o=2)
         for o in range(2):
-            nc.vector.tensor_copy(kw[o][:].bitcast(U16), halves[:, o, :])
+            nc.vector.tensor_copy(kw[o][:].bitcast(U16).rearrange("p (u b m) -> p u b m", u=2, b=2), halves[:, o])
         vs_g = sb.tile([P, N], F32, name="vs_g", tag="kw_then_vs_g", align_bytes=64)
-        nc.vector.tensor_copy(by_place(vs_g[:].bitcast(U32)), vs_pool[:].bitcast(U32).indirect(offsets[:]))
+        nc.vector.tensor_copy(by_half(vs_g[:].bitcast(U32)), vs_pool[:].bitcast(U32).indirect(offsets[:]))
         v_g = [
             sb.tile([P, N], BF16, name="v_g0", align_bytes=64),
             sb.tile([P, N], BF16, name="v_g1", tag="vs_then_v_g", align_bytes=64),
         ]
-        nc.vector.tensor_copy(by_pair(v_g[1][:]), v_pool1[:].indirect(offsets[:]))
+        nc.vector.tensor_copy(by_half(v_g[1][:]), v_pool1[:].indirect(offsets[:]))
 
         v_half = sb.tile([P, T], BF16, name="v_half", align_bytes=64)
         nc.scalar.activation(v_half[:], v_pool0[:], ACT.Copy)
-        nc.scalar.activation(by_place(v_g[0][:]), v_half[:].indirect(offsets[:]), ACT.Copy)
+        nc.scalar.activation(by_half(v_g[0][:]), v_half[:].indirect(offsets[:]), ACT.Copy)
 
         def turn(gathered, name, bank):
             turned = ps.tile([P, 4, P], F32, name=name, tag=bank)
             for t in range(4):
-                nc.tensor.transpose(turned[:, t, :], gathered[:, t * P : (t + 1) * P], ident[:])
+                u, b = divmod(t, 2)
+                nc.tensor.transpose(turned[:, t, :], gathered[:, 2 * P * u + b : 2 * P * (u + 1) : 2], ident[:])
             return turned
 
         kb_t = turn(kb_g, "kb_t", "bank7")
@@ -149,16 +145,12 @@ def tile_attend_rel2_kb_srtq256n512t1024_kernel(tc, q_words, q_scales, k_words, 
         vs_t = turn(vs_g, "vs_t", "bank1")
         v_in = sb.tile([P, 2, P * 4], BF16, name="v_in", align_bytes=64)
 
-        v0_t = ps.tile([P, 4, P], BF16, name="v0_t", tag="bank0")
-        for t in range(4):
-            nc.tensor.transpose(v0_t[:, t, :], v_g[0][:, t * P : (t + 1) * P], ident_bf[:])
-        nc.scalar.copy(v_in[:, 0, :].rearrange("p (e t) -> p e t", t=4), v0_t[:].rearrange("p t e -> p e t"))
-
-        v1_t = ps.tile([P, 2, P], F32, name="v1_t", tag="bank2")
-        v1_words = v_g[1][:].bitcast(F32)
-        for u in range(2):
-            nc.tensor.transpose(v1_t[:, u, :], v1_words[:, u * P : (u + 1) * P], ident[:])
-        nc.scalar.copy(v_in[:, 1, :].bitcast(F32).rearrange("p (e u) -> p e u", u=2), v1_t[:].rearrange("p u e -> p e u"))
+        for h in range(2):
+            v_t = ps.tile([P, 2, P], F32, name="v%d_t" % h, tag=("bank0", "bank2")[h])
+            v_words = v_g[h][:].bitcast(F32)
+            for u in range(2):
+                nc.tensor.transpose(v_t[:, u, :], v_words[:, u * P : (u + 1) * P], ident[:])
+            nc.scalar.copy(v_in[:, h, :].bitcast(F32).rearrange("p (e u) -> p e u", u=2), v_t[:].rearrange("p u e -> p e u"))
 
         w_in = sb.tile([P, 2, P, 4], BF16, name="w_in", align_bytes=64)
         wq = sb.tile([P, NQ], U32, name="wq", align_bytes=64)

@@ -27,10 +27,13 @@ def tile_attend_rel2_kb_srtq256n512t1024_kernel(tc, q_words, q_scales, k_words, 
         ps = ctx.enter_context(tc.psum_pool(name="ps", bufs=1))
 
         offsets = sb.tile([P, N // 16], U16, name="offsets")
-        ks_pool = sb.tile([P, T // 4], I32, name="ks_pool", tag="ks_then_kw_g", align_bytes=64)
-        kb_pool = sb.tile([P, T], F32, name="kb_pool", tag="kb_then_qw", align_bytes=64)
+        ks_pool = sb.tile([P, T // 4], I32, name="ks_pool", tag="ks_kw_g_v_g", align_bytes=64)
+        kb_pool = sb.tile([P, T], F32, name="kb_pool", align_bytes=64)
         kw_pool = sb.tile([P, T], I32, name="kw_pool", tag="kw_then_vs_g", align_bytes=64)
-        vs_pool = sb.tile([P, T], F32, name="vs_pool", tag="vs_then_v_g", align_bytes=64)
+        vs_pool = sb.tile([P, T], F32, name="vs_pool", align_bytes=64)
+        v_pool0 = sb.tile([P, T], F32, name="v_pool0", align_bytes=64)
+        v_pool1 = sb.tile([P, T], F32, name="v_pool1", tag="v1_then_relu", align_bytes=64)
+        qw = sb.tile([P, 2, NQ], I32, name="qw", align_bytes=64)
         qs = sb.tile([P, 2, NQ], U8, name="qs", align_bytes=64)
         ident = sb.tile([P, P], F32, name="ident", align_bytes=64)
 
@@ -44,22 +47,21 @@ def tile_attend_rel2_kb_srtq256n512t1024_kernel(tc, q_words, q_scales, k_words, 
         ks_rows = k_scales.rearrange("o (Q r) t -> Q o r t", r=4)
         for Q in range(4):
             nc.sync.dma_start(ks_pool[32 * Q : 32 * Q + 8, :], ks_rows[Q].bitcast(I32))
-        nc.sync.dma_start(kw_pool[:], k_words[0].rearrange("g t b -> g (t b)").bitcast(I32))
-        v_pool0 = sb.tile([P, T], F32, name="v_pool0", align_bytes=64)
         nc.sync.dma_start(v_pool0[:], vT[0:P, :])
+        nc.sync.dma_start(kw_pool[:], k_words[0].rearrange("g t b -> g (t b)").bitcast(I32))
         qs_rows = q_scales[0].rearrange("o (Q r) q -> r Q o q", r=4)
         for r in range(4):
             nc.sync.dma_start(qs[r:P:32].bitcast(I32), qs_rows[r].bitcast(I32))
         nc.sync.dma_start(vs_pool[ROW:P, :], vs[0:1, :])
+        nc.sync.dma_start(qw[:], q_words[0].rearrange("o g q r -> g o (q r)").bitcast(I32))
+        nc.sync.dma_start(v_pool1[:], vT[P : 2 * P, :])
 
         def by_half(ap):
             return ap.rearrange("p (u g x) -> p g u x", u=2, x=16)
 
         kb_g = sb.tile([P, N], F32, name="kb_g", align_bytes=64)
         nc.vector.tensor_copy(by_half(kb_g[:].bitcast(U32)), kb_pool[:].bitcast(U32).indirect(offsets[:]))
-        qw = sb.tile([P, 2, NQ], I32, name="qw", tag="kb_then_qw", align_bytes=64)
-        nc.sync.dma_start(qw[:], q_words[0].rearrange("o g q r -> g o (q r)").bitcast(I32))
-        ks_g = sb.tile([P, N], U8, name="ks_g", tag="ks_g_then_v1", align_bytes=64)
+        ks_g = sb.tile([P, N], U8, name="ks_g", align_bytes=64)
         nc.vector.tensor_copy(ks_g[:], ks_pool[:].bitcast(U8).indirect(offsets[:]))
         kw = [sb.tile([P, 2 * N], U8, name="kw%d" % o, align_bytes=64) for o in range(2)]
         ks = [sb.tile([P, N], U8, name="ks%d" % o, align_bytes=64) for o in range(2)]
@@ -69,9 +71,7 @@ def tile_attend_rel2_kb_srtq256n512t1024_kernel(tc, q_words, q_scales, k_words, 
         )
         for Q in range(4):
             nc.sync.dma_start(ks[1][32 * Q : 32 * Q + 4, :].bitcast(I32), ks[0][32 * Q + 4 : 32 * Q + 8, :].bitcast(I32))
-        v_pool1 = sb.tile([P, T], F32, name="v_pool1", tag="ks_g_then_v1", align_bytes=64)
-        nc.sync.dma_start(v_pool1[:], vT[P : 2 * P, :])
-        kw_g = sb.tile([P, N], U32, name="kw_g", tag="ks_then_kw_g", align_bytes=64)
+        kw_g = sb.tile([P, N], U32, name="kw_g", tag="ks_kw_g_v_g", align_bytes=64)
         nc.vector.tensor_copy(by_half(kw_g[:]), kw_pool[:].bitcast(U32).indirect(offsets[:]))
         halves = kw_g[:].bitcast(U16).rearrange("p (u m b o) -> p o u b m", u=2, b=2, o=2)
         for o in range(2):
@@ -80,7 +80,7 @@ def tile_attend_rel2_kb_srtq256n512t1024_kernel(tc, q_words, q_scales, k_words, 
         nc.vector.tensor_copy(by_half(vs_g[:].bitcast(U32)), vs_pool[:].bitcast(U32).indirect(offsets[:]))
         v_g = [
             sb.tile([P, N], BF16, name="v_g0", align_bytes=64),
-            sb.tile([P, N], BF16, name="v_g1", tag="vs_then_v_g", align_bytes=64),
+            sb.tile([P, N], BF16, name="v_g1", tag="ks_kw_g_v_g", align_bytes=64),
         ]
         nc.vector.tensor_copy(by_half(v_g[1][:]), v_pool1[:].indirect(offsets[:]))
 
@@ -95,12 +95,23 @@ def tile_attend_rel2_kb_srtq256n512t1024_kernel(tc, q_words, q_scales, k_words, 
                 nc.tensor.transpose(turned[:, t, :], gathered[:, 2 * P * u + b : 2 * P * (u + 1) : 2], ident[:])
             return turned
 
+        v_in = sb.tile([P, 2, P * 4], BF16, name="v_in", align_bytes=64)
+
+        def turn_values(h, bank):
+            v_t = ps.tile([P, 2, P], F32, name="v%d_t" % h, tag=bank)
+            v_words = v_g[h][:].bitcast(F32)
+            for u in range(2):
+                nc.tensor.transpose(v_t[:, u, :], v_words[:, u * P : (u + 1) * P], ident[:])
+            nc.scalar.copy(v_in[:, h, :].bitcast(F32).rearrange("p (e u) -> p e u", u=2), v_t[:].rearrange("p u e -> p e u"))
+
         kb_t = turn(kb_g, "kb_t", "bank7")
         kb_col = sb.tile([P, 4], F32, name="kb_col")
         nc.scalar.copy(kb_col[:], kb_t[:, :, ROW])
+        turn_values(0, "bank7")
 
-        relu = sb.tile([P, 6, P], F32, name="relu", align_bytes=64)
-        relu_last = sb.tile([P, 2, P], F32, name="relu_last", tag="ks_g_then_v1", align_bytes=64)
+        relu_s = sb.tile([P, 8, P], F32, name="relu_s", align_bytes=64)
+        relu_v = sb.tile([P, 8, P], F32, name="relu_v", tag="v1_then_relu", align_bytes=64)
+        on_vector = (6,7,)
         p = sb.tile([P, 2, 4, P], F32, name="p", align_bytes=64)
         score_bank = [0, 1, 2, 3, 4, 5, 6, 7]
         scores = {}
@@ -122,60 +133,58 @@ def tile_attend_rel2_kb_srtq256n512t1024_kernel(tc, q_words, q_scales, k_words, 
             scores[i] = ps.tile([P, P], F32, name="score%d" % i, tag="bank%d" % score_bank[i])
             score_pass(i, 0)
 
-        for i in range(7):
+        for i in range(8):
             open_score(i)
 
         for qb in range(2):
             for t in range(4):
                 i = 4 * qb + t
-                if i == 7:
+                if i >= 8:
                     open_score(i)
                 score_pass(i, 1)
-                if i < 6:
-                    nc.scalar.activation(relu[:, i, :], scores[i][:], ACT.Relu, bias=kb_col[:, t : t + 1])
+                if i in on_vector:
+                    nc.vector.tensor_scalar(relu_v[:, i, :], scores[i][:], kb_col[:, t : t + 1], 0.0, ALU.add, ALU.max)
                 else:
-                    nc.vector.tensor_scalar(relu_last[:, i - 6, :], scores[i][:], kb_col[:, t : t + 1], 0.0, ALU.add, ALU.max)
+                    nc.scalar.activation(relu_s[:, i, :], scores[i][:], ACT.Relu, bias=kb_col[:, t : t + 1])
                 if i == 3:
-                    nc.scalar.activation(p[:, 0], relu[:, 0:4], ACT.Square)
-                if i == 5:
-                    nc.scalar.activation(p[:, 1, 0:2], relu[:, 4:6], ACT.Square)
-                if i == 7:
-                    nc.scalar.activation(p[:, 1, 2:4], relu_last[:], ACT.Square)
+                    nc.scalar.activation(p[:, 0], relu_s[:, 0:4], ACT.Square)
+                if i in (5, 7):
+                    relu = relu_v if i in on_vector else relu_s
+                    nc.scalar.activation(p[:, 1, t - 1 : t + 1], relu[:, i - 1 : i + 1], ACT.Square)
 
-        vs_t = turn(vs_g, "vs_t", "bank1")
-        v_in = sb.tile([P, 2, P * 4], BF16, name="v_in", align_bytes=64)
-
-        for h in range(2):
-            v_t = ps.tile([P, 2, P], F32, name="v%d_t" % h, tag=("bank0", "bank2")[h])
-            v_words = v_g[h][:].bitcast(F32)
-            for u in range(2):
-                nc.tensor.transpose(v_t[:, u, :], v_words[:, u * P : (u + 1) * P], ident[:])
-            nc.scalar.copy(v_in[:, h, :].bitcast(F32).rearrange("p (e u) -> p e u", u=2), v_t[:].rearrange("p u e -> p e u"))
+        vs_t = turn(vs_g, "vs_t", "bank0")
+        turn_values(1, "bank1")
 
         w_in = sb.tile([P, 2, P, 4], BF16, name="w_in", align_bytes=64)
         wq = sb.tile([P, NQ], U32, name="wq", align_bytes=64)
         wq_s = sb.tile([P, NQ], U8, name="wq_s", align_bytes=64)
         vq = sb.tile([P, DV], U32, name="vq", align_bytes=64)
         vq_s = sb.tile([P, DV], U8, name="vq_s", align_bytes=64)
-        for qb in range(2):
+        def weigh(qb):
             nc.vector.tensor_tensor(
                 w_in[:, qb],
                 p[:, qb].rearrange("p t q -> p q t"),
                 vs_t[:, :, ROW:P].to_broadcast([P, 4, P]).rearrange("p t q -> p q t"),
                 ALU.mult,
             )
-        nc.vector.quantize_mx(out=vq[:].bitcast(FP8X4), scales=vq_s[:], in_=v_in[:].rearrange("p h x -> p (h x)"))
-        for qb in range(2):
+
+        def quantise_weights(qb):
             cols = slice(qb * P, (qb + 1) * P)
             nc.vector.quantize_mx(
                 out=wq[:, cols].bitcast(FP8X4), scales=wq_s[:, cols], in_=w_in[:, qb].rearrange("p q t -> p (q t)")
             )
 
+        weigh(0)
+        weigh(1)
+        quantise_weights(0)
+        nc.vector.quantize_mx(out=vq[:].bitcast(FP8X4), scales=vq_s[:], in_=v_in[:].rearrange("p h x -> p (h x)"))
+        quantise_weights(1)
+
         total = [sb.tile([P, 1], F32, name="total%d" % qb) for qb in range(2)]
         inv = [sb.tile([P, 1], F32, name="inv%d" % qb) for qb in range(2)]
         spent = sb.tile([P, 2, P], F32, name="spent")
         for qb in range(2):
-            p_t = ps.tile([P, P], F32, name="p_t%d" % qb, tag="bank%d" % (3 + qb))
+            p_t = ps.tile([P, P], F32, name="p_t%d" % qb, tag="bank%d" % (2 + qb))
             for t in range(4):
                 nc.tensor.matmul(p_t[:], p[:, qb, t, :], ident[:], start=(t == 0), stop=(t == 3), is_transpose=True)
             nc.scalar.activation(spent[:, qb, :], p_t[:], ACT.Copy, bias=1.0 / P, accum_out=total[qb][:])
@@ -194,8 +203,8 @@ def tile_attend_rel2_kb_srtq256n512t1024_kernel(tc, q_words, q_scales, k_words, 
             rows = slice(qb * P, (qb + 1) * P)
             left, right = slice(0, P), slice(P, DV)
             res = sb.tile([P, DV], F32, name="res%d" % qb, align_bytes=64)
-            y_left = product(qb, left, "y%d_left" % qb, ("bank5", "bank7")[qb])
-            y_right = product(qb, right, "y%d_right" % qb, ("bank0", "bank6")[qb])
+            y_left = product(qb, left, "y%d_left" % qb, ("bank4", "bank6")[qb])
+            y_right = product(qb, right, "y%d_right" % qb, ("bank5", "bank7")[qb])
             nc.vector.tensor_scalar(res[:, left], y_left[:], inv[qb][:], None, ALU.mult)
             nc.scalar.activation(res[:, right], y_right[:], ACT.Copy, scale=inv[qb][:])
             nc.sync.dma_start(out[0, rows, left], res[:, left])

@@ -30,9 +30,8 @@ def tile_attend_rel2_kb_srtq256n512t1024_kernel(tc, q_words, q_scales, k_words, 
         ks_pool = sb.tile([P, T // 4], I32, name="ks_pool", tag="ks_kw_g_v_g", align_bytes=64)
         kb_pool = sb.tile([P, T], F32, name="kb_pool", align_bytes=64)
         kw_pool = sb.tile([P, T], I32, name="kw_pool", tag="kw_then_vs_g", align_bytes=64)
-        vs_pool = sb.tile([P, T], F32, name="vs_pool", align_bytes=64)
+        vs_pool = sb.tile([P, T], F32, name="vs_pool", tag="vs_then_v_g", align_bytes=64)
         v_pool0 = sb.tile([P, T], F32, name="v_pool0", align_bytes=64)
-        v_pool1 = sb.tile([P, T], F32, name="v_pool1", tag="v1_then_relu", align_bytes=64)
         qw = sb.tile([P, 2, NQ], I32, name="qw", align_bytes=64)
         qs = sb.tile([P, 2, NQ], U8, name="qs", align_bytes=64)
         ident = sb.tile([P, P], F32, name="ident", align_bytes=64)
@@ -47,21 +46,20 @@ def tile_attend_rel2_kb_srtq256n512t1024_kernel(tc, q_words, q_scales, k_words, 
         ks_rows = k_scales.rearrange("o (Q r) t -> Q o r t", r=4)
         for Q in range(4):
             nc.sync.dma_start(ks_pool[32 * Q : 32 * Q + 8, :], ks_rows[Q].bitcast(I32))
-        nc.sync.dma_start(v_pool0[:], vT[0:P, :])
         nc.sync.dma_start(kw_pool[:], k_words[0].rearrange("g t b -> g (t b)").bitcast(I32))
+        nc.sync.dma_start(vs_pool[ROW:P, :], vs[0:1, :])
         qs_rows = q_scales[0].rearrange("o (Q r) q -> r Q o q", r=4)
         for r in range(4):
             nc.sync.dma_start(qs[r:P:32].bitcast(I32), qs_rows[r].bitcast(I32))
-        nc.sync.dma_start(vs_pool[ROW:P, :], vs[0:1, :])
         nc.sync.dma_start(qw[:], q_words[0].rearrange("o g q r -> g o (q r)").bitcast(I32))
-        nc.sync.dma_start(v_pool1[:], vT[P : 2 * P, :])
+        nc.sync.dma_start(v_pool0[:], vT[0:P, :])
 
         def by_half(ap):
             return ap.rearrange("p (u g x) -> p g u x", u=2, x=16)
 
         kb_g = sb.tile([P, N], F32, name="kb_g", align_bytes=64)
         nc.vector.tensor_copy(by_half(kb_g[:].bitcast(U32)), kb_pool[:].bitcast(U32).indirect(offsets[:]))
-        ks_g = sb.tile([P, N], U8, name="ks_g", align_bytes=64)
+        ks_g = sb.tile([P, N], U8, name="ks_g", tag="v1_then_relu", align_bytes=64)
         nc.vector.tensor_copy(ks_g[:], ks_pool[:].bitcast(U8).indirect(offsets[:]))
         kw = [sb.tile([P, 2 * N], U8, name="kw%d" % o, align_bytes=64) for o in range(2)]
         ks = [sb.tile([P, N], U8, name="ks%d" % o, align_bytes=64) for o in range(2)]
@@ -71,6 +69,8 @@ def tile_attend_rel2_kb_srtq256n512t1024_kernel(tc, q_words, q_scales, k_words, 
         )
         for Q in range(4):
             nc.sync.dma_start(ks[1][32 * Q : 32 * Q + 4, :].bitcast(I32), ks[0][32 * Q + 4 : 32 * Q + 8, :].bitcast(I32))
+        v_pool1 = sb.tile([P, T], F32, name="v_pool1", tag="v1_then_relu", align_bytes=64)
+        nc.sync.dma_start(v_pool1[:], vT[P : 2 * P, :])
         kw_g = sb.tile([P, N], U32, name="kw_g", tag="ks_kw_g_v_g", align_bytes=64)
         nc.vector.tensor_copy(by_half(kw_g[:]), kw_pool[:].bitcast(U32).indirect(offsets[:]))
         halves = kw_g[:].bitcast(U16).rearrange("p (u m b o) -> p o u b m", u=2, b=2, o=2)
@@ -79,14 +79,12 @@ def tile_attend_rel2_kb_srtq256n512t1024_kernel(tc, q_words, q_scales, k_words, 
         vs_g = sb.tile([P, N], F32, name="vs_g", tag="kw_then_vs_g", align_bytes=64)
         nc.vector.tensor_copy(by_half(vs_g[:].bitcast(U32)), vs_pool[:].bitcast(U32).indirect(offsets[:]))
         v_g = [
-            sb.tile([P, N], BF16, name="v_g0", align_bytes=64),
-            sb.tile([P, N], BF16, name="v_g1", tag="ks_kw_g_v_g", align_bytes=64),
+            sb.tile([P, N], BF16, name="v_g0", tag="ks_kw_g_v_g", align_bytes=64),
+            sb.tile([P, N], BF16, name="v_g1", tag="vs_then_v_g", align_bytes=64),
         ]
+        nc.vector.tensor_copy(by_half(v_g[0][:]), v_pool0[:].indirect(offsets[:]))
         nc.vector.tensor_copy(by_half(v_g[1][:]), v_pool1[:].indirect(offsets[:]))
 
-        v_half = sb.tile([P, T], BF16, name="v_half", align_bytes=64)
-        nc.scalar.activation(v_half[:], v_pool0[:], ACT.Copy)
-        nc.scalar.activation(by_half(v_g[0][:]), v_half[:].indirect(offsets[:]), ACT.Copy)
 
         def turn(gathered, name, bank):
             turned = ps.tile([P, 4, P], F32, name=name, tag=bank)
@@ -107,11 +105,10 @@ def tile_attend_rel2_kb_srtq256n512t1024_kernel(tc, q_words, q_scales, k_words, 
         kb_t = turn(kb_g, "kb_t", "bank7")
         kb_col = sb.tile([P, 4], F32, name="kb_col")
         nc.scalar.copy(kb_col[:], kb_t[:, :, ROW])
-        turn_values(0, "bank7")
 
         relu_s = sb.tile([P, 8, P], F32, name="relu_s", align_bytes=64)
-        relu_v = sb.tile([P, 8, P], F32, name="relu_v", tag="v1_then_relu", align_bytes=64)
-        on_vector = (6,7,)
+        relu_v = relu_s
+        on_vector = ()
         p = sb.tile([P, 2, 4, P], F32, name="p", align_bytes=64)
         score_bank = [0, 1, 2, 3, 4, 5, 6, 7]
         scores = {}
@@ -153,7 +150,8 @@ def tile_attend_rel2_kb_srtq256n512t1024_kernel(tc, q_words, q_scales, k_words, 
                     nc.scalar.activation(p[:, 1, t - 1 : t + 1], relu[:, i - 1 : i + 1], ACT.Square)
 
         vs_t = turn(vs_g, "vs_t", "bank0")
-        turn_values(1, "bank1")
+        turn_values(0, "bank1")
+        turn_values(1, "bank4")
 
         w_in = sb.tile([P, 2, P, 4], BF16, name="w_in", align_bytes=64)
         wq = sb.tile([P, NQ], U32, name="wq", align_bytes=64)
@@ -203,7 +201,7 @@ def tile_attend_rel2_kb_srtq256n512t1024_kernel(tc, q_words, q_scales, k_words, 
             rows = slice(qb * P, (qb + 1) * P)
             left, right = slice(0, P), slice(P, DV)
             res = sb.tile([P, DV], F32, name="res%d" % qb, align_bytes=64)
-            y_left = product(qb, left, "y%d_left" % qb, ("bank4", "bank6")[qb])
+            y_left = product(qb, left, "y%d_left" % qb, ("bank1", "bank6")[qb])
             y_right = product(qb, right, "y%d_right" % qb, ("bank5", "bank7")[qb])
             nc.vector.tensor_scalar(res[:, left], y_left[:], inv[qb][:], None, ALU.mult)
             nc.scalar.activation(res[:, right], y_right[:], ACT.Copy, scale=inv[qb][:])

@@ -60,22 +60,32 @@ def tile_attend_rel2_kb_srtq256n512t1024_kernel(tc, q_words, q_scales, k_words, 
         kb_g = sb.tile([P, N], F32, name="kb_g", align_bytes=64)
         nc.vector.tensor_copy(by_half(kb_g[:].bitcast(U32)), kb_pool[:].bitcast(U32).indirect(offsets[:]))
         ks_g = sb.tile([P, N], U8, name="ks_g", tag="v1_then_relu", align_bytes=64)
-        nc.vector.tensor_copy(ks_g[:], ks_pool[:].bitcast(U8).indirect(offsets[:]))
+        half_list = [offsets[:, 0 : N // 32], offsets[:, N // 32 : N // 16]]
+        for c in range(2):
+            nc.vector.tensor_copy(ks_g[:, c * N // 2 : (c + 1) * N // 2], ks_pool[:].bitcast(U8).indirect(half_list[c]))
         kw = [sb.tile([P, 2 * N], U8, name="kw%d" % o, align_bytes=64) for o in range(2)]
         ks = [sb.tile([P, N], U8, name="ks%d" % o, align_bytes=64) for o in range(2)]
-        nc.vector.tensor_copy(
-            ks[0][:].rearrange("p (u b g j) -> p u b g j", u=2, b=2, j=8),
-            ks_g[:].rearrange("p (g u j b) -> p u b g j", u=2, j=8, b=2),
-        )
+        for c in range(2):
+            nc.vector.tensor_copy(
+                ks[0][:].rearrange("p (u b c g j) -> p c u b g j", u=2, b=2, c=2, j=8)[:, c],
+                ks_g[:, c * N // 2 : (c + 1) * N // 2].rearrange("p (g u j b) -> p u b g j", u=2, j=8, b=2),
+            )
         for Q in range(4):
             nc.sync.dma_start(ks[1][32 * Q : 32 * Q + 4, :].bitcast(I32), ks[0][32 * Q + 4 : 32 * Q + 8, :].bitcast(I32))
         v_pool1 = sb.tile([P, T], F32, name="v_pool1", tag="v1_then_relu", align_bytes=64)
         nc.sync.dma_start(v_pool1[:], vT[P : 2 * P, :])
-        kw_g = sb.tile([P, N], U32, name="kw_g", tag="ks_kw_g_v_g", align_bytes=64)
-        nc.vector.tensor_copy(by_half(kw_g[:]), kw_pool[:].bitcast(U32).indirect(offsets[:]))
-        halves = kw_g[:].bitcast(U16).rearrange("p (u m b o) -> p o u b m", u=2, b=2, o=2)
+        kw_g = [
+            sb.tile([P, N // 2], U32, name="kw_g0", align_bytes=64),
+            sb.tile([P, N // 2], U32, name="kw_g1", tag="ks_kw_g_v_g", align_bytes=64),
+        ]
+        for c in range(2):
+            nc.vector.tensor_copy(by_half(kw_g[c][:]), kw_pool[:].bitcast(U32).indirect(half_list[c]))
         for o in range(2):
-            nc.vector.tensor_copy(kw[o][:].bitcast(U16).rearrange("p (u b m) -> p u b m", u=2, b=2), halves[:, o])
+            for c in range(2):
+                nc.vector.tensor_copy(
+                    kw[o][:].bitcast(U16).rearrange("p (u b c m) -> p c u b m", u=2, b=2, c=2)[:, c],
+                    kw_g[c][:].bitcast(U16).rearrange("p (u m b o) -> p o u b m", u=2, b=2, o=2)[:, o],
+                )
         vs_g = sb.tile([P, N], F32, name="vs_g", tag="kw_then_vs_g", align_bytes=64)
         nc.vector.tensor_copy(by_half(vs_g[:].bitcast(U32)), vs_pool[:].bitcast(U32).indirect(offsets[:]))
         v_g = [
@@ -107,8 +117,8 @@ def tile_attend_rel2_kb_srtq256n512t1024_kernel(tc, q_words, q_scales, k_words, 
         nc.scalar.copy(kb_col[:], kb_t[:, :, ROW])
 
         relu_s = sb.tile([P, 8, P], F32, name="relu_s", align_bytes=64)
-        relu_v = relu_s
-        on_vector = ()
+        relu_v = sb.tile([P, 8, P], F32, name="relu_v", tag="v1_then_relu", align_bytes=64)
+        on_vector = (6,7,)
         p = sb.tile([P, 2, 4, P], F32, name="p", align_bytes=64)
         score_bank = [0, 1, 2, 3, 4, 5, 6, 7]
         scores = {}

@@ -93,7 +93,6 @@ def tile_attend_rel2_kb_srtq256n512t1024_kernel(tc, q_words, q_scales, k_words, 
             sb.tile([P, N], BF16, name="v_g1", tag="vs_then_v_g", align_bytes=64),
         ]
         nc.vector.tensor_copy(by_half(v_g[0][:]), v_pool0[:].indirect(offsets[:]))
-        nc.vector.tensor_copy(by_half(v_g[1][:]), v_pool1[:].indirect(offsets[:]))
 
 
         def turn(gathered, name, bank):
@@ -117,9 +116,9 @@ def tile_attend_rel2_kb_srtq256n512t1024_kernel(tc, q_words, q_scales, k_words, 
         nc.scalar.copy(kb_col[:], kb_t[:, :, ROW])
 
         relu_s = sb.tile([P, 8, P], F32, name="relu_s", align_bytes=64)
-        relu_v = sb.tile([P, 8, P], F32, name="relu_v", tag="v1_then_relu", align_bytes=64)
-        on_vector = (6,7,)
-        p = sb.tile([P, 2, 4, P], F32, name="p", align_bytes=64)
+        relu_v = sb.tile([P, 8, P], F32, name="relu_v", align_bytes=64)
+        on_vector = (4,5,)
+        p = sb.tile([P, 2, 2, P, 2], F32, name="p", align_bytes=64)
         score_bank = [0, 1, 2, 3, 4, 5, 6, 7]
         scores = {}
 
@@ -154,11 +153,12 @@ def tile_attend_rel2_kb_srtq256n512t1024_kernel(tc, q_words, q_scales, k_words, 
                 else:
                     nc.scalar.activation(relu_s[:, i, :], scores[i][:], ACT.Relu, bias=kb_col[:, t : t + 1])
                 if i == 3:
-                    nc.scalar.activation(p[:, 0], relu_s[:, 0:4], ACT.Square)
+                    nc.scalar.activation(p[:, 0], relu_s[:, 0:4].rearrange("p (u b) q -> p u q b", b=2), ACT.Square)
                 if i in (5, 7):
                     relu = relu_v if i in on_vector else relu_s
-                    nc.scalar.activation(p[:, 1, t - 1 : t + 1], relu[:, i - 1 : i + 1], ACT.Square)
+                    nc.scalar.activation(p[:, 1, t // 2], relu[:, i - 1 : i + 1].rearrange("p b q -> p q b"), ACT.Square)
 
+        nc.vector.tensor_copy(by_half(v_g[1][:]), v_pool1[:].indirect(offsets[:]))
         vs_t = turn(vs_g, "vs_t", "bank0")
         turn_values(0, "bank1")
         turn_values(1, "bank4")
@@ -170,9 +170,9 @@ def tile_attend_rel2_kb_srtq256n512t1024_kernel(tc, q_words, q_scales, k_words, 
         vq_s = sb.tile([P, DV], U8, name="vq_s", align_bytes=64)
         def weigh(qb):
             nc.vector.tensor_tensor(
-                w_in[:, qb],
-                p[:, qb].rearrange("p t q -> p q t"),
-                vs_t[:, :, ROW:P].to_broadcast([P, 4, P]).rearrange("p t q -> p q t"),
+                w_in[:, qb].rearrange("p q (u b) -> p q u b", b=2),
+                p[:, qb].rearrange("p u q b -> p q u b"),
+                vs_t[:, :, ROW:P].to_broadcast([P, 4, P]).rearrange("p (u b) q -> p q u b", b=2),
                 ALU.mult,
             )
 
@@ -194,7 +194,7 @@ def tile_attend_rel2_kb_srtq256n512t1024_kernel(tc, q_words, q_scales, k_words, 
         for qb in range(2):
             p_t = ps.tile([P, P], F32, name="p_t%d" % qb, tag="bank%d" % (2 + qb))
             for t in range(4):
-                nc.tensor.matmul(p_t[:], p[:, qb, t, :], ident[:], start=(t == 0), stop=(t == 3), is_transpose=True)
+                nc.tensor.matmul(p_t[:], p[:, qb, t // 2, :, t % 2], ident[:], start=(t == 0), stop=(t == 3), is_transpose=True)
             nc.scalar.activation(spent[:, qb, :], p_t[:], ACT.Copy, bias=1.0 / P, accum_out=total[qb][:])
             nc.vector.reciprocal(inv[qb][:], total[qb][:])
 

@@ -16,6 +16,7 @@ ALU = mybir.AluOpType
 
 P = 128
 ROW = P - 1
+TOP = P - 32
 N, T, D, DV, NQ = 512, 1024, 1024, 256, 256
 FLOPS = 2 * NQ * N * D + 2 * NQ * N * DV
 
@@ -33,58 +34,57 @@ def tile_attend_rel2_kb_srtq256n512t1024_kernel(tc, q_words, q_scales, k_words, 
         vs_pool = sb.tile([P, T], F32, name="vs_pool", tag="vs_then_v_g", align_bytes=64)
         v_pool0 = sb.tile([P, T], F32, name="v_pool0", align_bytes=64)
         qw = sb.tile([P, 2, NQ], I32, name="qw", align_bytes=64)
-        qs = sb.tile([P, 2, NQ], U8, name="qs", align_bytes=64)
+        staged = sb.tile([P, N + NQ], U8, name="staged", align_bytes=64)
+        planes = sb.tile([P, 2, N + NQ], U8, name="planes", align_bytes=64)
         ident = sb.tile([P, P], F32, name="ident", align_bytes=64)
 
         make_identity(nc, ident[:])
-        nc.vector.memset(ks_pool[:], 0)
+        nc.vector.memset(ks_pool[0:TOP, :], 0)
         nc.vector.memset(kb_pool[0:ROW, :].bitcast(I32), 0)
         nc.vector.memset(vs_pool[0:ROW, :].bitcast(I32), 0)
 
         nc.sync.dma_start(offsets[:], offs)
+        nc.sync.dma_start(ks_pool[TOP:P, :], k_scales.rearrange("o f t -> f o t").bitcast(I32))
         nc.sync.dma_start(kb_pool[ROW:P, :], kb[0:1, :])
-        ks_rows = k_scales.rearrange("o (Q r) t -> Q o r t", r=4)
-        for Q in range(4):
-            nc.sync.dma_start(ks_pool[32 * Q : 32 * Q + 8, :], ks_rows[Q].bitcast(I32))
         nc.sync.dma_start(kw_pool[:], k_words[0].rearrange("g t b -> g (t b)").bitcast(I32))
+        nc.sync.dma_start(staged[TOP:P, N : N + NQ].bitcast(I32), q_scales[0].rearrange("o f q -> f o q").bitcast(I32))
         nc.sync.dma_start(vs_pool[ROW:P, :], vs[0:1, :])
-        qs_rows = q_scales[0].rearrange("o (Q r) q -> r Q o q", r=4)
-        for r in range(4):
-            nc.sync.dma_start(qs[r:P:32].bitcast(I32), qs_rows[r].bitcast(I32))
         nc.sync.dma_start(qw[:], q_words[0].rearrange("o g q r -> g o (q r)").bitcast(I32))
         nc.sync.dma_start(v_pool0[:], vT[0:P, :])
 
         def by_half(ap):
             return ap.rearrange("p (u g x) -> p g u x", u=2, x=16)
 
-        kb_g = sb.tile([P, N], F32, name="kb_g", align_bytes=64)
-        nc.vector.tensor_copy(by_half(kb_g[:].bitcast(U32)), kb_pool[:].bitcast(U32).indirect(offsets[:]))
         ks_g = sb.tile([P, N], U8, name="ks_g", tag="v1_then_relu", align_bytes=64)
         half_list = [offsets[:, 0 : N // 32], offsets[:, N // 32 : N // 16]]
         for c in range(2):
             nc.vector.tensor_copy(ks_g[:, c * N // 2 : (c + 1) * N // 2], ks_pool[:].bitcast(U8).indirect(half_list[c]))
-        kw = [sb.tile([P, 2 * N], U8, name="kw%d" % o, align_bytes=64) for o in range(2)]
-        ks = [sb.tile([P, N], U8, name="ks%d" % o, align_bytes=64) for o in range(2)]
         for c in range(2):
             nc.vector.tensor_copy(
-                ks[0][:].rearrange("p (u b c g j) -> p c u b g j", u=2, b=2, c=2, j=8)[:, c],
+                staged[:, 0:N].rearrange("p (u b c g j) -> p c u b g j", u=2, b=2, c=2, j=8)[:, c],
                 ks_g[:, c * N // 2 : (c + 1) * N // 2].rearrange("p (g u j b) -> p u b g j", u=2, j=8, b=2),
             )
         for Q in range(4):
-            nc.sync.dma_start(ks[1][32 * Q : 32 * Q + 4, :].bitcast(I32), ks[0][32 * Q + 4 : 32 * Q + 8, :].bitcast(I32))
+            nc.sync.dma_start(
+                planes[32 * Q : 32 * Q + 4].rearrange("p o x -> p (o x)").bitcast(I32),
+                staged[TOP + 8 * Q : TOP + 8 * Q + 8, :].bitcast(I32),
+            )
         v_pool1 = sb.tile([P, T], F32, name="v_pool1", tag="v1_then_relu", align_bytes=64)
         nc.sync.dma_start(v_pool1[:], vT[P : 2 * P, :])
+        kb_g = sb.tile([P, N], F32, name="kb_g", align_bytes=64)
+        nc.vector.tensor_copy(by_half(kb_g[:].bitcast(U32)), kb_pool[:].bitcast(U32).indirect(offsets[:]))
         kw_g = [
             sb.tile([P, N // 2], U32, name="kw_g0", align_bytes=64),
             sb.tile([P, N // 2], U32, name="kw_g1", tag="ks_kw_g_v_g", align_bytes=64),
         ]
         for c in range(2):
             nc.vector.tensor_copy(by_half(kw_g[c][:]), kw_pool[:].bitcast(U32).indirect(half_list[c]))
-        for o in range(2):
+        kw = [sb.tile([P, 2, 2, 2 * P], U8, name="kw%d" % u, align_bytes=64) for u in range(2)]
+        for u in range(2):
             for c in range(2):
                 nc.vector.tensor_copy(
-                    kw[o][:].bitcast(U16).rearrange("p (u b c m) -> p c u b m", u=2, b=2, c=2)[:, c],
-                    kw_g[c][:].bitcast(U16).rearrange("p (u m b o) -> p o u b m", u=2, b=2, o=2)[:, o],
+                    kw[u][:].bitcast(U16).rearrange("p o b (c m) -> p c o b m", c=2)[:, c],
+                    kw_g[c][:].bitcast(U16).rearrange("p (u m b o) -> p u o b m", u=2, b=2, o=2)[:, u],
                 )
         vs_g = sb.tile([P, N], F32, name="vs_g", tag="kw_then_vs_g", align_bytes=64)
         nc.vector.tensor_copy(by_half(vs_g[:].bitcast(U32)), vs_pool[:].bitcast(U32).indirect(offsets[:]))
@@ -115,11 +115,8 @@ def tile_attend_rel2_kb_srtq256n512t1024_kernel(tc, q_words, q_scales, k_words, 
         kb_col = sb.tile([P, 4], F32, name="kb_col")
         nc.scalar.copy(kb_col[:], kb_t[:, :, ROW])
 
-        relu_s = sb.tile([P, 8, P], F32, name="relu_s", align_bytes=64)
-        relu_v = sb.tile([P, 8, P], F32, name="relu_v", align_bytes=64)
-        on_vector = (4,5,)
+        relu = sb.tile([P, 8, P], F32, name="relu", align_bytes=64)
         p = sb.tile([P, 2, 2, P, 2], F32, name="p", align_bytes=64)
-        score_bank = [0, 1, 2, 3, 4, 5, 6, 7]
         scores = {}
 
         def score_pass(i, o):
@@ -127,36 +124,23 @@ def tile_attend_rel2_kb_srtq256n512t1024_kernel(tc, q_words, q_scales, k_words, 
             cols = slice(qb * P, (qb + 1) * P)
             nc.tensor.matmul_mx(
                 out=scores[i][:],
-                lhsT=kw[o][:, 2 * P * t : 2 * P * (t + 1)].bitcast(FP4X4),
-                lhsT_scale=ks[o][:, P * t : P * (t + 1)],
+                lhsT=kw[t // 2][:, o, t % 2, :].bitcast(FP4X4),
+                lhsT_scale=planes[:, o, P * t : P * (t + 1)],
                 rhs=qw[:, o, cols].bitcast(FP8X4),
-                rhs_scale=qs[:, o, cols],
+                rhs_scale=planes[:, o, N + qb * P : N + (qb + 1) * P],
                 start=(o == 0),
                 stop=(o == 1),
             )
 
-        def open_score(i):
-            scores[i] = ps.tile([P, P], F32, name="score%d" % i, tag="bank%d" % score_bank[i])
-            score_pass(i, 0)
-
-        for i in range(8):
-            open_score(i)
-
         for qb in range(2):
             for t in range(4):
                 i = 4 * qb + t
-                if i >= 8:
-                    open_score(i)
+                scores[i] = ps.tile([P, P], F32, name="score%d" % i, tag="bank%d" % i)
+                score_pass(i, 0)
                 score_pass(i, 1)
-                if i in on_vector:
-                    nc.vector.tensor_scalar(relu_v[:, i, :], scores[i][:], kb_col[:, t : t + 1], 0.0, ALU.add, ALU.max)
-                else:
-                    nc.scalar.activation(relu_s[:, i, :], scores[i][:], ACT.Relu, bias=kb_col[:, t : t + 1])
-                if i == 3:
-                    nc.scalar.activation(p[:, 0], relu_s[:, 0:4].rearrange("p (u b) q -> p u q b", b=2), ACT.Square)
-                if i in (5, 7):
-                    relu = relu_v if i in on_vector else relu_s
-                    nc.scalar.activation(p[:, 1, t // 2], relu[:, i - 1 : i + 1].rearrange("p b q -> p q b"), ACT.Square)
+                nc.scalar.activation(relu[:, i, :], scores[i][:], ACT.Relu, bias=kb_col[:, t : t + 1])
+                if t % 2 == 1:
+                    nc.scalar.activation(p[:, qb, t // 2], relu[:, i - 1 : i + 1].rearrange("p b q -> p q b"), ACT.Square)
 
         nc.vector.tensor_copy(by_half(v_g[1][:]), v_pool1[:].indirect(offsets[:]))
         vs_t = turn(vs_g, "vs_t", "bank0")

@@ -29,10 +29,9 @@ def tile_attend_rel2_kb_srtq256n512t1024_kernel(tc, q_words, q_scales, k_words, 
 
         offsets = sb.tile([P, N // 16], U16, name="offsets")
         ks_pool = sb.tile([P, T // 4], I32, name="ks_pool", tag="ks_kw_g_v_g", align_bytes=64)
-        kb_pool = sb.tile([P, T], F32, name="kb_pool", align_bytes=64)
+        kb_pool = sb.tile([P, T], F32, name="kb_pool", tag="kb_then_v1", align_bytes=64)
         kw_pool = sb.tile([P, T], I32, name="kw_pool", tag="kw_then_vs_g", align_bytes=64)
         vs_pool = sb.tile([P, T], F32, name="vs_pool", tag="vs_then_v_g", align_bytes=64)
-        v_pool0 = sb.tile([P, T], F32, name="v_pool0", align_bytes=64)
         qw = sb.tile([P, 2, NQ], I32, name="qw", align_bytes=64)
         staged = sb.tile([P, N + NQ], U8, name="staged", align_bytes=64)
         planes = sb.tile([P, 2, N + NQ], U8, name="planes", align_bytes=64)
@@ -45,12 +44,11 @@ def tile_attend_rel2_kb_srtq256n512t1024_kernel(tc, q_words, q_scales, k_words, 
 
         nc.sync.dma_start(offsets[:], offs)
         nc.sync.dma_start(ks_pool[TOP:P, :], k_scales.rearrange("o f t -> f o t").bitcast(I32))
+        nc.sync.dma_start(staged[TOP:P, N : N + NQ].bitcast(I32), q_scales[0].rearrange("o f q -> f o q").bitcast(I32))
         nc.sync.dma_start(kb_pool[ROW:P, :], kb[0:1, :])
         nc.sync.dma_start(kw_pool[:], k_words[0].rearrange("g t b -> g (t b)").bitcast(I32))
-        nc.sync.dma_start(staged[TOP:P, N : N + NQ].bitcast(I32), q_scales[0].rearrange("o f q -> f o q").bitcast(I32))
         nc.sync.dma_start(vs_pool[ROW:P, :], vs[0:1, :])
         nc.sync.dma_start(qw[:], q_words[0].rearrange("o g q r -> g o (q r)").bitcast(I32))
-        nc.sync.dma_start(v_pool0[:], vT[0:P, :])
 
         def by_half(ap):
             return ap.rearrange("p (u g x) -> p g u x", u=2, x=16)
@@ -69,10 +67,12 @@ def tile_attend_rel2_kb_srtq256n512t1024_kernel(tc, q_words, q_scales, k_words, 
                 planes[32 * Q : 32 * Q + 4].rearrange("p o x -> p (o x)").bitcast(I32),
                 staged[TOP + 8 * Q : TOP + 8 * Q + 8, :].bitcast(I32),
             )
-        v_pool1 = sb.tile([P, T], F32, name="v_pool1", tag="v1_then_relu", align_bytes=64)
-        nc.sync.dma_start(v_pool1[:], vT[P : 2 * P, :])
+        v_pool0 = sb.tile([P, T], F32, name="v_pool0", tag="v1_then_relu", align_bytes=64)
+        nc.sync.dma_start(v_pool0[:], vT[0:P, :])
         kb_g = sb.tile([P, N], F32, name="kb_g", align_bytes=64)
         nc.vector.tensor_copy(by_half(kb_g[:].bitcast(U32)), kb_pool[:].bitcast(U32).indirect(offsets[:]))
+        v_pool1 = sb.tile([P, T], F32, name="v_pool1", tag="kb_then_v1", align_bytes=64)
+        nc.sync.dma_start(v_pool1[:], vT[P : 2 * P, :])
         kw_g = [
             sb.tile([P, N // 2], U32, name="kw_g0", align_bytes=64),
             sb.tile([P, N // 2], U32, name="kw_g1", tag="ks_kw_g_v_g", align_bytes=64),
@@ -147,7 +147,7 @@ def tile_attend_rel2_kb_srtq256n512t1024_kernel(tc, q_words, q_scales, k_words, 
         turn_values(0, "bank1")
         turn_values(1, "bank4")
 
-        w_in = sb.tile([P, 2, P, 4], BF16, name="w_in", align_bytes=64)
+        w_in = sb.tile([P, 2, P, 4], BF16, name="w_in", tag="kb_then_v1", align_bytes=64)
         wq = sb.tile([P, NQ], U32, name="wq", align_bytes=64)
         wq_s = sb.tile([P, NQ], U8, name="wq_s", align_bytes=64)
         vq = sb.tile([P, DV], U32, name="vq", align_bytes=64)

@@ -88,6 +88,9 @@ def tile_attend_rel2_kb_srtq256n512t1024_kernel(tc, q_words, q_scales, k_words, 
                 )
         vs_g = sb.tile([P, N], F32, name="vs_g", tag="kw_then_vs_g", align_bytes=64)
         nc.vector.tensor_copy(by_half(vs_g[:].bitcast(U32)), vs_pool[:].bitcast(U32).indirect(offsets[:]))
+        vs_col = sb.tile([P, 2, 8], F32, name="vs_col", tag="vs_col_then_vq", align_bytes=64)
+        for u in range(2):
+            nc.sync.dma_start(vs_col[:, u, 0:2], vs_g[ROW:P, u * N // 2 : (u + 1) * N // 2])
         v_g = [
             sb.tile([P, N], BF16, name="v_g0", tag="ks_kw_g_v_g", align_bytes=64),
             sb.tile([P, N], BF16, name="v_g1", tag="vs_then_v_g", align_bytes=64),
@@ -102,20 +105,11 @@ def tile_attend_rel2_kb_srtq256n512t1024_kernel(tc, q_words, q_scales, k_words, 
                 nc.tensor.transpose(turned[:, t, :], gathered[:, 2 * P * u + b : 2 * P * (u + 1) : 2], ident[:])
             return turned
 
-        v_in = sb.tile([P, 2, P * 4], BF16, name="v_in", align_bytes=64)
-
-        def turn_values(h, bank):
-            v_t = ps.tile([P, 2, P], F32, name="v%d_t" % h, tag=bank)
-            v_words = v_g[h][:].bitcast(F32)
-            for u in range(2):
-                nc.tensor.transpose(v_t[:, u, :], v_words[:, u * P : (u + 1) * P], ident[:])
-            nc.scalar.copy(v_in[:, h, :].bitcast(F32).rearrange("p (e u) -> p e u", u=2), v_t[:].rearrange("p u e -> p e u"))
-
         kb_t = turn(kb_g, "kb_t", "bank7")
         kb_col = sb.tile([P, 4], F32, name="kb_col")
         nc.scalar.copy(kb_col[:], kb_t[:, :, ROW])
 
-        relu = sb.tile([P, 8, P], F32, name="relu", align_bytes=64)
+        relu = sb.tile([P, 8, P], F32, name="relu", tag="relu_then_v_in", align_bytes=64)
         p = sb.tile([P, 2, 2, P, 2], F32, name="p", align_bytes=64)
         scores = {}
 
@@ -143,20 +137,24 @@ def tile_attend_rel2_kb_srtq256n512t1024_kernel(tc, q_words, q_scales, k_words, 
                     nc.scalar.activation(p[:, qb, t // 2], relu[:, i - 1 : i + 1].rearrange("p b q -> p q b"), ACT.Square)
 
         nc.vector.tensor_copy(by_half(v_g[1][:]), v_pool1[:].indirect(offsets[:]))
-        vs_t = turn(vs_g, "vs_t", "bank0")
-        turn_values(0, "bank1")
-        turn_values(1, "bank4")
+        v_t = ps.tile([P, 2, 2, P], F32, name="v_t", tag="bank6")
+        for h in range(2):
+            v_words = v_g[h][:].bitcast(F32)
+            for u in range(2):
+                nc.tensor.transpose(v_t[:, h, u, :], v_words[:, u * P : (u + 1) * P], ident[:])
+        v_in = sb.tile([P, 2, P * 4], BF16, name="v_in", tag="relu_then_v_in", align_bytes=64)
+        nc.scalar.copy(v_in[:].bitcast(F32).rearrange("p h (e u) -> p h e u", u=2), v_t[:].rearrange("p h u e -> p h e u"))
 
         w_in = sb.tile([P, 2, P, 4], BF16, name="w_in", tag="kb_then_v1", align_bytes=64)
         wq = sb.tile([P, NQ], U32, name="wq", align_bytes=64)
         wq_s = sb.tile([P, NQ], U8, name="wq_s", align_bytes=64)
-        vq = sb.tile([P, DV], U32, name="vq", align_bytes=64)
+        vq = sb.tile([P, DV], U32, name="vq", tag="vs_col_then_vq", align_bytes=64)
         vq_s = sb.tile([P, DV], U8, name="vq_s", align_bytes=64)
         def weigh(qb):
             nc.vector.tensor_tensor(
                 w_in[:, qb].rearrange("p q (u b) -> p q u b", b=2),
                 p[:, qb].rearrange("p u q b -> p q u b"),
-                vs_t[:, :, ROW:P].to_broadcast([P, 4, P]).rearrange("p (u b) q -> p q u b", b=2),
+                vs_col[:, :, 0:2].unsqueeze(1).to_broadcast([P, P, 2, 2]),
                 ALU.mult,
             )
 
@@ -176,7 +174,7 @@ def tile_attend_rel2_kb_srtq256n512t1024_kernel(tc, q_words, q_scales, k_words, 
         inv = [sb.tile([P, 1], F32, name="inv%d" % qb) for qb in range(2)]
         spent = sb.tile([P, 2, P], F32, name="spent")
         for qb in range(2):
-            p_t = ps.tile([P, P], F32, name="p_t%d" % qb, tag="bank%d" % (2 + qb))
+            p_t = ps.tile([P, P], F32, name="p_t%d" % qb, tag=("bank7", "bank2")[qb])
             for t in range(4):
                 nc.tensor.matmul(p_t[:], p[:, qb, t // 2, :, t % 2], ident[:], start=(t == 0), stop=(t == 3), is_transpose=True)
             nc.scalar.activation(spent[:, qb, :], p_t[:], ACT.Copy, bias=1.0 / P, accum_out=total[qb][:])
@@ -195,8 +193,8 @@ def tile_attend_rel2_kb_srtq256n512t1024_kernel(tc, q_words, q_scales, k_words, 
             rows = slice(qb * P, (qb + 1) * P)
             left, right = slice(0, P), slice(P, DV)
             res = sb.tile([P, DV], F32, name="res%d" % qb, align_bytes=64)
-            y_left = product(qb, left, "y%d_left" % qb, ("bank1", "bank6")[qb])
-            y_right = product(qb, right, "y%d_right" % qb, ("bank5", "bank7")[qb])
+            y_left = product(qb, left, "y%d_left" % qb, ("bank0", "bank3")[qb])
+            y_right = product(qb, right, "y%d_right" % qb, ("bank1", "bank4")[qb])
             nc.vector.tensor_scalar(res[:, left], y_left[:], inv[qb][:], None, ALU.mult)
             nc.scalar.activation(res[:, right], y_right[:], ACT.Copy, scale=inv[qb][:])
             nc.sync.dma_start(out[0, rows, left], res[:, left])

@@ -88,9 +88,6 @@ def tile_attend_rel2_kb_srtq256n512t1024_kernel(tc, q_words, q_scales, k_words, 
                 )
         vs_g = sb.tile([P, N], F32, name="vs_g", tag="kw_then_vs_g", align_bytes=64)
         nc.vector.tensor_copy(by_half(vs_g[:].bitcast(U32)), vs_pool[:].bitcast(U32).indirect(offsets[:]))
-        vs_col = sb.tile([P, 2, 8], F32, name="vs_col", tag="vs_col_then_vq", align_bytes=64)
-        for u in range(2):
-            nc.sync.dma_start(vs_col[:, u, 0:2], vs_g[ROW:P, u * N // 2 : (u + 1) * N // 2])
         v_g = [
             sb.tile([P, N], BF16, name="v_g0", tag="ks_kw_g_v_g", align_bytes=64),
             sb.tile([P, N], BF16, name="v_g1", tag="vs_then_v_g", align_bytes=64),
@@ -137,24 +134,25 @@ def tile_attend_rel2_kb_srtq256n512t1024_kernel(tc, q_words, q_scales, k_words, 
                     nc.scalar.activation(p[:, qb, t // 2], relu[:, i - 1 : i + 1].rearrange("p b q -> p q b"), ACT.Square)
 
         nc.vector.tensor_copy(by_half(v_g[1][:]), v_pool1[:].indirect(offsets[:]))
-        v_t = ps.tile([P, 2, 2, P], F32, name="v_t", tag="bank6")
+        vs_t = turn(vs_g, "vs_t", "bank0")
+        v_in = sb.tile([P, 2, P * 4], BF16, name="v_in", tag="relu_then_v_in", align_bytes=64)
         for h in range(2):
+            v_t = ps.tile([P, 2, P], F32, name="v%d_t" % h, tag=("bank6", "bank5")[h])
             v_words = v_g[h][:].bitcast(F32)
             for u in range(2):
-                nc.tensor.transpose(v_t[:, h, u, :], v_words[:, u * P : (u + 1) * P], ident[:])
-        v_in = sb.tile([P, 2, P * 4], BF16, name="v_in", tag="relu_then_v_in", align_bytes=64)
-        nc.scalar.copy(v_in[:].bitcast(F32).rearrange("p h (e u) -> p h e u", u=2), v_t[:].rearrange("p h u e -> p h e u"))
+                nc.tensor.transpose(v_t[:, u, :], v_words[:, u * P : (u + 1) * P], ident[:])
+            nc.scalar.copy(v_in[:, h, :].bitcast(F32).rearrange("p (e u) -> p e u", u=2), v_t[:].rearrange("p u e -> p e u"))
 
         w_in = sb.tile([P, 2, P, 4], BF16, name="w_in", tag="kb_then_v1", align_bytes=64)
         wq = sb.tile([P, NQ], U32, name="wq", align_bytes=64)
         wq_s = sb.tile([P, NQ], U8, name="wq_s", align_bytes=64)
-        vq = sb.tile([P, DV], U32, name="vq", tag="vs_col_then_vq", align_bytes=64)
+        vq = sb.tile([P, DV], U32, name="vq", align_bytes=64)
         vq_s = sb.tile([P, DV], U8, name="vq_s", align_bytes=64)
         def weigh(qb):
             nc.vector.tensor_tensor(
                 w_in[:, qb].rearrange("p q (u b) -> p q u b", b=2),
                 p[:, qb].rearrange("p u q b -> p q u b"),
-                vs_col[:, :, 0:2].unsqueeze(1).to_broadcast([P, P, 2, 2]),
+                vs_t[:, :, ROW:P].to_broadcast([P, 4, P]).rearrange("p (u b) q -> p q u b", b=2),
                 ALU.mult,
             )
 
@@ -193,8 +191,8 @@ def tile_attend_rel2_kb_srtq256n512t1024_kernel(tc, q_words, q_scales, k_words, 
             rows = slice(qb * P, (qb + 1) * P)
             left, right = slice(0, P), slice(P, DV)
             res = sb.tile([P, DV], F32, name="res%d" % qb, align_bytes=64)
-            y_left = product(qb, left, "y%d_left" % qb, ("bank0", "bank3")[qb])
-            y_right = product(qb, right, "y%d_right" % qb, ("bank1", "bank4")[qb])
+            y_left = product(qb, left, "y%d_left" % qb, ("bank1", "bank3")[qb])
+            y_right = product(qb, right, "y%d_right" % qb, ("bank4", "bank6")[qb])
             nc.vector.tensor_scalar(res[:, left], y_left[:], inv[qb][:], None, ALU.mult)
             nc.scalar.activation(res[:, right], y_right[:], ACT.Copy, scale=inv[qb][:])
             nc.sync.dma_start(out[0, rows, left], res[:, left])

@@ -32,7 +32,7 @@ def tile_attend_rel2_kb_srtq256n512t1024_kernel(tc, q_words, q_scales, k_words, 
         kb_pool = sb.tile([P, T], F32, name="kb_pool", tag="kb_then_v1", align_bytes=64)
         kw_pool = sb.tile([P, T], I32, name="kw_pool", tag="kw_then_vs_g", align_bytes=64)
         vs_pool = sb.tile([P, T], F32, name="vs_pool", tag="vs_then_v_g", align_bytes=64)
-        qw = sb.tile([P, 2, NQ], I32, name="qw", align_bytes=64)
+        v_pool0 = sb.tile([P, T], F32, name="v_pool0", align_bytes=64)
         staged = sb.tile([P, N + NQ], U8, name="staged", align_bytes=64)
         planes = sb.tile([P, 2, N + NQ], U8, name="planes", align_bytes=64)
         ident = sb.tile([P, P], F32, name="ident", align_bytes=64)
@@ -48,7 +48,10 @@ def tile_attend_rel2_kb_srtq256n512t1024_kernel(tc, q_words, q_scales, k_words, 
         nc.sync.dma_start(kb_pool[ROW:P, :], kb[0:1, :])
         nc.sync.dma_start(kw_pool[:], k_words[0].rearrange("g t b -> g (t b)").bitcast(I32))
         nc.sync.dma_start(vs_pool[ROW:P, :], vs[0:1, :])
-        nc.sync.dma_start(qw[:], q_words[0].rearrange("o g q r -> g o (q r)").bitcast(I32))
+        q_rows = q_words[0].rearrange("o g (c q) r -> c g o (q r)", c=2)
+        qw = [sb.tile([P, 2, P], I32, name="qw0", align_bytes=64)]
+        nc.sync.dma_start(qw[0][:], q_rows[0].bitcast(I32))
+        nc.sync.dma_start(v_pool0[:], vT[0:P, :])
 
         def by_half(ap):
             return ap.rearrange("p (u g x) -> p g u x", u=2, x=16)
@@ -67,8 +70,8 @@ def tile_attend_rel2_kb_srtq256n512t1024_kernel(tc, q_words, q_scales, k_words, 
                 planes[32 * Q : 32 * Q + 4].rearrange("p o x -> p (o x)").bitcast(I32),
                 staged[TOP + 8 * Q : TOP + 8 * Q + 8, :].bitcast(I32),
             )
-        v_pool0 = sb.tile([P, T], F32, name="v_pool0", tag="v1_then_relu", align_bytes=64)
-        nc.sync.dma_start(v_pool0[:], vT[0:P, :])
+        qw.append(sb.tile([P, 2, P], I32, name="qw1", tag="v1_then_relu", align_bytes=64))
+        nc.sync.dma_start(qw[1][:], q_rows[1].bitcast(I32))
         kb_g = sb.tile([P, N], F32, name="kb_g", align_bytes=64)
         nc.vector.tensor_copy(by_half(kb_g[:].bitcast(U32)), kb_pool[:].bitcast(U32).indirect(offsets[:]))
         v_pool1 = sb.tile([P, T], F32, name="v_pool1", tag="kb_then_v1", align_bytes=64)
@@ -112,12 +115,11 @@ def tile_attend_rel2_kb_srtq256n512t1024_kernel(tc, q_words, q_scales, k_words, 
 
         def score_pass(i, o):
             qb, t = divmod(i, 4)
-            cols = slice(qb * P, (qb + 1) * P)
             nc.tensor.matmul_mx(
                 out=scores[i][:],
                 lhsT=kw[t // 2][:, o, t % 2, :].bitcast(FP4X4),
                 lhsT_scale=planes[:, o, P * t : P * (t + 1)],
-                rhs=qw[:, o, cols].bitcast(FP8X4),
+                rhs=qw[qb][:, o, :].bitcast(FP8X4),
                 rhs_scale=planes[:, o, N + qb * P : N + (qb + 1) * P],
                 start=(o == 0),
                 stop=(o == 1),
@@ -168,15 +170,15 @@ def tile_attend_rel2_kb_srtq256n512t1024_kernel(tc, q_words, q_scales, k_words, 
         nc.vector.quantize_mx(out=vq[:].bitcast(FP8X4), scales=vq_s[:], in_=v_in[:].rearrange("p h x -> p (h x)"))
         quantise_weights(1)
 
-        total = [sb.tile([P, 1], F32, name="total%d" % qb) for qb in range(2)]
-        inv = [sb.tile([P, 1], F32, name="inv%d" % qb) for qb in range(2)]
+        total = sb.tile([P, 2], F32, name="total")
+        inv = sb.tile([P, 2], F32, name="inv")
         spent = sb.tile([P, 2, P], F32, name="spent")
         for qb in range(2):
             p_t = ps.tile([P, P], F32, name="p_t%d" % qb, tag=("bank7", "bank2")[qb])
             for t in range(4):
                 nc.tensor.matmul(p_t[:], p[:, qb, t // 2, :, t % 2], ident[:], start=(t == 0), stop=(t == 3), is_transpose=True)
-            nc.scalar.activation(spent[:, qb, :], p_t[:], ACT.Copy, bias=1.0 / P, accum_out=total[qb][:])
-            nc.vector.reciprocal(inv[qb][:], total[qb][:])
+            nc.scalar.activation(spent[:, qb, :], p_t[:], ACT.Copy, bias=1.0 / P, accum_out=total[:, qb : qb + 1])
+        nc.vector.reciprocal(inv[:], total[:])
 
         def product(qb, cols, name, bank):
             rows = slice(qb * P, (qb + 1) * P)
@@ -193,7 +195,7 @@ def tile_attend_rel2_kb_srtq256n512t1024_kernel(tc, q_words, q_scales, k_words, 
             res = sb.tile([P, DV], F32, name="res%d" % qb, align_bytes=64)
             y_left = product(qb, left, "y%d_left" % qb, ("bank1", "bank3")[qb])
             y_right = product(qb, right, "y%d_right" % qb, ("bank4", "bank6")[qb])
-            nc.vector.tensor_scalar(res[:, left], y_left[:], inv[qb][:], None, ALU.mult)
-            nc.scalar.activation(res[:, right], y_right[:], ACT.Copy, scale=inv[qb][:])
+            nc.vector.tensor_scalar(res[:, left], y_left[:], inv[:, qb : qb + 1], None, ALU.mult)
+            nc.scalar.activation(res[:, right], y_right[:], ACT.Copy, scale=inv[:, qb : qb + 1])
             nc.sync.dma_start(out[0, rows, left], res[:, left])
             nc.scalar.dma_start(out[0, rows, right], res[:, right])

@@ -28,13 +28,14 @@ def tile_attend_rel2_kb_srtq256n512t1024_kernel(tc, q_words, q_scales, k_words, 
         ps = ctx.enter_context(tc.psum_pool(name="ps", bufs=1))
 
         offsets = sb.tile([P, N // 16], U16, name="offsets")
-        ks_pool = sb.tile([P, T // 4], I32, name="ks_pool", tag="ks_kw_g_v_g", align_bytes=64)
-        kb_pool = sb.tile([P, T], F32, name="kb_pool", tag="kb_then_v1", align_bytes=64)
-        kw_pool = sb.tile([P, T], I32, name="kw_pool", tag="kw_then_vs_g", align_bytes=64)
-        vs_pool = sb.tile([P, T], F32, name="vs_pool", tag="vs_then_v_g", align_bytes=64)
+        ks_pool = sb.tile([P, T // 4], I32, name="ks_pool", align_bytes=64)
+        kb_pool = sb.tile([P, T], F32, name="kb_pool", align_bytes=64)
+        vs_pool = sb.tile([P, T], F32, name="vs_pool", align_bytes=64)
+        kw_pool = sb.tile([P, T], I32, name="kw_pool", align_bytes=64)
         v_pool0 = sb.tile([P, T], F32, name="v_pool0", align_bytes=64)
         staged = sb.tile([P, N + NQ], U8, name="staged", align_bytes=64)
         planes = sb.tile([P, 2, N + NQ], U8, name="planes", align_bytes=64)
+        qw = sb.tile([P, 2, NQ], I32, name="qw", align_bytes=64)
         ident = sb.tile([P, P], F32, name="ident", align_bytes=64)
 
         make_identity(nc, ident[:])
@@ -42,119 +43,96 @@ def tile_attend_rel2_kb_srtq256n512t1024_kernel(tc, q_words, q_scales, k_words, 
         nc.vector.memset(kb_pool[0:ROW, :].bitcast(I32), 0)
         nc.vector.memset(vs_pool[0:ROW, :].bitcast(I32), 0)
 
+        warm = sb.tile([P, 1], F32, name="warm")
+        nc.scalar.activation(warm[0:32, :], kb_pool[0:32, 0:1], ACT.Relu)
+
         nc.sync.dma_start(offsets[:], offs)
         nc.sync.dma_start(ks_pool[TOP:P, :], k_scales.rearrange("o f t -> f o t").bitcast(I32))
         nc.sync.dma_start(staged[TOP:P, N : N + NQ].bitcast(I32), q_scales[0].rearrange("o f q -> f o q").bitcast(I32))
         nc.sync.dma_start(kb_pool[ROW:P, :], kb[0:1, :])
         nc.sync.dma_start(kw_pool[:], k_words[0].rearrange("g t b -> g (t b)").bitcast(I32))
         nc.sync.dma_start(vs_pool[ROW:P, :], vs[0:1, :])
-        q_rows = q_words[0].rearrange("o g (c q) r -> c g o (q r)", c=2)
-        qw = [sb.tile([P, 2, P], I32, name="qw0", align_bytes=64)]
-        nc.sync.dma_start(qw[0][:], q_rows[0].bitcast(I32))
+        nc.sync.dma_start(qw[:], q_words[0].rearrange("o g q r -> g o (q r)").bitcast(I32))
         nc.sync.dma_start(v_pool0[:], vT[0:P, :])
 
-        def by_half(ap):
-            return ap.rearrange("p (u g x) -> p g u x", u=2, x=16)
+        def by_place(ap):
+            return ap.rearrange("p (t m) -> p m t", t=4)
 
-        ks_g = sb.tile([P, N], U8, name="ks_g", tag="v1_then_relu", align_bytes=64)
-        half_list = [offsets[:, 0 : N // 32], offsets[:, N // 32 : N // 16]]
-        for c in range(2):
-            nc.vector.tensor_copy(ks_g[:, c * N // 2 : (c + 1) * N // 2], ks_pool[:].bitcast(U8).indirect(half_list[c]))
-        for c in range(2):
-            nc.vector.tensor_copy(
-                staged[:, 0:N].rearrange("p (u b c g j) -> p c u b g j", u=2, b=2, c=2, j=8)[:, c],
-                ks_g[:, c * N // 2 : (c + 1) * N // 2].rearrange("p (g u j b) -> p u b g j", u=2, j=8, b=2),
-            )
+        ks_g = sb.tile([P, N], U8, name="ks_g", tag="ks_g_then_v1", align_bytes=64)
+        nc.vector.tensor_copy(by_place(ks_g[:]), ks_pool[:].bitcast(U8).indirect(offsets[:]))
+        nc.vector.tensor_copy(staged[:, 0:N].bitcast(I32), ks_g[:].bitcast(I32))
         for Q in range(4):
             nc.sync.dma_start(
                 planes[32 * Q : 32 * Q + 4].rearrange("p o x -> p (o x)").bitcast(I32),
                 staged[TOP + 8 * Q : TOP + 8 * Q + 8, :].bitcast(I32),
             )
-        qw.append(sb.tile([P, 2, P], I32, name="qw1", tag="v1_then_relu", align_bytes=64))
-        nc.sync.dma_start(qw[1][:], q_rows[1].bitcast(I32))
-        kb_g = sb.tile([P, N], F32, name="kb_g", align_bytes=64)
-        nc.vector.tensor_copy(by_half(kb_g[:].bitcast(U32)), kb_pool[:].bitcast(U32).indirect(offsets[:]))
-        v_pool1 = sb.tile([P, T], F32, name="v_pool1", tag="kb_then_v1", align_bytes=64)
+        v_pool1 = sb.tile([P, T], F32, name="v_pool1", tag="ks_g_then_v1", align_bytes=64)
         nc.sync.dma_start(v_pool1[:], vT[P : 2 * P, :])
-        kw_g = [
-            sb.tile([P, N // 2], U32, name="kw_g0", align_bytes=64),
-            sb.tile([P, N // 2], U32, name="kw_g1", tag="ks_kw_g_v_g", align_bytes=64),
-        ]
-        for c in range(2):
-            nc.vector.tensor_copy(by_half(kw_g[c][:]), kw_pool[:].bitcast(U32).indirect(half_list[c]))
-        kw = [sb.tile([P, 2, 2, 2 * P], U8, name="kw%d" % u, align_bytes=64) for u in range(2)]
-        for u in range(2):
-            for c in range(2):
-                nc.vector.tensor_copy(
-                    kw[u][:].bitcast(U16).rearrange("p o b (c m) -> p c o b m", c=2)[:, c],
-                    kw_g[c][:].bitcast(U16).rearrange("p (u m b o) -> p u o b m", u=2, b=2, o=2)[:, u],
-                )
-        vs_g = sb.tile([P, N], F32, name="vs_g", tag="kw_then_vs_g", align_bytes=64)
-        nc.vector.tensor_copy(by_half(vs_g[:].bitcast(U32)), vs_pool[:].bitcast(U32).indirect(offsets[:]))
-        v_g = [
-            sb.tile([P, N], BF16, name="v_g0", tag="ks_kw_g_v_g", align_bytes=64),
-            sb.tile([P, N], BF16, name="v_g1", tag="vs_then_v_g", align_bytes=64),
-        ]
-        nc.vector.tensor_copy(by_half(v_g[0][:]), v_pool0[:].indirect(offsets[:]))
+        kw_g = sb.tile([P, N], U32, name="kw_g", tag="kw_g_then_v_g", align_bytes=64)
+        nc.vector.tensor_copy(by_place(kw_g[:]), kw_pool[:].bitcast(U32).indirect(offsets[:]))
+        kw = [sb.tile([P, 2 * N], U8, name="kw%d" % o, align_bytes=64) for o in range(2)]
+        for o in range(2):
+            nc.vector.tensor_copy(kw[o][:].bitcast(U16), kw_g[:].bitcast(U16).rearrange("p (m o) -> p o m", o=2)[:, o])
 
+        kb_g = sb.tile([P, N], F32, name="kb_g", align_bytes=64)
+        nc.scalar.activation(kb_g[:], kb_pool[:].indirect(offsets[:]), ACT.Copy)
+        vs_g = sb.tile([P, N], F32, name="vs_g", align_bytes=64)
+        nc.scalar.activation(vs_g[:], vs_pool[:].indirect(offsets[:]), ACT.Copy)
+        vs_col = sb.tile([P, 4], F32, name="vs_col")
+        nc.sync.dma_start(vs_col[:], vs_g[ROW:P, :].rearrange("o (m t) -> o m t", t=4))
 
-        def turn(gathered, name, bank):
-            turned = ps.tile([P, 4, P], F32, name=name, tag=bank)
-            for t in range(4):
-                u, b = divmod(t, 2)
-                nc.tensor.transpose(turned[:, t, :], gathered[:, 2 * P * u + b : 2 * P * (u + 1) : 2], ident[:])
-            return turned
-
-        kb_t = turn(kb_g, "kb_t", "bank7")
+        kb_t = ps.tile([P, 4, P], F32, name="kb_t", tag="bank7")
+        for t in range(4):
+            nc.tensor.transpose(kb_t[:, t, :], kb_g[:, t:N:4], ident[:])
         kb_col = sb.tile([P, 4], F32, name="kb_col")
         nc.scalar.copy(kb_col[:], kb_t[:, :, ROW])
 
-        relu = sb.tile([P, 8, P], F32, name="relu", tag="relu_then_v_in", align_bytes=64)
+        v_g = [
+            sb.tile([P, N], BF16, name="v_g0", tag="kw_g_then_v_g", align_bytes=64),
+            sb.tile([P, N], BF16, name="v_g1", align_bytes=64),
+        ]
+        nc.vector.tensor_copy(v_g[0][:], v_pool0[:].indirect(offsets[:]))
+        nc.vector.tensor_copy(v_g[1][:], v_pool1[:].indirect(offsets[:]))
+
+        scores = [ps.tile([P, P], F32, name="score%d" % i, tag="bank%d" % i) for i in range(8)]
+        relu = sb.tile([P, 8, P], F32, name="relu", align_bytes=64)
         p = sb.tile([P, 2, 2, P, 2], F32, name="p", align_bytes=64)
-        scores = {}
-
-        def score_pass(i, o):
+        for i in range(8):
             qb, t = divmod(i, 4)
-            nc.tensor.matmul_mx(
-                out=scores[i][:],
-                lhsT=kw[t // 2][:, o, t % 2, :].bitcast(FP4X4),
-                lhsT_scale=planes[:, o, P * t : P * (t + 1)],
-                rhs=qw[qb][:, o, :].bitcast(FP8X4),
-                rhs_scale=planes[:, o, N + qb * P : N + (qb + 1) * P],
-                start=(o == 0),
-                stop=(o == 1),
-            )
+            for o in range(2):
+                nc.tensor.matmul_mx(
+                    out=scores[i][:],
+                    lhsT=kw[o][:, 2 * P * t : 2 * P * (t + 1)].bitcast(FP4X4),
+                    lhsT_scale=planes[:, o, P * t : P * (t + 1)],
+                    rhs=qw[:, o, qb * P : (qb + 1) * P].bitcast(FP8X4),
+                    rhs_scale=planes[:, o, N + qb * P : N + (qb + 1) * P],
+                    start=(o == 0),
+                    stop=(o == 1),
+                )
+            nc.scalar.activation(relu[:, i, :], scores[i][:], ACT.Relu, bias=kb_col[:, t : t + 1])
+            if t % 2 == 1:
+                nc.scalar.activation(p[:, qb, t // 2], relu[:, i - 1 : i + 1].rearrange("p b q -> p q b"), ACT.Square)
 
-        for qb in range(2):
-            for t in range(4):
-                i = 4 * qb + t
-                scores[i] = ps.tile([P, P], F32, name="score%d" % i, tag="bank%d" % i)
-                score_pass(i, 0)
-                score_pass(i, 1)
-                nc.scalar.activation(relu[:, i, :], scores[i][:], ACT.Relu, bias=kb_col[:, t : t + 1])
-                if t % 2 == 1:
-                    nc.scalar.activation(p[:, qb, t // 2], relu[:, i - 1 : i + 1].rearrange("p b q -> p q b"), ACT.Square)
-
-        nc.vector.tensor_copy(by_half(v_g[1][:]), v_pool1[:].indirect(offsets[:]))
-        vs_t = turn(vs_g, "vs_t", "bank0")
-        v_in = sb.tile([P, 2, P * 4], BF16, name="v_in", tag="relu_then_v_in", align_bytes=64)
+        v_in = sb.tile([P, 2, P * 4], BF16, name="v_in", align_bytes=64)
         for h in range(2):
             v_t = ps.tile([P, 2, P], F32, name="v%d_t" % h, tag=("bank6", "bank5")[h])
             v_words = v_g[h][:].bitcast(F32)
             for u in range(2):
-                nc.tensor.transpose(v_t[:, u, :], v_words[:, u * P : (u + 1) * P], ident[:])
+                nc.tensor.transpose(v_t[:, u, :], v_words[:, u : 2 * P : 2], ident[:])
             nc.scalar.copy(v_in[:, h, :].bitcast(F32).rearrange("p (e u) -> p e u", u=2), v_t[:].rearrange("p u e -> p e u"))
 
-        w_in = sb.tile([P, 2, P, 4], BF16, name="w_in", tag="kb_then_v1", align_bytes=64)
+        w_in = sb.tile([P, 2, P, 4], BF16, name="w_in", align_bytes=64)
         wq = sb.tile([P, NQ], U32, name="wq", align_bytes=64)
         wq_s = sb.tile([P, NQ], U8, name="wq_s", align_bytes=64)
         vq = sb.tile([P, DV], U32, name="vq", align_bytes=64)
         vq_s = sb.tile([P, DV], U8, name="vq_s", align_bytes=64)
+        vs_wide = vs_col[:].rearrange("p (t o) -> p t o", o=1).to_broadcast([P, 4, P])
+
         def weigh(qb):
             nc.vector.tensor_tensor(
                 w_in[:, qb].rearrange("p q (u b) -> p q u b", b=2),
                 p[:, qb].rearrange("p u q b -> p q u b"),
-                vs_t[:, :, ROW:P].to_broadcast([P, 4, P]).rearrange("p (u b) q -> p q u b", b=2),
+                vs_wide.rearrange("p (u b) q -> p q u b", b=2),
                 ALU.mult,
             )
 
@@ -193,8 +171,8 @@ def tile_attend_rel2_kb_srtq256n512t1024_kernel(tc, q_words, q_scales, k_words, 
             rows = slice(qb * P, (qb + 1) * P)
             left, right = slice(0, P), slice(P, DV)
             res = sb.tile([P, DV], F32, name="res%d" % qb, align_bytes=64)
-            y_left = product(qb, left, "y%d_left" % qb, ("bank1", "bank3")[qb])
-            y_right = product(qb, right, "y%d_right" % qb, ("bank4", "bank6")[qb])
+            y_left = product(qb, left, "y%d_left" % qb, ("bank1", "bank5")[qb])
+            y_right = product(qb, right, "y%d_right" % qb, ("bank0", "bank6")[qb])
             nc.vector.tensor_scalar(res[:, left], y_left[:], inv[:, qb : qb + 1], None, ALU.mult)
             nc.scalar.activation(res[:, right], y_right[:], ACT.Copy, scale=inv[:, qb : qb + 1])
             nc.sync.dma_start(out[0, rows, left], res[:, left])

@@ -78,12 +78,15 @@ def tile_attend_rel2_kb_srtq256n512t1024_kernel(tc, q_words, q_scales, k_words, 
         nc.scalar.activation(kb_g[:], kb_pool[:].indirect(offsets[:]), ACT.Copy)
         vs_g = sb.tile([P, N], F32, name="vs_g", align_bytes=64)
         nc.scalar.activation(vs_g[:], vs_pool[:].indirect(offsets[:]), ACT.Copy)
-        vs_col = sb.tile([P, 4], F32, name="vs_col")
-        nc.sync.dma_start(vs_col[:], vs_g[ROW:P, :].rearrange("o (m t) -> o m t", t=4))
 
-        kb_t = ps.tile([P, 4, P], F32, name="kb_t", tag="bank7")
-        for t in range(4):
-            nc.tensor.transpose(kb_t[:, t, :], kb_g[:, t:N:4], ident[:])
+        def turn(gathered, name, bank):
+            turned = ps.tile([P, 4, P], F32, name=name, tag=bank)
+            for t in range(4):
+                nc.tensor.transpose(turned[:, t, :], gathered[:, t:N:4], ident[:])
+            return turned
+
+        kb_t = turn(kb_g, "kb_t", "bank6")
+        vs_t = turn(vs_g, "vs_t", "bank7")
         kb_col = sb.tile([P, 4], F32, name="kb_col")
         nc.scalar.copy(kb_col[:], kb_t[:, :, ROW])
 
@@ -94,14 +97,14 @@ def tile_attend_rel2_kb_srtq256n512t1024_kernel(tc, q_words, q_scales, k_words, 
         nc.vector.tensor_copy(v_g[0][:], v_pool0[:].indirect(offsets[:]))
         nc.vector.tensor_copy(v_g[1][:], v_pool1[:].indirect(offsets[:]))
 
-        scores = [ps.tile([P, P], F32, name="score%d" % i, tag="bank%d" % i) for i in range(8)]
         relu = sb.tile([P, 8, P], F32, name="relu", align_bytes=64)
         p = sb.tile([P, 2, 2, P, 2], F32, name="p", align_bytes=64)
         for i in range(8):
             qb, t = divmod(i, 4)
+            score = ps.tile([P, P], F32, name="score%d" % i, tag="bank%d" % (i % 7))
             for o in range(2):
                 nc.tensor.matmul_mx(
-                    out=scores[i][:],
+                    out=score[:],
                     lhsT=kw[o][:, 2 * P * t : 2 * P * (t + 1)].bitcast(FP4X4),
                     lhsT_scale=planes[:, o, P * t : P * (t + 1)],
                     rhs=qw[:, o, qb * P : (qb + 1) * P].bitcast(FP8X4),
@@ -109,7 +112,7 @@ def tile_attend_rel2_kb_srtq256n512t1024_kernel(tc, q_words, q_scales, k_words, 
                     start=(o == 0),
                     stop=(o == 1),
                 )
-            nc.scalar.activation(relu[:, i, :], scores[i][:], ACT.Relu, bias=kb_col[:, t : t + 1])
+            nc.scalar.activation(relu[:, i, :], score[:], ACT.Relu, bias=kb_col[:, t : t + 1])
             if t % 2 == 1:
                 nc.scalar.activation(p[:, qb, t // 2], relu[:, i - 1 : i + 1].rearrange("p b q -> p q b"), ACT.Square)
 
@@ -126,7 +129,7 @@ def tile_attend_rel2_kb_srtq256n512t1024_kernel(tc, q_words, q_scales, k_words, 
         wq_s = sb.tile([P, NQ], U8, name="wq_s", align_bytes=64)
         vq = sb.tile([P, DV], U32, name="vq", align_bytes=64)
         vq_s = sb.tile([P, DV], U8, name="vq_s", align_bytes=64)
-        vs_wide = vs_col[:].rearrange("p (t o) -> p t o", o=1).to_broadcast([P, 4, P])
+        vs_wide = vs_t[:, :, ROW:P].to_broadcast([P, 4, P])
 
         def weigh(qb):
             nc.vector.tensor_tensor(
@@ -152,7 +155,7 @@ def tile_attend_rel2_kb_srtq256n512t1024_kernel(tc, q_words, q_scales, k_words, 
         inv = sb.tile([P, 2], F32, name="inv")
         spent = sb.tile([P, 2, P], F32, name="spent")
         for qb in range(2):
-            p_t = ps.tile([P, P], F32, name="p_t%d" % qb, tag=("bank7", "bank2")[qb])
+            p_t = ps.tile([P, P], F32, name="p_t%d" % qb, tag=("bank0", "bank2")[qb])
             for t in range(4):
                 nc.tensor.matmul(p_t[:], p[:, qb, t // 2, :, t % 2], ident[:], start=(t == 0), stop=(t == 3), is_transpose=True)
             nc.scalar.activation(spent[:, qb, :], p_t[:], ACT.Copy, bias=1.0 / P, accum_out=total[:, qb : qb + 1])
@@ -171,8 +174,8 @@ def tile_attend_rel2_kb_srtq256n512t1024_kernel(tc, q_words, q_scales, k_words, 
             rows = slice(qb * P, (qb + 1) * P)
             left, right = slice(0, P), slice(P, DV)
             res = sb.tile([P, DV], F32, name="res%d" % qb, align_bytes=64)
-            y_left = product(qb, left, "y%d_left" % qb, ("bank1", "bank5")[qb])
-            y_right = product(qb, right, "y%d_right" % qb, ("bank0", "bank6")[qb])
+            y_left = product(qb, left, "y%d_left" % qb, ("bank1", "bank3")[qb])
+            y_right = product(qb, right, "y%d_right" % qb, ("bank4", "bank6")[qb])
             nc.vector.tensor_scalar(res[:, left], y_left[:], inv[:, qb : qb + 1], None, ALU.mult)
             nc.scalar.activation(res[:, right], y_right[:], ACT.Copy, scale=inv[:, qb : qb + 1])
             nc.sync.dma_start(out[0, rows, left], res[:, left])

@@ -25,6 +25,7 @@ def tile_attend_rel2_kb_srtq256n512t1024_kernel(tc, q_words, q_scales, k_words, 
     nc = tc.nc
     with ExitStack() as ctx:
         sb = ctx.enter_context(tc.tile_pool(name="sb", bufs=1))
+        placed = ctx.enter_context(tc.tile_pool(name="placed", bufs=1))
         ps = ctx.enter_context(tc.psum_pool(name="ps", bufs=1))
 
         offsets = sb.tile([P, N // 16], U16, name="offsets")
@@ -35,30 +36,31 @@ def tile_attend_rel2_kb_srtq256n512t1024_kernel(tc, q_words, q_scales, k_words, 
         v_pool0 = sb.tile([P, T], F32, name="v_pool0", align_bytes=64)
         staged = sb.tile([P, N + NQ], U8, name="staged", align_bytes=64)
         planes = sb.tile([P, 2, N + NQ], U8, name="planes", align_bytes=64)
-        qw = sb.tile([P, 2, NQ], I32, name="qw", align_bytes=64)
         ident = sb.tile([P, P], F32, name="ident", align_bytes=64)
 
         make_identity(nc, ident[:])
         nc.vector.memset(ks_pool[0:TOP, :], 0)
-        nc.vector.memset(kb_pool[0:ROW, :].bitcast(I32), 0)
         nc.vector.memset(vs_pool[0:ROW, :].bitcast(I32), 0)
+        nc.vector.memset(kb_pool[0:ROW, :].bitcast(I32), 0)
 
         warm = sb.tile([P, 1], F32, name="warm")
-        nc.scalar.activation(warm[0:32, :], kb_pool[0:32, 0:1], ACT.Relu)
+        nc.scalar.activation(warm[0:32, :], vs_pool[0:32, 0:1], ACT.Relu)
 
         nc.sync.dma_start(offsets[:], offs)
         nc.sync.dma_start(ks_pool[TOP:P, :], k_scales.rearrange("o f t -> f o t").bitcast(I32))
         nc.sync.dma_start(staged[TOP:P, N : N + NQ].bitcast(I32), q_scales[0].rearrange("o f q -> f o q").bitcast(I32))
+        nc.sync.dma_start(vs_pool[ROW:P, :], vs[0:1, :])
         nc.sync.dma_start(kb_pool[ROW:P, :], kb[0:1, :])
         nc.sync.dma_start(kw_pool[:], k_words[0].rearrange("g t b -> g (t b)").bitcast(I32))
-        nc.sync.dma_start(vs_pool[ROW:P, :], vs[0:1, :])
-        nc.sync.dma_start(qw[:], q_words[0].rearrange("o g q r -> g o (q r)").bitcast(I32))
+        q_rows = q_words[0].rearrange("o g (c q) r -> c g o (q r)", c=2)
+        qw = [sb.tile([P, 2, P], I32, name="qw0", align_bytes=64)]
+        nc.sync.dma_start(qw[0][:], q_rows[0].bitcast(I32))
         nc.sync.dma_start(v_pool0[:], vT[0:P, :])
 
         def by_place(ap):
             return ap.rearrange("p (t m) -> p m t", t=4)
 
-        ks_g = sb.tile([P, N], U8, name="ks_g", tag="ks_g_then_v1", align_bytes=64)
+        ks_g = placed.tile([P, N], U8, name="ks_g", offset=8 * P - N // 2, align_bytes=64)
         nc.vector.tensor_copy(by_place(ks_g[:]), ks_pool[:].bitcast(U8).indirect(offsets[:]))
         nc.vector.tensor_copy(staged[:, 0:N].bitcast(I32), ks_g[:].bitcast(I32))
         for Q in range(4):
@@ -66,27 +68,27 @@ def tile_attend_rel2_kb_srtq256n512t1024_kernel(tc, q_words, q_scales, k_words, 
                 planes[32 * Q : 32 * Q + 4].rearrange("p o x -> p (o x)").bitcast(I32),
                 staged[TOP + 8 * Q : TOP + 8 * Q + 8, :].bitcast(I32),
             )
-        v_pool1 = sb.tile([P, T], F32, name="v_pool1", tag="ks_g_then_v1", align_bytes=64)
+        qw.append(placed.tile([P, 2, P], I32, name="qw1", offset=0, align_bytes=64))
+        nc.sync.dma_start(qw[1][:], q_rows[1].bitcast(I32))
+        v_pool1 = placed.tile([P, T], F32, name="v_pool1", offset=8 * P, align_bytes=64)
         nc.sync.dma_start(v_pool1[:], vT[P : 2 * P, :])
+        kb_g = sb.tile([P, N], F32, name="kb_g", align_bytes=64)
+        nc.vector.tensor_copy(by_place(kb_g[:].bitcast(U32)), kb_pool[:].bitcast(U32).indirect(offsets[:]))
         kw_g = sb.tile([P, N], U32, name="kw_g", tag="kw_g_then_v_g", align_bytes=64)
         nc.vector.tensor_copy(by_place(kw_g[:]), kw_pool[:].bitcast(U32).indirect(offsets[:]))
-        kw = [sb.tile([P, 2 * N], U8, name="kw%d" % o, align_bytes=64) for o in range(2)]
-        for o in range(2):
-            nc.vector.tensor_copy(kw[o][:].bitcast(U16), kw_g[:].bitcast(U16).rearrange("p (m o) -> p o m", o=2)[:, o])
+        kw = [sb.tile([P, 2, N], U8, name="kw%d" % u, align_bytes=64) for u in range(2)]
+        for u in range(2):
+            nc.vector.tensor_copy(kw[u][:].bitcast(U16), kw_g[:].bitcast(U16).rearrange("p (u m o) -> p u o m", u=2, o=2)[:, u])
 
-        kb_g = sb.tile([P, N], F32, name="kb_g", align_bytes=64)
-        nc.scalar.activation(kb_g[:], kb_pool[:].indirect(offsets[:]), ACT.Copy)
         vs_g = sb.tile([P, N], F32, name="vs_g", align_bytes=64)
         nc.scalar.activation(vs_g[:], vs_pool[:].indirect(offsets[:]), ACT.Copy)
 
-        def turn(gathered, name, bank):
-            turned = ps.tile([P, 4, P], F32, name=name, tag=bank)
-            for t in range(4):
-                nc.tensor.transpose(turned[:, t, :], gathered[:, t:N:4], ident[:])
-            return turned
-
-        kb_t = turn(kb_g, "kb_t", "bank6")
-        vs_t = turn(vs_g, "vs_t", "bank7")
+        vs_t = ps.tile([P, 4, P], F32, name="vs_t", tag="bank7")
+        kb_t = ps.tile([P, 4, P], F32, name="kb_t", tag="bank6")
+        for t in range(4):
+            nc.tensor.transpose(vs_t[:, t, :], vs_g[:, t:N:4], ident[:])
+        for t in range(4):
+            nc.tensor.transpose(kb_t[:, t, :], kb_g[:, t * P : (t + 1) * P], ident[:])
         kb_col = sb.tile([P, 4], F32, name="kb_col")
         nc.scalar.copy(kb_col[:], kb_t[:, :, ROW])
 
@@ -94,10 +96,10 @@ def tile_attend_rel2_kb_srtq256n512t1024_kernel(tc, q_words, q_scales, k_words, 
             sb.tile([P, N], BF16, name="v_g0", tag="kw_g_then_v_g", align_bytes=64),
             sb.tile([P, N], BF16, name="v_g1", align_bytes=64),
         ]
-        nc.vector.tensor_copy(v_g[0][:], v_pool0[:].indirect(offsets[:]))
-        nc.vector.tensor_copy(v_g[1][:], v_pool1[:].indirect(offsets[:]))
+        for h, v_pool in enumerate((v_pool0, v_pool1)):
+            nc.vector.tensor_copy(v_g[h][:].rearrange("p (u m b) -> p m u b", u=2, b=2), v_pool[:].indirect(offsets[:]))
 
-        relu = sb.tile([P, 8, P], F32, name="relu", align_bytes=64)
+        relu = sb.tile([P, 8, P], F32, name="relu", tag="relu_then_v_in", align_bytes=64)
         p = sb.tile([P, 2, 2, P, 2], F32, name="p", align_bytes=64)
         for i in range(8):
             qb, t = divmod(i, 4)
@@ -105,9 +107,9 @@ def tile_attend_rel2_kb_srtq256n512t1024_kernel(tc, q_words, q_scales, k_words, 
             for o in range(2):
                 nc.tensor.matmul_mx(
                     out=score[:],
-                    lhsT=kw[o][:, 2 * P * t : 2 * P * (t + 1)].bitcast(FP4X4),
+                    lhsT=kw[t // 2][:, o, 2 * P * (t % 2) : 2 * P * (t % 2 + 1)].bitcast(FP4X4),
                     lhsT_scale=planes[:, o, P * t : P * (t + 1)],
-                    rhs=qw[:, o, qb * P : (qb + 1) * P].bitcast(FP8X4),
+                    rhs=qw[qb][:, o, :].bitcast(FP8X4),
                     rhs_scale=planes[:, o, N + qb * P : N + (qb + 1) * P],
                     start=(o == 0),
                     stop=(o == 1),
@@ -116,15 +118,15 @@ def tile_attend_rel2_kb_srtq256n512t1024_kernel(tc, q_words, q_scales, k_words, 
             if t % 2 == 1:
                 nc.scalar.activation(p[:, qb, t // 2], relu[:, i - 1 : i + 1].rearrange("p b q -> p q b"), ACT.Square)
 
-        v_in = sb.tile([P, 2, P * 4], BF16, name="v_in", align_bytes=64)
+        v_in = sb.tile([P, 2, P * 4], BF16, name="v_in", tag="relu_then_v_in", align_bytes=64)
         for h in range(2):
             v_t = ps.tile([P, 2, P], F32, name="v%d_t" % h, tag=("bank6", "bank5")[h])
             v_words = v_g[h][:].bitcast(F32)
             for u in range(2):
-                nc.tensor.transpose(v_t[:, u, :], v_words[:, u : 2 * P : 2], ident[:])
+                nc.tensor.transpose(v_t[:, u, :], v_words[:, u * P : (u + 1) * P], ident[:])
             nc.scalar.copy(v_in[:, h, :].bitcast(F32).rearrange("p (e u) -> p e u", u=2), v_t[:].rearrange("p u e -> p e u"))
 
-        w_in = sb.tile([P, 2, P, 4], BF16, name="w_in", align_bytes=64)
+        w_in = placed.tile([P, 2, P, 4], BF16, name="w_in", offset=8 * P, align_bytes=64)
         wq = sb.tile([P, NQ], U32, name="wq", align_bytes=64)
         wq_s = sb.tile([P, NQ], U8, name="wq_s", align_bytes=64)
         vq = sb.tile([P, DV], U32, name="vq", align_bytes=64)

@@ -1,7 +1,6 @@
 from contextlib import ExitStack
 
 import concourse.mybir as mybir
-from concourse.masks import make_identity
 
 F32 = mybir.dt.float32
 BF16 = mybir.dt.bfloat16
@@ -32,26 +31,30 @@ def tile_attend_rel2_kb_srtq256n512t1024_kernel(tc, q_words, q_scales, k_words, 
         ks_pool = sb.tile([P, T // 4], I32, name="ks_pool", align_bytes=64)
         kb_pool = sb.tile([P, T], F32, name="kb_pool", align_bytes=64)
         vs_pool = sb.tile([P, T], F32, name="vs_pool", align_bytes=64)
-        kw_pool = sb.tile([P, T], I32, name="kw_pool", align_bytes=64)
+        kw_pool = sb.tile([P, T], I32, name="kw_pool", tag="kw_then_vs_g", align_bytes=64)
         v_pool0 = sb.tile([P, T], F32, name="v_pool0", align_bytes=64)
         staged = sb.tile([P, N + NQ], U8, name="staged", align_bytes=64)
         planes = sb.tile([P, 2, N + NQ], U8, name="planes", align_bytes=64)
         ident = sb.tile([P, P], F32, name="ident", align_bytes=64)
 
-        make_identity(nc, ident[:])
+        zeros = placed.tile([P, 2 * P + T], F32, name="zeros", offset=0, align_bytes=64)
+        nc.gpsimd.memset(zeros[:, 0:P], 0.0)
+        nc.gpsimd.affine_select(
+            out=ident[:], in_=zeros[:, 0:P], compare_op=ALU.not_equal, fill=1.0, base=0, pattern=[[-1, P]], channel_multiplier=1
+        )
         nc.vector.memset(ks_pool[0:TOP, :], 0)
-        nc.vector.memset(vs_pool[0:ROW, :].bitcast(I32), 0)
         nc.vector.memset(kb_pool[0:ROW, :].bitcast(I32), 0)
+        nc.vector.memset(vs_pool[0:ROW, :].bitcast(I32), 0)
 
         warm = sb.tile([P, 1], F32, name="warm")
-        nc.scalar.activation(warm[0:32, :], vs_pool[0:32, 0:1], ACT.Relu)
+        nc.scalar.activation(warm[0:32, :], kb_pool[0:32, 0:1], ACT.Relu)
 
         nc.sync.dma_start(offsets[:], offs)
         nc.sync.dma_start(ks_pool[TOP:P, :], k_scales.rearrange("o f t -> f o t").bitcast(I32))
         nc.sync.dma_start(staged[TOP:P, N : N + NQ].bitcast(I32), q_scales[0].rearrange("o f q -> f o q").bitcast(I32))
-        nc.sync.dma_start(vs_pool[ROW:P, :], vs[0:1, :])
         nc.sync.dma_start(kb_pool[ROW:P, :], kb[0:1, :])
         nc.sync.dma_start(kw_pool[:], k_words[0].rearrange("g t b -> g (t b)").bitcast(I32))
+        nc.sync.dma_start(vs_pool[ROW:P, :], vs[0:1, :])
         q_rows = q_words[0].rearrange("o g (c q) r -> c g o (q r)", c=2)
         qw = [sb.tile([P, 2, P], I32, name="qw0", align_bytes=64)]
         nc.sync.dma_start(qw[0][:], q_rows[0].bitcast(I32))
@@ -60,7 +63,7 @@ def tile_attend_rel2_kb_srtq256n512t1024_kernel(tc, q_words, q_scales, k_words, 
         def by_place(ap):
             return ap.rearrange("p (t m) -> p m t", t=4)
 
-        ks_g = placed.tile([P, N], U8, name="ks_g", offset=8 * P - N // 2, align_bytes=64)
+        ks_g = sb.tile([P, N], U8, name="ks_g", align_bytes=64)
         nc.vector.tensor_copy(by_place(ks_g[:]), ks_pool[:].bitcast(U8).indirect(offsets[:]))
         nc.vector.tensor_copy(staged[:, 0:N].bitcast(I32), ks_g[:].bitcast(I32))
         for Q in range(4):
@@ -72,26 +75,22 @@ def tile_attend_rel2_kb_srtq256n512t1024_kernel(tc, q_words, q_scales, k_words, 
         nc.sync.dma_start(qw[1][:], q_rows[1].bitcast(I32))
         v_pool1 = placed.tile([P, T], F32, name="v_pool1", offset=8 * P, align_bytes=64)
         nc.sync.dma_start(v_pool1[:], vT[P : 2 * P, :])
-        kb_g = sb.tile([P, N], F32, name="kb_g", align_bytes=64)
-        nc.vector.tensor_copy(by_place(kb_g[:].bitcast(U32)), kb_pool[:].bitcast(U32).indirect(offsets[:]))
         kw_g = sb.tile([P, N], U32, name="kw_g", tag="kw_g_then_v_g", align_bytes=64)
         nc.vector.tensor_copy(by_place(kw_g[:]), kw_pool[:].bitcast(U32).indirect(offsets[:]))
         kw = [sb.tile([P, 2, N], U8, name="kw%d" % u, align_bytes=64) for u in range(2)]
         for u in range(2):
             nc.vector.tensor_copy(kw[u][:].bitcast(U16), kw_g[:].bitcast(U16).rearrange("p (u m o) -> p u o m", u=2, o=2)[:, u])
 
-        vs_g = sb.tile([P, N], F32, name="vs_g", align_bytes=64)
-        nc.scalar.activation(vs_g[:], vs_pool[:].indirect(offsets[:]), ACT.Copy)
-
-        vs_t = ps.tile([P, 4, P], F32, name="vs_t", tag="bank7")
-        kb_t = ps.tile([P, 4, P], F32, name="kb_t", tag="bank6")
+        kb_g = sb.tile([P, N], F32, name="kb_g", align_bytes=64)
+        nc.scalar.activation(kb_g[:], kb_pool[:].indirect(offsets[:]), ACT.Copy)
+        kb_t = ps.tile([P, 4, P], F32, name="kb_t", tag="bank7")
         for t in range(4):
-            nc.tensor.transpose(vs_t[:, t, :], vs_g[:, t:N:4], ident[:])
-        for t in range(4):
-            nc.tensor.transpose(kb_t[:, t, :], kb_g[:, t * P : (t + 1) * P], ident[:])
+            nc.tensor.transpose(kb_t[:, t, :], kb_g[:, t:N:4], ident[:])
         kb_col = sb.tile([P, 4], F32, name="kb_col")
         nc.scalar.copy(kb_col[:], kb_t[:, :, ROW])
 
+        vs_g = sb.tile([P, N], F32, name="vs_g", tag="kw_then_vs_g", align_bytes=64)
+        nc.vector.tensor_copy(by_place(vs_g[:].bitcast(U32)), vs_pool[:].bitcast(U32).indirect(offsets[:]))
         v_g = [
             sb.tile([P, N], BF16, name="v_g0", tag="kw_g_then_v_g", align_bytes=64),
             sb.tile([P, N], BF16, name="v_g1", align_bytes=64),
@@ -103,7 +102,7 @@ def tile_attend_rel2_kb_srtq256n512t1024_kernel(tc, q_words, q_scales, k_words, 
         p = sb.tile([P, 2, 2, P, 2], F32, name="p", align_bytes=64)
         for i in range(8):
             qb, t = divmod(i, 4)
-            score = ps.tile([P, P], F32, name="score%d" % i, tag="bank%d" % (i % 7))
+            score = ps.tile([P, P], F32, name="score%d" % i, tag="bank%d" % i)
             for o in range(2):
                 nc.tensor.matmul_mx(
                     out=score[:],
@@ -118,6 +117,9 @@ def tile_attend_rel2_kb_srtq256n512t1024_kernel(tc, q_words, q_scales, k_words, 
             if t % 2 == 1:
                 nc.scalar.activation(p[:, qb, t // 2], relu[:, i - 1 : i + 1].rearrange("p b q -> p q b"), ACT.Square)
 
+        vs_t = ps.tile([P, 4, P], F32, name="vs_t", tag="bank0")
+        for t in range(4):
+            nc.tensor.transpose(vs_t[:, t, :], vs_g[:, t * P : (t + 1) * P], ident[:])
         v_in = sb.tile([P, 2, P * 4], BF16, name="v_in", tag="relu_then_v_in", align_bytes=64)
         for h in range(2):
             v_t = ps.tile([P, 2, P], F32, name="v%d_t" % h, tag=("bank6", "bank5")[h])
@@ -126,7 +128,7 @@ def tile_attend_rel2_kb_srtq256n512t1024_kernel(tc, q_words, q_scales, k_words, 
                 nc.tensor.transpose(v_t[:, u, :], v_words[:, u * P : (u + 1) * P], ident[:])
             nc.scalar.copy(v_in[:, h, :].bitcast(F32).rearrange("p (e u) -> p e u", u=2), v_t[:].rearrange("p u e -> p e u"))
 
-        w_in = placed.tile([P, 2, P, 4], BF16, name="w_in", offset=8 * P, align_bytes=64)
+        w_in = placed.tile([P, 2, P, 4], BF16, name="w_in", offset=16 * P, align_bytes=64)
         wq = sb.tile([P, NQ], U32, name="wq", align_bytes=64)
         wq_s = sb.tile([P, NQ], U8, name="wq_s", align_bytes=64)
         vq = sb.tile([P, DV], U32, name="vq", align_bytes=64)
@@ -147,6 +149,8 @@ def tile_attend_rel2_kb_srtq256n512t1024_kernel(tc, q_words, q_scales, k_words, 
                 out=wq[:, cols].bitcast(FP8X4), scales=wq_s[:, cols], in_=w_in[:, qb].rearrange("p q t -> p (q t)")
             )
 
+        p0_sum = placed.tile([P, 2, P], F32, name="p0_sum", offset=8 * P, align_bytes=64)
+        nc.vector.tensor_tensor(p0_sum[:], p[:, 0, 0].rearrange("p q b -> p b q"), p[:, 0, 1].rearrange("p q b -> p b q"), ALU.add)
         weigh(0)
         weigh(1)
         quantise_weights(0)
@@ -156,10 +160,11 @@ def tile_attend_rel2_kb_srtq256n512t1024_kernel(tc, q_words, q_scales, k_words, 
         total = sb.tile([P, 2], F32, name="total")
         inv = sb.tile([P, 2], F32, name="inv")
         spent = sb.tile([P, 2, P], F32, name="spent")
+        parts = ([p0_sum[:, b, :] for b in range(2)], [p[:, 1, t // 2, :, t % 2] for t in range(4)])
         for qb in range(2):
-            p_t = ps.tile([P, P], F32, name="p_t%d" % qb, tag=("bank0", "bank2")[qb])
-            for t in range(4):
-                nc.tensor.matmul(p_t[:], p[:, qb, t // 2, :, t % 2], ident[:], start=(t == 0), stop=(t == 3), is_transpose=True)
+            p_t = ps.tile([P, P], F32, name="p_t%d" % qb, tag=("bank7", "bank2")[qb])
+            for j, part in enumerate(parts[qb]):
+                nc.tensor.matmul(p_t[:], part, ident[:], start=(j == 0), stop=(j == len(parts[qb]) - 1), is_transpose=True)
             nc.scalar.activation(spent[:, qb, :], p_t[:], ACT.Copy, bias=1.0 / P, accum_out=total[:, qb : qb + 1])
         nc.vector.reciprocal(inv[:], total[:])
 

@@ -31,32 +31,33 @@ def tile_attend_rel2_kb_srtq256n512t1024_kernel(tc, q_words, q_scales, k_words, 
         ks_pool = sb.tile([P, T // 4], I32, name="ks_pool", align_bytes=64)
         kb_pool = sb.tile([P, T], F32, name="kb_pool", align_bytes=64)
         vs_pool = sb.tile([P, T], F32, name="vs_pool", align_bytes=64)
-        kw_pool = sb.tile([P, T], I32, name="kw_pool", tag="kw_then_vs_g", align_bytes=64)
-        v_pool0 = sb.tile([P, T], F32, name="v_pool0", align_bytes=64)
+        kw_pool = sb.tile([P, T], I32, name="kw_pool", tag="kw_then_vs_g", align_bytes=256)
+        v_pool0 = sb.tile([P, T], F32, name="v_pool0", align_bytes=256)
         staged = sb.tile([P, N + NQ], U8, name="staged", align_bytes=64)
         planes = sb.tile([P, 2, N + NQ], U8, name="planes", align_bytes=64)
         ident = sb.tile([P, P], F32, name="ident", align_bytes=64)
 
-        zeros = placed.tile([P, 2 * P + T], F32, name="zeros", offset=0, align_bytes=64)
-        nc.gpsimd.memset(zeros[:, 0:P], 0.0)
+        warm = sb.tile([P, 2], F32, name="warm")
+        nc.gpsimd.memset(warm[:, 0:1], 0.0)
+        nc.scalar.activation(warm[:, 1:2], warm[:, 0:1], ACT.Relu)
+
+        zeros = placed.tile([P, P], F32, name="zeros", offset=8 * P - 64, align_bytes=64)
+        nc.gpsimd.memset(zeros[:], 0.0)
         nc.gpsimd.affine_select(
-            out=ident[:], in_=zeros[:, 0:P], compare_op=ALU.not_equal, fill=1.0, base=0, pattern=[[-1, P]], channel_multiplier=1
+            out=ident[:], in_=zeros[:], compare_op=ALU.not_equal, fill=1.0, base=0, pattern=[[-1, P]], channel_multiplier=1
         )
         nc.vector.memset(ks_pool[0:TOP, :], 0)
         nc.vector.memset(kb_pool[0:ROW, :].bitcast(I32), 0)
         nc.vector.memset(vs_pool[0:ROW, :].bitcast(I32), 0)
 
-        warm = sb.tile([P, 1], F32, name="warm")
-        nc.scalar.activation(warm[0:32, :], kb_pool[0:32, 0:1], ACT.Relu)
-
         nc.sync.dma_start(offsets[:], offs)
         nc.sync.dma_start(ks_pool[TOP:P, :], k_scales.rearrange("o f t -> f o t").bitcast(I32))
-        nc.sync.dma_start(staged[TOP:P, N : N + NQ].bitcast(I32), q_scales[0].rearrange("o f q -> f o q").bitcast(I32))
-        nc.sync.dma_start(kb_pool[ROW:P, :], kb[0:1, :])
         nc.sync.dma_start(kw_pool[:], k_words[0].rearrange("g t b -> g (t b)").bitcast(I32))
+        nc.sync.dma_start(kb_pool[ROW:P, :], kb[0:1, :])
+        nc.sync.dma_start(staged[TOP:P, N : N + NQ].bitcast(I32), q_scales[0].rearrange("o f q -> f o q").bitcast(I32))
         nc.sync.dma_start(vs_pool[ROW:P, :], vs[0:1, :])
         q_rows = q_words[0].rearrange("o g (c q) r -> c g o (q r)", c=2)
-        qw = [sb.tile([P, 2, P], I32, name="qw0", align_bytes=64)]
+        qw = [sb.tile([P, 2, P], I32, name="qw0", align_bytes=256)]
         nc.sync.dma_start(qw[0][:], q_rows[0].bitcast(I32))
         nc.sync.dma_start(v_pool0[:], vT[0:P, :])
 
@@ -71,9 +72,9 @@ def tile_attend_rel2_kb_srtq256n512t1024_kernel(tc, q_words, q_scales, k_words, 
                 planes[32 * Q : 32 * Q + 4].rearrange("p o x -> p (o x)").bitcast(I32),
                 staged[TOP + 8 * Q : TOP + 8 * Q + 8, :].bitcast(I32),
             )
-        qw.append(placed.tile([P, 2, P], I32, name="qw1", offset=0, align_bytes=64))
+        qw.append(placed.tile([P, 2, P], I32, name="qw1", offset=0, align_bytes=256))
         nc.sync.dma_start(qw[1][:], q_rows[1].bitcast(I32))
-        v_pool1 = placed.tile([P, T], F32, name="v_pool1", offset=8 * P, align_bytes=64)
+        v_pool1 = placed.tile([P, T], F32, name="v_pool1", offset=10 * P, align_bytes=256)
         nc.sync.dma_start(v_pool1[:], vT[P : 2 * P, :])
         kw_g = sb.tile([P, N], U32, name="kw_g", tag="kw_g_then_v_g", align_bytes=64)
         nc.vector.tensor_copy(by_place(kw_g[:]), kw_pool[:].bitcast(U32).indirect(offsets[:]))
@@ -89,7 +90,7 @@ def tile_attend_rel2_kb_srtq256n512t1024_kernel(tc, q_words, q_scales, k_words, 
         kb_col = sb.tile([P, 4], F32, name="kb_col")
         nc.scalar.copy(kb_col[:], kb_t[:, :, ROW])
 
-        vs_g = sb.tile([P, N], F32, name="vs_g", tag="kw_then_vs_g", align_bytes=64)
+        vs_g = sb.tile([P, N], F32, name="vs_g", tag="kw_then_vs_g", align_bytes=256)
         nc.vector.tensor_copy(by_place(vs_g[:].bitcast(U32)), vs_pool[:].bitcast(U32).indirect(offsets[:]))
         v_g = [
             sb.tile([P, N], BF16, name="v_g0", tag="kw_g_then_v_g", align_bytes=64),
@@ -128,7 +129,7 @@ def tile_attend_rel2_kb_srtq256n512t1024_kernel(tc, q_words, q_scales, k_words, 
                 nc.tensor.transpose(v_t[:, u, :], v_words[:, u * P : (u + 1) * P], ident[:])
             nc.scalar.copy(v_in[:, h, :].bitcast(F32).rearrange("p (e u) -> p e u", u=2), v_t[:].rearrange("p u e -> p e u"))
 
-        w_in = placed.tile([P, 2, P, 4], BF16, name="w_in", offset=16 * P, align_bytes=64)
+        w_in = placed.tile([P, 2, P, 4], BF16, name="w_in", offset=18 * P, align_bytes=64)
         wq = sb.tile([P, NQ], U32, name="wq", align_bytes=64)
         wq_s = sb.tile([P, NQ], U8, name="wq_s", align_bytes=64)
         vq = sb.tile([P, DV], U32, name="vq", align_bytes=64)
@@ -149,7 +150,7 @@ def tile_attend_rel2_kb_srtq256n512t1024_kernel(tc, q_words, q_scales, k_words, 
                 out=wq[:, cols].bitcast(FP8X4), scales=wq_s[:, cols], in_=w_in[:, qb].rearrange("p q t -> p (q t)")
             )
 
-        p0_sum = placed.tile([P, 2, P], F32, name="p0_sum", offset=8 * P, align_bytes=64)
+        p0_sum = placed.tile([P, 2, P], F32, name="p0_sum", offset=10 * P, align_bytes=64)
         nc.vector.tensor_tensor(p0_sum[:], p[:, 0, 0].rearrange("p q b -> p b q"), p[:, 0, 1].rearrange("p q b -> p b q"), ALU.add)
         weigh(0)
         weigh(1)
@@ -185,5 +186,4 @@ def tile_attend_rel2_kb_srtq256n512t1024_kernel(tc, q_words, q_scales, k_words, 
             y_right = product(qb, right, "y%d_right" % qb, ("bank4", "bank6")[qb])
             nc.vector.tensor_scalar(res[:, left], y_left[:], inv[:, qb : qb + 1], None, ALU.mult)
             nc.scalar.activation(res[:, right], y_right[:], ACT.Copy, scale=inv[:, qb : qb + 1])
-            nc.sync.dma_start(out[0, rows, left], res[:, left])
-            nc.scalar.dma_start(out[0, rows, right], res[:, right])
+            nc.sync.dma_start(out[0, rows, :], res[:])

@@ -41,14 +41,16 @@ def tile_attend_rel2_kb_srtq256n512t1024_kernel(tc, q_words, q_scales, k_words, 
         nc.gpsimd.memset(warm[:, 0:1], 0.0)
         nc.scalar.activation(warm[:, 1:2], warm[:, 0:1], ACT.Relu)
 
+        nc.gpsimd.memset(vs_pool[0:ROW, :].bitcast(I32), 0)
         zeros = placed.tile([P, P], F32, name="zeros", offset=8 * P - 64, align_bytes=64)
         nc.gpsimd.memset(zeros[:], 0.0)
         nc.gpsimd.affine_select(
             out=ident[:], in_=zeros[:], compare_op=ALU.not_equal, fill=1.0, base=0, pattern=[[-1, P]], channel_multiplier=1
         )
-        nc.vector.memset(ks_pool[0:TOP, :], 0)
-        nc.vector.memset(kb_pool[0:ROW, :].bitcast(I32), 0)
-        nc.vector.memset(vs_pool[0:ROW, :].bitcast(I32), 0)
+        for rows in (ks_pool[0:TOP, :], kb_pool[0:ROW, :].bitcast(I32)):
+            last = rows.shape[1] - 1
+            nc.vector.memset(rows[:, 0:last], 0)
+            nc.vector.memset(rows[:, last : last + 1], 0)
 
         nc.sync.dma_start(offsets[:], offs)
         nc.sync.dma_start(ks_pool[TOP:P, :], k_scales.rearrange("o f t -> f o t").bitcast(I32))

@@ -54,8 +54,8 @@ def tile_attend_rel2_kb_srtq256n512t1024_kernel(tc, q_words, q_scales, k_words, 
 
         nc.sync.dma_start(offsets[:], offs)
         nc.sync.dma_start(ks_pool[TOP:P, :], k_scales.rearrange("o f t -> f o t").bitcast(I32))
-        nc.sync.dma_start(kw_pool[:], k_words[0].rearrange("g t b -> g (t b)").bitcast(I32))
         nc.sync.dma_start(kb_pool[ROW:P, :], kb[0:1, :])
+        nc.sync.dma_start(kw_pool[:], k_words[0].rearrange("g t b -> g (t b)").bitcast(I32))
         nc.sync.dma_start(staged[TOP:P, N : N + NQ].bitcast(I32), q_scales[0].rearrange("o f q -> f o q").bitcast(I32))
         nc.sync.dma_start(vs_pool[ROW:P, :], vs[0:1, :])
         q_rows = q_words[0].rearrange("o g (c q) r -> c g o (q r)", c=2)

from contextlib import ExitStack

import concourse.mybir as mybir

F32 = mybir.dt.float32
BF16 = mybir.dt.bfloat16
I32 = mybir.dt.int32
U32 = mybir.dt.uint32
U16 = mybir.dt.uint16
U8 = mybir.dt.uint8
FP8X4 = mybir.dt.float8_e4m3fn_x4
FP4X4 = mybir.dt.float4_e2m1fn_x4
ACT = mybir.ActivationFunctionType
ALU = mybir.AluOpType

P = 128
ROW = P - 1
TOP = P - 32
N, T, D, DV, NQ = 512, 1024, 1024, 256, 256
FLOPS = 2 * NQ * N * D + 2 * NQ * N * DV


def tile_attend_rel2_kb_srtq256n512t1024_kernel(tc, q_words, q_scales, k_words, k_scales, vT, vs, kb, offs, out):
    nc = tc.nc
    with ExitStack() as ctx:
        sb = ctx.enter_context(tc.tile_pool(name="sb", bufs=1))
        placed = ctx.enter_context(tc.tile_pool(name="placed", bufs=1))
        ps = ctx.enter_context(tc.psum_pool(name="ps", bufs=1))

        offsets = sb.tile([P, N // 16], U16, name="offsets")
        ks_pool = sb.tile([P, T // 4], I32, name="ks_pool", align_bytes=64)
        kb_pool = sb.tile([P, T], F32, name="kb_pool", align_bytes=64)
        vs_pool = sb.tile([P, T], F32, name="vs_pool", align_bytes=64)
        kw_pool = sb.tile([P, T], I32, name="kw_pool", tag="kw_then_vs_g", align_bytes=256)
        v_pool0 = sb.tile([P, T], F32, name="v_pool0", align_bytes=256)
        staged = sb.tile([P, N + NQ], U8, name="staged", align_bytes=64)
        planes = sb.tile([P, 2, N + NQ], U8, name="planes", align_bytes=64)
        ident = sb.tile([P, P], F32, name="ident", align_bytes=64)

        warm = sb.tile([P, 2], F32, name="warm")
        nc.gpsimd.memset(warm[:, 0:1], 0.0)
        nc.scalar.activation(warm[:, 1:2], warm[:, 0:1], ACT.Relu)

        nc.gpsimd.memset(vs_pool[0:ROW, :].bitcast(I32), 0)
        zeros = placed.tile([P, P], F32, name="zeros", offset=8 * P - 64, align_bytes=64)
        nc.gpsimd.memset(zeros[:], 0.0)
        nc.gpsimd.affine_select(
            out=ident[:], in_=zeros[:], compare_op=ALU.not_equal, fill=1.0, base=0, pattern=[[-1, P]], channel_multiplier=1
        )
        for rows in (ks_pool[0:TOP, :], kb_pool[0:ROW, :].bitcast(I32)):
            last = rows.shape[1] - 1
            nc.vector.memset(rows[:, 0:last], 0)
            nc.vector.memset(rows[:, last : last + 1], 0)

        nc.sync.dma_start(offsets[:], offs)
        nc.sync.dma_start(ks_pool[TOP:P, :], k_scales.rearrange("o f t -> f o t").bitcast(I32))
        nc.sync.dma_start(kb_pool[ROW:P, :], kb[0:1, :])
        nc.sync.dma_start(kw_pool[:], k_words[0].rearrange("g t b -> g (t b)").bitcast(I32))
        nc.sync.dma_start(staged[TOP:P, N : N + NQ].bitcast(I32), q_scales[0].rearrange("o f q -> f o q").bitcast(I32))
        nc.sync.dma_start(vs_pool[ROW:P, :], vs[0:1, :])
        q_rows = q_words[0].rearrange("o g (c q) r -> c g o (q r)", c=2)
        qw = [sb.tile([P, 2, P], I32, name="qw0", align_bytes=256)]
        nc.sync.dma_start(qw[0][:], q_rows[0].bitcast(I32))
        nc.sync.dma_start(v_pool0[:], vT[0:P, :])

        def by_place(ap):
            return ap.rearrange("p (t m) -> p m t", t=4)

        ks_g = sb.tile([P, N], U8, name="ks_g", align_bytes=64)
        nc.vector.tensor_copy(by_place(ks_g[:]), ks_pool[:].bitcast(U8).indirect(offsets[:]))
        nc.vector.tensor_copy(staged[:, 0:N].bitcast(I32), ks_g[:].bitcast(I32))
        for Q in range(4):
            nc.sync.dma_start(
                planes[32 * Q : 32 * Q + 4].rearrange("p o x -> p (o x)").bitcast(I32),
                staged[TOP + 8 * Q : TOP + 8 * Q + 8, :].bitcast(I32),
            )
        qw.append(placed.tile([P, 2, P], I32, name="qw1", offset=0, align_bytes=256))
        nc.sync.dma_start(qw[1][:], q_rows[1].bitcast(I32))
        v_pool1 = placed.tile([P, T], F32, name="v_pool1", offset=10 * P, align_bytes=256)
        nc.sync.dma_start(v_pool1[:], vT[P : 2 * P, :])
        kw_g = sb.tile([P, N], U32, name="kw_g", tag="kw_g_then_v_g", align_bytes=64)
        nc.vector.tensor_copy(by_place(kw_g[:]), kw_pool[:].bitcast(U32).indirect(offsets[:]))
        kw = [sb.tile([P, 2, N], U8, name="kw%d" % u, align_bytes=64) for u in range(2)]
        for u in range(2):
            nc.vector.tensor_copy(kw[u][:].bitcast(U16), kw_g[:].bitcast(U16).rearrange("p (u m o) -> p u o m", u=2, o=2)[:, u])

        kb_g = sb.tile([P, N], F32, name="kb_g", align_bytes=64)
        nc.scalar.activation(kb_g[:], kb_pool[:].indirect(offsets[:]), ACT.Copy)
        kb_t = ps.tile([P, 4, P], F32, name="kb_t", tag="bank7")
        for t in range(4):
            nc.tensor.transpose(kb_t[:, t, :], kb_g[:, t:N:4], ident[:])
        kb_col = sb.tile([P, 4], F32, name="kb_col")
        nc.scalar.copy(kb_col[:], kb_t[:, :, ROW])

        vs_g = sb.tile([P, N], F32, name="vs_g", tag="kw_then_vs_g", align_bytes=256)
        nc.vector.tensor_copy(by_place(vs_g[:].bitcast(U32)), vs_pool[:].bitcast(U32).indirect(offsets[:]))
        v_g = [
            sb.tile([P, N], BF16, name="v_g0", tag="kw_g_then_v_g", align_bytes=64),
            sb.tile([P, N], BF16, name="v_g1", align_bytes=64),
        ]
        for h, v_pool in enumerate((v_pool0, v_pool1)):
            nc.vector.tensor_copy(v_g[h][:].rearrange("p (u m b) -> p m u b", u=2, b=2), v_pool[:].indirect(offsets[:]))

        relu = sb.tile([P, 8, P], F32, name="relu", tag="relu_then_v_in", align_bytes=64)
        p = sb.tile([P, 2, 2, P, 2], F32, name="p", align_bytes=64)
        for i in range(8):
            qb, t = divmod(i, 4)
            score = ps.tile([P, P], F32, name="score%d" % i, tag="bank%d" % i)
            for o in range(2):
                nc.tensor.matmul_mx(
                    out=score[:],
                    lhsT=kw[t // 2][:, o, 2 * P * (t % 2) : 2 * P * (t % 2 + 1)].bitcast(FP4X4),
                    lhsT_scale=planes[:, o, P * t : P * (t + 1)],
                    rhs=qw[qb][:, o, :].bitcast(FP8X4),
                    rhs_scale=planes[:, o, N + qb * P : N + (qb + 1) * P],
                    start=(o == 0),
                    stop=(o == 1),
                )
            nc.scalar.activation(relu[:, i, :], score[:], ACT.Relu, bias=kb_col[:, t : t + 1])
            if t % 2 == 1:
                nc.scalar.activation(p[:, qb, t // 2], relu[:, i - 1 : i + 1].rearrange("p b q -> p q b"), ACT.Square)

        vs_t = ps.tile([P, 4, P], F32, name="vs_t", tag="bank0")
        for t in range(4):
            nc.tensor.transpose(vs_t[:, t, :], vs_g[:, t * P : (t + 1) * P], ident[:])
        v_in = sb.tile([P, 2, P * 4], BF16, name="v_in", tag="relu_then_v_in", align_bytes=64)
        for h in range(2):
            v_t = ps.tile([P, 2, P], F32, name="v%d_t" % h, tag=("bank6", "bank5")[h])
            v_words = v_g[h][:].bitcast(F32)
            for u in range(2):
                nc.tensor.transpose(v_t[:, u, :], v_words[:, u * P : (u + 1) * P], ident[:])
            nc.scalar.copy(v_in[:, h, :].bitcast(F32).rearrange("p (e u) -> p e u", u=2), v_t[:].rearrange("p u e -> p e u"))

        w_in = placed.tile([P, 2, P, 4], BF16, name="w_in", offset=18 * P, align_bytes=64)
        wq = sb.tile([P, NQ], U32, name="wq", align_bytes=64)
        wq_s = sb.tile([P, NQ], U8, name="wq_s", align_bytes=64)
        vq = sb.tile([P, DV], U32, name="vq", align_bytes=64)
        vq_s = sb.tile([P, DV], U8, name="vq_s", align_bytes=64)
        vs_wide = vs_t[:, :, ROW:P].to_broadcast([P, 4, P])

        def weigh(qb):
            nc.vector.tensor_tensor(
                w_in[:, qb].rearrange("p q (u b) -> p q u b", b=2),
                p[:, qb].rearrange("p u q b -> p q u b"),
                vs_wide.rearrange("p (u b) q -> p q u b", b=2),
                ALU.mult,
            )

        def quantise_weights(qb):
            cols = slice(qb * P, (qb + 1) * P)
            nc.vector.quantize_mx(
                out=wq[:, cols].bitcast(FP8X4), scales=wq_s[:, cols], in_=w_in[:, qb].rearrange("p q t -> p (q t)")
            )

        p0_sum = placed.tile([P, 2, P], F32, name="p0_sum", offset=10 * P, align_bytes=64)
        nc.vector.tensor_tensor(p0_sum[:], p[:, 0, 0].rearrange("p q b -> p b q"), p[:, 0, 1].rearrange("p q b -> p b q"), ALU.add)
        weigh(0)
        weigh(1)
        quantise_weights(0)
        nc.vector.quantize_mx(out=vq[:].bitcast(FP8X4), scales=vq_s[:], in_=v_in[:].rearrange("p h x -> p (h x)"))
        quantise_weights(1)

        total = sb.tile([P, 2], F32, name="total")
        inv = sb.tile([P, 2], F32, name="inv")
        spent = sb.tile([P, 2, P], F32, name="spent")
        parts = ([p0_sum[:, b, :] for b in range(2)], [p[:, 1, t // 2, :, t % 2] for t in range(4)])
        for qb in range(2):
            p_t = ps.tile([P, P], F32, name="p_t%d" % qb, tag=("bank7", "bank2")[qb])
            for j, part in enumerate(parts[qb]):
                nc.tensor.matmul(p_t[:], part, ident[:], start=(j == 0), stop=(j == len(parts[qb]) - 1), is_transpose=True)
            nc.scalar.activation(spent[:, qb, :], p_t[:], ACT.Copy, bias=1.0 / P, accum_out=total[:, qb : qb + 1])
        nc.vector.reciprocal(inv[:], total[:])

        def product(qb, cols, name, bank):
            rows = slice(qb * P, (qb + 1) * P)
            y = ps.tile([P, cols.stop - cols.start], F32, name=name, tag=bank)
            nc.tensor.matmul_mx(
                out=y[:], lhsT=wq[:, rows].bitcast(FP8X4), lhsT_scale=wq_s[:, rows],
                rhs=vq[:, cols].bitcast(FP8X4), rhs_scale=vq_s[:, cols], start=True, stop=True,
            )
            return y

        for qb in range(2):
            rows = slice(qb * P, (qb + 1) * P)
            left, right = slice(0, P), slice(P, DV)
            res = sb.tile([P, DV], F32, name="res%d" % qb, align_bytes=64)
            y_left = product(qb, left, "y%d_left" % qb, ("bank1", "bank3")[qb])
            y_right = product(qb, right, "y%d_right" % qb, ("bank4", "bank6")[qb])
            nc.vector.tensor_scalar(res[:, left], y_left[:], inv[:, qb : qb + 1], None, ALU.mult)
            nc.scalar.activation(res[:, right], y_right[:], ACT.Copy, scale=inv[:, qb : qb + 1])
            nc.sync.dma_start(out[0, rows, :], res[:])
